import numpy as np
import ml_dtypes


def mxq(x, axis, fmt="e4m3"):
    dtype, down = {"e4m3": (ml_dtypes.float8_e4m3fn, 7), "e5m2": (ml_dtypes.float8_e5m2, 14)}[fmt]
    v = np.moveaxis(np.asarray(x, np.float32).astype(ml_dtypes.bfloat16).astype(np.float64), axis, -1)
    blocks = v.reshape(v.shape[:-1] + (-1, 32))
    amax = np.abs(blocks).max(-1, keepdims=True)
    byte = np.maximum(np.where(amax > 0, np.frexp(amax)[1] - 1 + 127, 0) - down, 1)
    scale = np.exp2(byte - 127.0)
    codes = (blocks / scale).astype(np.float32).astype(dtype).astype(np.float64)
    return np.moveaxis((codes * scale).reshape(v.shape), -1, axis)


WIDE = False


def mx_kscale(k):
    if not WIDE:
        return np.ones(k)
    levels = np.array([10, -10, 5, -5, 0])
    if k % 512:
        return np.exp2(np.random.permutation(np.resize(levels, k // 32))).repeat(32)
    a = np.empty((k // 512, 16))
    for p in range(k // 512):
        a[p, :8] = np.random.permutation(np.resize(levels, 8))
        for g in range(8):
            far = levels[np.abs(levels - a[p, g]) >= 10]
            a[p, g + 8] = far[np.random.randint(len(far))]
    return np.exp2(a.ravel()).repeat(32)


BF16 = ml_dtypes.bfloat16


def bf(x):
    return np.asarray(x, np.float32).astype(BF16)


def f64(x):
    return np.asarray(x).astype(np.float64)


E2M1 = np.array([0.0, 0.5, 1.0, 1.5, 2.0, 3.0, 4.0, 6.0, -0.0, -0.5, -1.0, -1.5, -2.0, -3.0, -4.0, -6.0])


def pack_weight(w, fmt):
    k, n = w.shape
    w = f64(bf(w)).reshape(k // 32, 32, n)
    amax = np.abs(w).max(1)
    if fmt == "e4m3":
        byte = np.frexp(amax)[1] - 1 + 127 - 7
    else:
        mant, ex = np.frexp(amax / 6.0)
        byte = np.where(mant > 0.5, ex, ex - 1) + 127
    byte = np.clip(np.where(amax > 0, byte, 1), 1, 254)
    scaled = (w * np.exp2(127.0 - byte)[:, None, :]).reshape(k, n).astype(np.float32)
    by_word = np.ascontiguousarray(scaled.reshape(k // 512, 128, 4, n).transpose(0, 1, 3, 2))
    if fmt == "e4m3":
        words = by_word.astype(ml_dtypes.float8_e4m3fn).view(np.uint8)
    else:
        c = by_word.astype(ml_dtypes.float4_e2m1fn).view(np.uint8) & 0xF
        words = c[..., 0::2] | (c[..., 1::2] << 4)
    return np.ascontiguousarray(words), np.ascontiguousarray(byte.astype(np.uint8).reshape(k // 512, 16, n))


def unpack_weight(words, scales, fmt):
    g, p, n, _ = words.shape
    if fmt == "e4m3":
        vals = np.ascontiguousarray(words).view(ml_dtypes.float8_e4m3fn).astype(np.float64)
    else:
        nib = np.empty((g, p, n, 4), np.uint8)
        nib[..., 0::2] = words & 0xF
        nib[..., 1::2] = words >> 4
        vals = E2M1[nib]
    vals = vals * np.repeat(np.exp2(scales.astype(np.float64) - 127.0), 8, axis=1)[..., None]
    return vals.transpose(0, 1, 3, 2).reshape(g * 512, n)
def pack4(w):
    words, scales = pack_weight(w, "e2m1")
    return words.reshape(words.shape[0], 128, -1), scales


def unpack4(words, scales):
    return unpack_weight(words.reshape(words.shape[0], 128, -1, 2), scales, "e2m1")


N, D, F, L, Q = 1024, 1024, 1024, 512, 512


def draw0():
    a, b, u = mx_kscale(D), mx_kscale(L), mx_kscale(N)
    lam = np.random.uniform(0.5, 1.5, F)
    x = bf(np.random.standard_normal((N, D)) * a)
    w_words, w_scales = pack4(np.random.standard_normal((D, F)) * lam / np.sqrt(D) / a[:, None])
    s = bf((1.0 + 0.3 * np.random.standard_normal(N)) * u)
    t = bf(np.random.standard_normal((N, Q)) / u[:, None])
    g = bf(np.random.standard_normal((N, L)) * b / u[:, None])
    beta_words, beta_scales = pack4(np.random.standard_normal((L, Q)) / np.sqrt(L) / b[:, None])
    tau = bf(np.random.uniform(0.5, 1.5, Q))
    return {
        "x": x,
        "w_words": w_words,
        "w_scales": w_scales,
        "s": s,
        "t": t,
        "g": g,
        "beta_words": beta_words,
        "beta_scales": beta_scales,
        "tau": tau,
    }


def candidate_nodes(x, w_words, w_scales):
    return np.tanh(mxq(f64(x), 1, "e4m3") @ unpack4(w_words, w_scales))


def network_residual(t, g, beta_words, beta_scales):
    return f64(t) - (mxq(f64(g), 1, "e4m3") @ unpack4(beta_words, beta_scales))


def core(x, w_words, w_scales, s, t, g, beta_words, beta_scales, tau):
    h = candidate_nodes(x, w_words, w_scales)
    e = network_residual(t, g, beta_words, beta_scales)
    hs = f64(s)[:, None] * h
    c = mxq(hs, 0, "e4m3").T @ mxq(e, 0, "e4m3")
    hh = np.sum(np.square(h), axis=0)
    return np.square(c) / hh[:, None] - f64(tau)[None, :]


def e4m3fn_bytes(y):
    return np.clip(np.asarray(y, np.float64), -448.0, 448.0).astype(np.float32).astype(ml_dtypes.float8_e4m3fn).view(np.uint8)


def e4m3fn_values(b):
    return np.asarray(b, np.uint8).view(ml_dtypes.float8_e4m3fn).astype(np.float64)


def setup_inputs():
    d = draw0()
    x0 = np.asarray(d['x']).astype(np.float64)
    s = (np.max(np.abs(x0), axis=(0,), keepdims=True) / 448.0).astype(np.float32)
    out = {}
    for k, v in d.items():
        if k == 'x':
            out['x_bytes'] = e4m3fn_bytes(x0 / s.astype(np.float64))
            out['x_scale'] = s
        else:
            out[k] = v
    return out


def reference(x_bytes, x_scale, w_words, w_scales, s, t, g, beta_words, beta_scales, tau):
    return core(e4m3fn_values(x_bytes) * x_scale.astype(np.float64), w_words, w_scales, s, t, g, beta_words, beta_scales, tau)

@@ -1,0 +1,402 @@
+from contextlib import ExitStack
+
+import concourse.mybir as mybir
+from concourse.masks import make_identity
+
+F32 = mybir.dt.float32
+BF16 = mybir.dt.bfloat16
+I32 = mybir.dt.int32
+U32 = mybir.dt.uint32
+U8 = mybir.dt.uint8
+FP8 = mybir.dt.float8_e4m3fn
+FP8X4 = mybir.dt.float8_e4m3fn_x4
+FP4X4 = mybir.dt.float4_e2m1fn_x4
+ACT = mybir.ActivationFunctionType
+ALU = mybir.AluOpType
+
+N, D, F, L, Q = 1024, 1024, 1024, 512, 512
+FLOPS = 2 * N * D * F + 2 * N * L * Q + 2 * N * F * Q
+
+P = 128
+J = 4
+BANK = 512
+ROW_TILES = N // P
+NODE_HALF = F // 2
+FP4_BYTES = 2
+
+X_LOADS = (1, 1, 2, 4)
+SINGLE_ROW_TILES = 4
+WARM_UP_MATMULS = 5
+LAST_BLOCK_PARTS = 2
+
+TURNED_BANKS = 4
+PREACT_BANKS = 2
+PRODUCT_BANKS = 2
+
+
+def tile_stochasticconfigurationcandidatescores_w4_kernel(
+    tc, x_bytes, x_scale, w_words, w_scales, gain, target, hidden, beta_words, beta_scales, tau, out
+):
+    nc = tc.nc
+    with ExitStack() as ctx:
+        keep = ctx.enter_context(tc.tile_pool(name="keep", bufs=1))
+        psum = ctx.enter_context(tc.psum_pool(name="psum", bufs=1))
+
+        def sbuf(name, shape, dtype):
+            return keep.tile(shape, dtype, name=name, align_bytes=64)
+
+        x_raw = [sbuf("x_raw%d" % i, [P, n, D], U8) for i, n in enumerate(X_LOADS)]
+        x_scl = sbuf("x_scl", [P, 2, J], F32)
+        w_wrd = [sbuf("w_wrd%d" % b, [P, 2, FP4_BYTES * NODE_HALF], U8) for b in range(2)]
+        w_scl = sbuf("w_scl", [P, 2, F], U8)
+        b_wrd = sbuf("b_wrd", [P, FP4_BYTES * Q], U8)
+        b_scl = sbuf("b_scl", [P, Q], U8)
+        hid = [sbuf("hid%d" % v, [P, J, L], BF16) for v in range(2)]
+        tgt = [sbuf("tgt%d" % v, [P, J, Q], BF16) for v in range(2)]
+        gain_q = sbuf("gain_q", [P, 2, J], BF16)
+        tau_b = sbuf("tau_b", [P, Q], BF16)
+
+        x_wide = [sbuf("x_wide%d" % r, [P, D], BF16) for r in range(ROW_TILES)]
+        x_val = [sbuf("x_val%d" % i, [P, 2, 2, P, J], BF16) for i in range(4)]
+        x_cod = [sbuf("x_cod%d" % i, [P, 2, 2, P], U32) for i in range(4)]
+        x_csc = [sbuf("x_csc%d" % i, [P, 2, 2, P], U8) for i in range(4)]
+        g_val = [sbuf("g_val%d" % v, [P, J, P, J], BF16) for v in range(2)]
+        g_cod = [sbuf("g_cod%d" % v, [P, J, P], U32) for v in range(2)]
+        g_csc = [sbuf("g_csc%d" % v, [P, J, P], U8) for v in range(2)]
+        e_val = [sbuf("e_val%d" % v, [P, Q, J], BF16) for v in range(2)]
+        e_cod = [sbuf("e_cod%d" % v, [P, Q], U32) for v in range(2)]
+        e_csc = [sbuf("e_csc%d" % v, [P, Q], U8) for v in range(2)]
+        chunks = [(b, v) for b in range(2) for v in range(2)]
+        h = {k: sbuf("h%d%d" % k, [P, J, NODE_HALF], F32) for k in chunks}
+        hs_val = {k: sbuf("hs_val%d%d" % k, [P, NODE_HALF, J], BF16) for k in chunks}
+        hs_cod = {k: sbuf("hs_cod%d%d" % k, [P, NODE_HALF], U32) for k in chunks}
+        hs_csc = {k: sbuf("hs_csc%d%d" % k, [P, NODE_HALF], U8) for k in chunks}
+        hh_part = [sbuf("hh_part%d" % b, [P, 4, 2], F32) for b in range(2)]
+        hh_sum = [sbuf("hh_sum%d" % b, [P, 4], F32) for b in range(2)]
+        hh_inv = [sbuf("hh_inv%d" % b, [P, 4], F32) for b in range(2)]
+        squares = sbuf("squares", [P, BANK], BF16)
+        c_sq = [sbuf("c_sq%d" % i, [P, Q], F32) for i in range(8)]
+        res = [sbuf("res%d" % i, [P, Q], F32) for i in range(8)]
+
+        ident = sbuf("ident", [P, P], F32)
+        zeros = sbuf("zeros", [P, BANK], BF16)
+        dummy = sbuf("dummy", [P, 2], F32)
+
+        banks = {}
+
+        def new_bank(key, tag, bufs):
+            banks[key] = psum.tile([P, BANK], F32, name="bank_" + tag, tag=tag, bufs=bufs)
+            return banks[key]
+
+        x_place = [(i, n) for i, count in enumerate(X_LOADS) for n in range(count)]
+
+        def x_widen(copy, r, k0, k1):
+            i, n = x_place[r]
+            copy(x_wide[r][:, k0:k1], x_raw[i][:, n, k0:k1].bitcast(FP8))
+
+        def x_turn(r):
+            bank = new_bank(("x", r), "turned", TURNED_BANKS)
+            words = x_wide[r][:].bitcast(F32)
+            for v in range(2):
+                for u in range(2):
+                    at = (2 * v + u) * P
+                    nc.tensor.transpose(
+                        bank[:, at : at + P], words[:, 256 * v + u : 256 * (v + 1) : 2], ident[:]
+                    )
+
+        def x_scale_out(r, v):
+            turned = banks["x", r][:, 256 * v : 256 * (v + 1)].bitcast(BF16)
+            nc.vector.tensor_tensor(
+                out=x_val[r // 2][:, r % 2, v].rearrange("p r (u e) -> p r u e", u=2),
+                in0=turned.rearrange("p (u r e) -> p r u e", u=2, e=2),
+                in1=x_scl[:, v, :].rearrange("p (u e) -> p u e", u=2).unsqueeze(1).to_broadcast([P, P, 2, 2]),
+                op=ALU.mult,
+            )
+
+        def x_quantise(r):
+            i, n = r // 2, r % 2
+            nc.vector.quantize_mx(
+                out=x_cod[i][:, n].rearrange("p v r -> p (v r)").bitcast(FP8X4),
+                scales=x_csc[i][:, n].rearrange("p v r -> p (v r)"),
+                in_=x_val[i][:, n].rearrange("p v r j -> p (v r j)"),
+            )
+
+        def x_quantise_pair(i):
+            nc.vector.quantize_mx(
+                out=x_cod[i][:].rearrange("p n v r -> p (n v r)").bitcast(FP8X4),
+                scales=x_csc[i][:].rearrange("p n v r -> p (n v r)"),
+                in_=x_val[i][:].rearrange("p n v r j -> p (n v r j)"),
+            )
+
+        def preact(r, b):
+            bank = new_bank(("xw", r, b), "preact", PREACT_BANKS)
+            for v in range(2):
+                nc.tensor.matmul_mx(
+                    out=bank[:],
+                    lhsT=x_cod[r // 2][:, r % 2, v, :].bitcast(FP8X4),
+                    lhsT_scale=x_csc[r // 2][:, r % 2, v, :],
+                    rhs=w_wrd[b][:, v, :].bitcast(FP4X4),
+                    rhs_scale=w_scl[:, v, b * NODE_HALF : (b + 1) * NODE_HALF],
+                    start=(v == 0),
+                    stop=(v == 1),
+                )
+
+        def tanh(r, b):
+            nc.scalar.activation(out=h[b, r // J][:, r % J, :], in_=banks["xw", r, b][:], func=ACT.Tanh)
+
+        def g_turn(i):
+            bank = new_bank(("g", i), "turned", TURNED_BANKS)
+            for n in range(2):
+                words = hid[i // 2][:, 2 * (i % 2) + n, :].bitcast(F32)
+                for u in range(2):
+                    at = (2 * n + u) * P
+                    nc.tensor.transpose(bank[:, at : at + P], words[:, u:256:2], ident[:])
+
+        def g_copy_out(i):
+            n = 2 * (i % 2)
+            nc.scalar.copy(
+                g_val[i // 2][:, n : n + 2].bitcast(F32),
+                banks["g", i][:].rearrange("p (n u r) -> p n r u", n=2, u=2),
+            )
+
+        def g_quantise(v):
+            nc.vector.quantize_mx(
+                out=g_cod[v][:].rearrange("p n r -> p (n r)").bitcast(FP8X4),
+                scales=g_csc[v][:].rearrange("p n r -> p (n r)"),
+                in_=g_val[v][:].rearrange("p n r j -> p (n r j)"),
+            )
+
+        def beta_product(v, qb):
+            bank = new_bank(("gb", v, qb), "product", PRODUCT_BANKS)
+            for j in range(J):
+                nc.tensor.matmul_mx(
+                    out=bank[:, j * P : (j + 1) * P],
+                    lhsT=g_cod[v][:, j, :].bitcast(FP8X4),
+                    lhsT_scale=g_csc[v][:, j, :],
+                    rhs=b_wrd[:, qb * P * FP4_BYTES : (qb + 1) * P * FP4_BYTES].bitcast(FP4X4),
+                    rhs_scale=b_scl[:, qb * P : (qb + 1) * P],
+                    start=True,
+                    stop=True,
+                )
+
+        def residual(v, qb):
+            cols = slice(qb * P, (qb + 1) * P)
+            nc.vector.tensor_tensor(
+                out=e_val[v][:, cols, :].rearrange("p (c i) j -> p c j i", i=4),
+                in0=tgt[v][:, :, cols].rearrange("p j (c i) -> p c j i", i=4),
+                in1=banks["gb", v, qb][:].rearrange("p (j c i) -> p c j i", j=J, i=4),
+                op=ALU.subtract,
+            )
+
+        def e_quantise(v):
+            nc.vector.quantize_mx(
+                out=e_cod[v][:].bitcast(FP8X4), scales=e_csc[v][:], in_=e_val[v][:].rearrange("p q j -> p (q j)")
+            )
+
+        def h_turn(b, v, nb):
+            bank = new_bank(("h", b, v, nb), "turned", TURNED_BANKS)
+            for j in range(J):
+                nc.tensor.transpose(bank[:, j * P : (j + 1) * P], h[b, v][:, j, nb * P : (nb + 1) * P], ident[:])
+
+        def energy(b, v, nb):
+            nc.scalar.activation(
+                out=squares[:],
+                in_=banks["h", b, v, nb][:],
+                func=ACT.Square,
+                accum_out=hh_part[b][:, nb, v : v + 1],
+            )
+
+        def energy_inverse(b):
+            nc.vector.tensor_tensor(out=hh_sum[b][:], in0=hh_part[b][:, :, 0], in1=hh_part[b][:, :, 1], op=ALU.add)
+            nc.vector.reciprocal(out=hh_inv[b][:], in_=hh_sum[b][:])
+
+        def apply_gain(b, v, part):
+            cols = slice(part * 256, (part + 1) * 256)
+            nc.vector.tensor_tensor(
+                out=hs_val[b, v][:, cols, :].rearrange("p (c i) j -> p c j i", i=4),
+                in0=h[b, v][:, :, cols].rearrange("p j (c i) -> p c j i", i=4),
+                in1=gain_q[:, v, :].unsqueeze(1).unsqueeze(3).to_broadcast([P, 64, J, 4]),
+                op=ALU.mult,
+            )
+
+        def hs_quantise(b, v, n0, n1):
+            nc.vector.quantize_mx(
+                out=hs_cod[b, v][:, n0:n1].bitcast(FP8X4),
+                scales=hs_csc[b, v][:, n0:n1],
+                in_=hs_val[b, v][:, n0:n1, :].rearrange("p f j -> p (f j)"),
+            )
+
+        def correlate(b, nb):
+            bank = new_bank(("c", b, nb), "product", PRODUCT_BANKS)
+            cols = slice(nb * P, (nb + 1) * P)
+            for v in range(2):
+                nc.tensor.matmul_mx(
+                    out=bank[:],
+                    lhsT=hs_cod[b, v][:, cols].bitcast(FP8X4),
+                    lhsT_scale=hs_csc[b, v][:, cols],
+                    rhs=e_cod[v][:].bitcast(FP8X4),
+                    rhs_scale=e_csc[v][:],
+                    start=(v == 0),
+                    stop=(v == 1),
+                )
+
+        def square(b, nb):
+            nc.scalar.activation(out=c_sq[4 * b + nb][:], in_=banks["c", b, nb][:], func=ACT.Square)
+
+        def score(b, nb, parts=1):
+            i = 4 * b + nb
+            width = Q // parts
+            for n in range(parts):
+                cols = slice(n * width, (n + 1) * width)
+                nc.vector.scalar_tensor_tensor(
+                    out=res[i][:, cols],
+                    in0=c_sq[i][:, cols],
+                    scalar=hh_inv[b][:, nb : nb + 1],
+                    in1=tau_b[:, cols],
+                    op0=ALU.mult,
+                    op1=ALU.subtract,
+                )
+                nc.sync.dma_start(out=out[i * P : (i + 1) * P, cols], in_=res[i][:, cols])
+
+        make_identity(nc, ident[:])
+        nc.vector.memset(dummy[:], 0.0)
+        nc.scalar.activation(out=dummy[:, 1:2], in_=dummy[:, 0:1], func=ACT.Tanh)
+        nc.vector.memset(w_scl[:].rearrange("p v n -> p (v n)").bitcast(I32), 0)
+        nc.vector.memset(b_scl[:].bitcast(I32), 0)
+        nc.vector.memset(zeros[:], 0.0)
+        warm = new_bank("warm", "product", PRODUCT_BANKS)
+        for n in range(WARM_UP_MATMULS):
+            nc.tensor.matmul(warm[:], zeros[:, 0:P], zeros[:], start=True, stop=True)
+
+        load = nc.sync.dma_start
+        x_rows = x_bytes.rearrange("(v p j) k -> v p j k", p=P, j=J)
+        hid_rows = hidden.rearrange("(v p j) k -> v p j k", p=P, j=J)
+        tgt_rows = target.rearrange("(v p j) q -> v p j q", p=P, j=J)
+        w_rows = w_words.rearrange("v p n -> p v n")
+
+        def load_x(i):
+            r = sum(X_LOADS[:i])
+            load(out=x_raw[i][:], in_=x_rows[r // J][:, r % J : r % J + X_LOADS[i], :])
+
+        def load_w(b):
+            width = FP4_BYTES * NODE_HALF
+            load(out=w_wrd[b][:].bitcast(I32), in_=w_rows[:, :, b * width : (b + 1) * width].bitcast(I32))
+
+        load_x(0)
+        load_x(1)
+        load(out=x_scl[:], in_=x_scale.rearrange("o (v p j) -> p (o v) j", p=P, j=J))
+        load_x(2)
+        load_w(0)
+        for quadrant in range(4):
+            load(
+                out=w_scl[32 * quadrant : 32 * quadrant + 4, :, :].bitcast(I32),
+                in_=w_scales[:, 4 * quadrant : 4 * quadrant + 4, :].rearrange("v r n -> r v n").bitcast(I32),
+            )
+        load_x(3)
+        load(out=gain_q[:], in_=gain.rearrange("(v p j) -> p v j", p=P, j=J))
+        load(out=hid[0][:], in_=hid_rows[0])
+        load_w(1)
+        load(out=b_wrd[:].bitcast(I32), in_=beta_words[0].bitcast(I32))
+        for quadrant in range(4):
+            load(
+                out=b_scl[32 * quadrant : 32 * quadrant + 4, :].bitcast(I32),
+                in_=beta_scales[0][4 * quadrant : 4 * quadrant + 4, :].bitcast(I32),
+            )
+        load(out=hid[1][:], in_=hid_rows[1])
+        load(out=tgt[0][:], in_=tgt_rows[0])
+        load(out=tgt[1][:], in_=tgt_rows[1])
+        load(out=tau_b[:], in_=tau.partition_broadcast(P))
+
+        with tc.manual_schedule():
+            for r in range(-3, ROW_TILES + 2):
+                if r + 3 == 0:
+                    x_widen(nc.vector.tensor_copy, 0, 0, 512)
+                    x_widen(nc.scalar.copy, 0, 512, D)
+                elif r + 3 == 1:
+                    x_widen(nc.vector.tensor_copy, 1, 0, D)
+                elif r + 3 < ROW_TILES:
+                    x_widen(nc.scalar.copy, r + 3, 0, D)
+                if 0 <= r + 1 < ROW_TILES:
+                    x_turn(r + 1)
+                if 0 <= r - 5 < 4:
+                    g_turn(r - 5)
+                    g_copy_out(r - 5)
+                if 0 <= r < ROW_TILES:
+                    x_scale_out(r, 0)
+                if 0 <= r - 1 < SINGLE_ROW_TILES:
+                    x_quantise(r - 1)
+                elif SINGLE_ROW_TILES < r <= ROW_TILES and r % 2 == 0:
+                    x_quantise_pair(r // 2 - 1)
+                if 0 <= r < ROW_TILES:
+                    x_scale_out(r, 1)
+                if 0 <= r - 2:
+                    preact(r - 2, 0)
+                    tanh(r - 2, 0)
+                if 0 <= r - 5 < 2:
+                    preact(r - 5, 1)
+                    tanh(r - 5, 1)
+                if r == 7:
+                    apply_gain(0, 0, 0)
+                if r == 8:
+                    g_quantise(0)
+
+            beta_product(0, 0)
+            beta_product(0, 1)
+            for step in range(0, 8, 2):
+                pair = (divmod(step, 4), divmod(step + 1, 4))
+                ahead = (step + 2, step + 3) if step < 6 else ()
+                for k in ahead:
+                    preact(k, 1)
+                for k in ahead:
+                    beta_product(*divmod(k, 4))
+                for k in ahead:
+                    tanh(k, 1)
+                for v, nb in pair:
+                    h_turn(0, v, nb)
+                if step < 6:
+                    apply_gain(0, *divmod(step // 2 + 1, 2))
+                if step == 0:
+                    g_quantise(1)
+                for v, qb in pair:
+                    residual(v, qb)
+                for v, nb in pair:
+                    energy(0, v, nb)
+                if step == 4:
+                    e_quantise(0)
+                else:
+                    if step > 0:
+                        hs_quantise(0, step // 4, 0, NODE_HALF)
+            e_quantise(1)
+
+            for step in range(0, 8, 2):
+                pair = (divmod(step, 4), divmod(step + 1, 4))
+                for v, nb in pair:
+                    h_turn(1, v, nb)
+                blocks = (step - 2, step - 1) if step in (2, 4) else ()
+                for nb in blocks:
+                    correlate(0, nb)
+                for v, nb in pair:
+                    energy(1, v, nb)
+                for nb in blocks:
+                    square(0, nb)
+            apply_gain(1, 0, 0)
+            apply_gain(1, 0, 1)
+            energy_inverse(0)
+            apply_gain(1, 1, 0)
+            hs_quantise(1, 0, 0, NODE_HALF)
+            apply_gain(1, 1, 1)
+            hs_quantise(1, 1, 0, 256)
+            hs_quantise(1, 1, 256, NODE_HALF)
+
+            for nb in (0, 1):
+                correlate(1, nb)
+                square(1, nb)
+            for nb in (0, 1, 2):
+                score(0, nb)
+            energy_inverse(1)
+            score(0, 3)
+            for nb in range(4):
+                if nb + 2 < 4:
+                    correlate(1, nb + 2)
+                    square(1, nb + 2)
+                score(1, nb, parts=LAST_BLOCK_PARTS if nb == 3 else 1)

@@ -22,16 +22,21 @@ J = 4
 BANK = 512
 ROW_TILES = N // P
 NODE_HALF = F // 2
+NODE_QUARTER = F // 4
 FP4_BYTES = 2
 
-X_LOADS = (1, 1, 2, 4)
-SINGLE_ROW_TILES = 4
-WARM_UP_MATMULS = 5
+X_LOADS = (1, 1, 2, 2, 2)
+WARM_UP_MATMULS = 3
 LAST_BLOCK_PARTS = 2
 
-TURNED_BANKS = 4
-PREACT_BANKS = 2
-PRODUCT_BANKS = 2
+BANK_RINGS = {
+    "warm": (7,),
+    "turn in": (0, 1, 2, 3),
+    "preact": (4, 5),
+    "beta": (6, 7, 3),
+    "turn h": (0, 1, 2),
+    "corr": (6, 7, 3),
+}
 
 
 def tile_stochasticconfigurationcandidatescores_w4_kernel(
@@ -68,13 +73,13 @@ def tile_stochasticconfigurationcandidatescores_w4_kernel(
         e_csc = [sbuf("e_csc%d" % v, [P, Q], U8) for v in range(2)]
         chunks = [(b, v) for b in range(2) for v in range(2)]
         h = {k: sbuf("h%d%d" % k, [P, J, NODE_HALF], F32) for k in chunks}
-        hs_val = {k: sbuf("hs_val%d%d" % k, [P, NODE_HALF, J], BF16) for k in chunks}
-        hs_cod = {k: sbuf("hs_cod%d%d" % k, [P, NODE_HALF], U32) for k in chunks}
-        hs_csc = {k: sbuf("hs_csc%d%d" % k, [P, NODE_HALF], U8) for k in chunks}
-        hh_part = [sbuf("hh_part%d" % b, [P, 4, 2], F32) for b in range(2)]
-        hh_sum = [sbuf("hh_sum%d" % b, [P, 4], F32) for b in range(2)]
-        hh_inv = [sbuf("hh_inv%d" % b, [P, 4], F32) for b in range(2)]
-        squares = sbuf("squares", [P, BANK], BF16)
+        hs_val = [sbuf("hs_val%d" % n, [P, 2, NODE_QUARTER, J], BF16) for n in range(4)]
+        hs_cod = [sbuf("hs_cod%d" % n, [P, 2, NODE_QUARTER], U32) for n in range(4)]
+        hs_csc = [sbuf("hs_csc%d" % n, [P, 2, NODE_QUARTER], U8) for n in range(4)]
+        hh_part = [sbuf("hh_part%d" % n, [P, 2, 2], F32) for n in range(4)]
+        hh_sum = [sbuf("hh_sum%d" % n, [P, 2], F32) for n in range(4)]
+        hh_inv = [sbuf("hh_inv%d" % n, [P, 2], F32) for n in range(4)]
+        squares = [sbuf("squares%d" % v, [P, BANK], BF16) for v in range(2)]
         c_sq = [sbuf("c_sq%d" % i, [P, Q], F32) for i in range(8)]
         res = [sbuf("res%d" % i, [P, Q], F32) for i in range(8)]
 
@@ -84,8 +89,13 @@ def tile_stochasticconfigurationcandidatescores_w4_kernel(
 
         banks = {}
 
-        def new_bank(key, tag, bufs):
-            banks[key] = psum.tile([P, BANK], F32, name="bank_" + tag, tag=tag, bufs=bufs)
+        taken = {kind: [] for kind in BANK_RINGS}
+
+        def new_bank(key, kind):
+            ring = BANK_RINGS[kind]
+            number = ring[len(taken[kind]) % len(ring)]
+            taken[kind].append(key)
+            banks[key] = psum.tile([P, BANK], F32, name="bank%d" % number, tag="bank%d" % number, bufs=1)
             return banks[key]
 
         x_place = [(i, n) for i, count in enumerate(X_LOADS) for n in range(count)]
@@ -95,21 +105,20 @@ def tile_stochasticconfigurationcandidatescores_w4_kernel(
             copy(x_wide[r][:, k0:k1], x_raw[i][:, n, k0:k1].bitcast(FP8))
 
         def x_turn(r):
-            bank = new_bank(("x", r), "turned", TURNED_BANKS)
+            bank = new_bank(("x", r), "turn in")
             words = x_wide[r][:].bitcast(F32)
             for v in range(2):
                 for u in range(2):
-                    at = (2 * v + u) * P
+                    at = (2 * u + v) * P
                     nc.tensor.transpose(
                         bank[:, at : at + P], words[:, 256 * v + u : 256 * (v + 1) : 2], ident[:]
                     )
 
-        def x_scale_out(r, v):
-            turned = banks["x", r][:, 256 * v : 256 * (v + 1)].bitcast(BF16)
+        def x_scale_out(r):
             nc.vector.tensor_tensor(
-                out=x_val[r // 2][:, r % 2, v].rearrange("p r (u e) -> p r u e", u=2),
-                in0=turned.rearrange("p (u r e) -> p r u e", u=2, e=2),
-                in1=x_scl[:, v, :].rearrange("p (u e) -> p u e", u=2).unsqueeze(1).to_broadcast([P, P, 2, 2]),
+                out=x_val[r // 2][:, r % 2].rearrange("p v r (u e) -> p v r u e", u=2),
+                in0=banks["x", r][:].bitcast(BF16).rearrange("p (u v r e) -> p v r u e", u=2, v=2, e=2),
+                in1=x_scl[:].rearrange("p v (u e) -> p v u e", u=2).unsqueeze(2).to_broadcast([P, 2, P, 2, 2]),
                 op=ALU.mult,
             )
 
@@ -121,15 +130,8 @@ def tile_stochasticconfigurationcandidatescores_w4_kernel(
                 in_=x_val[i][:, n].rearrange("p v r j -> p (v r j)"),
             )
 
-        def x_quantise_pair(i):
-            nc.vector.quantize_mx(
-                out=x_cod[i][:].rearrange("p n v r -> p (n v r)").bitcast(FP8X4),
-                scales=x_csc[i][:].rearrange("p n v r -> p (n v r)"),
-                in_=x_val[i][:].rearrange("p n v r j -> p (n v r j)"),
-            )
-
         def preact(r, b):
-            bank = new_bank(("xw", r, b), "preact", PREACT_BANKS)
+            bank = new_bank(("xw", r, b), "preact")
             for v in range(2):
                 nc.tensor.matmul_mx(
                     out=bank[:],
@@ -144,8 +146,12 @@ def tile_stochasticconfigurationcandidatescores_w4_kernel(
         def tanh(r, b):
             nc.scalar.activation(out=h[b, r // J][:, r % J, :], in_=banks["xw", r, b][:], func=ACT.Tanh)
 
+        def nodes(r, b):
+            preact(r, b)
+            tanh(r, b)
+
         def g_turn(i):
-            bank = new_bank(("g", i), "turned", TURNED_BANKS)
+            bank = new_bank(("g", i), "turn in")
             for n in range(2):
                 words = hid[i // 2][:, 2 * (i % 2) + n, :].bitcast(F32)
                 for u in range(2):
@@ -159,6 +165,10 @@ def tile_stochasticconfigurationcandidatescores_w4_kernel(
                 banks["g", i][:].rearrange("p (n u r) -> p n r u", n=2, u=2),
             )
 
+        def g_in(i):
+            g_turn(i)
+            g_copy_out(i)
+
         def g_quantise(v):
             nc.vector.quantize_mx(
                 out=g_cod[v][:].rearrange("p n r -> p (n r)").bitcast(FP8X4),
@@ -167,7 +177,7 @@ def tile_stochasticconfigurationcandidatescores_w4_kernel(
             )
 
         def beta_product(v, qb):
-            bank = new_bank(("gb", v, qb), "product", PRODUCT_BANKS)
+            bank = new_bank(("gb", v, qb), "beta")
             for j in range(J):
                 nc.tensor.matmul_mx(
                     out=bank[:, j * P : (j + 1) * P],
@@ -193,65 +203,82 @@ def tile_stochasticconfigurationcandidatescores_w4_kernel(
                 out=e_cod[v][:].bitcast(FP8X4), scales=e_csc[v][:], in_=e_val[v][:].rearrange("p q j -> p (q j)")
             )
 
-        def h_turn(b, v, nb):
-            bank = new_bank(("h", b, v, nb), "turned", TURNED_BANKS)
+        def h_turn(i, v):
+            bank = new_bank(("h", i, v), "turn h")
+            at = i % 4 * P
             for j in range(J):
-                nc.tensor.transpose(bank[:, j * P : (j + 1) * P], h[b, v][:, j, nb * P : (nb + 1) * P], ident[:])
+                nc.tensor.transpose(bank[:, j * P : (j + 1) * P], h[i // 4, v][:, j, at : at + P], ident[:])
 
-        def energy(b, v, nb):
+        def energy(i, v):
             nc.scalar.activation(
-                out=squares[:],
-                in_=banks["h", b, v, nb][:],
+                out=squares[i % 2][:],
+                in_=banks["h", i, v][:],
                 func=ACT.Square,
-                accum_out=hh_part[b][:, nb, v : v + 1],
+                accum_out=hh_part[i // 2][:, i % 2, v : v + 1],
             )
 
-        def energy_inverse(b):
-            nc.vector.tensor_tensor(out=hh_sum[b][:], in0=hh_part[b][:, :, 0], in1=hh_part[b][:, :, 1], op=ALU.add)
-            nc.vector.reciprocal(out=hh_inv[b][:], in_=hh_sum[b][:])
+        def node_energy(i, v):
+            h_turn(i, v)
+            energy(i, v)
 
-        def apply_gain(b, v, part):
-            cols = slice(part * 256, (part + 1) * 256)
+        def energy_sum(n):
+            nc.vector.tensor_tensor(out=hh_sum[n][:], in0=hh_part[n][:, :, 0], in1=hh_part[n][:, :, 1], op=ALU.add)
+
+        def energy_inverse(n):
+            nc.vector.reciprocal(out=hh_inv[n][:], in_=hh_sum[n][:])
+
+        def apply_gain(n, v):
+            at = n % 2 * NODE_QUARTER
             nc.vector.tensor_tensor(
-                out=hs_val[b, v][:, cols, :].rearrange("p (c i) j -> p c j i", i=4),
-                in0=h[b, v][:, :, cols].rearrange("p j (c i) -> p c j i", i=4),
-                in1=gain_q[:, v, :].unsqueeze(1).unsqueeze(3).to_broadcast([P, 64, J, 4]),
+                out=hs_val[n][:, v].rearrange("p (c i) j -> p c j i", i=4),
+                in0=h[n // 2, v][:, :, at : at + NODE_QUARTER].rearrange("p j (c i) -> p c j i", i=4),
+                in1=gain_q[:, v, :].unsqueeze(1).unsqueeze(3).to_broadcast([P, NODE_QUARTER // 4, J, 4]),
                 op=ALU.mult,
             )
 
-        def hs_quantise(b, v, n0, n1):
+        def hs_quantise(n):
             nc.vector.quantize_mx(
-                out=hs_cod[b, v][:, n0:n1].bitcast(FP8X4),
-                scales=hs_csc[b, v][:, n0:n1],
-                in_=hs_val[b, v][:, n0:n1, :].rearrange("p f j -> p (f j)"),
+                out=hs_cod[n][:].rearrange("p v f -> p (v f)").bitcast(FP8X4),
+                scales=hs_csc[n][:].rearrange("p v f -> p (v f)"),
+                in_=hs_val[n][:].rearrange("p v f j -> p (v f j)"),
             )
 
-        def correlate(b, nb):
-            bank = new_bank(("c", b, nb), "product", PRODUCT_BANKS)
-            cols = slice(nb * P, (nb + 1) * P)
+        def hs_quantise_half(n, v):
+            nc.vector.quantize_mx(
+                out=hs_cod[n][:, v].bitcast(FP8X4),
+                scales=hs_csc[n][:, v],
+                in_=hs_val[n][:, v].rearrange("p f j -> p (f j)"),
+            )
+
+        def correlate(i):
+            bank = new_bank(("c", i), "corr")
+            cols = slice(i % 2 * P, (i % 2 + 1) * P)
             for v in range(2):
                 nc.tensor.matmul_mx(
                     out=bank[:],
-                    lhsT=hs_cod[b, v][:, cols].bitcast(FP8X4),
-                    lhsT_scale=hs_csc[b, v][:, cols],
+                    lhsT=hs_cod[i // 2][:, v, cols].bitcast(FP8X4),
+                    lhsT_scale=hs_csc[i // 2][:, v, cols],
                     rhs=e_cod[v][:].bitcast(FP8X4),
                     rhs_scale=e_csc[v][:],
                     start=(v == 0),
                     stop=(v == 1),
                 )
 
-        def square(b, nb):
-            nc.scalar.activation(out=c_sq[4 * b + nb][:], in_=banks["c", b, nb][:], func=ACT.Square)
+        def square(i):
+            nc.scalar.activation(out=c_sq[i][:], in_=banks["c", i][:], func=ACT.Square)
 
-        def score(b, nb, parts=1):
-            i = 4 * b + nb
+        def correlation_squared(i):
+            correlate(i)
+            square(i)
+
+        def score(i, parts=1):
             width = Q // parts
-            for n in range(parts):
-                cols = slice(n * width, (n + 1) * width)
+            for part in range(parts):
+                cols = slice(part * width, (part + 1) * width)
                 nc.vector.scalar_tensor_tensor(
                     out=res[i][:, cols],
                     in0=c_sq[i][:, cols],
-                    scalar=hh_inv[b][:, nb : nb + 1],
+                    scalar=hh_inv[i // 2][:, i % 2 : i % 2 + 1],
                     in1=tau_b[:, cols],
                     op0=ALU.mult,
                     op1=ALU.subtract,
@@ -261,12 +288,16 @@ def tile_stochasticconfigurationcandidatescores_w4_kernel(
         make_identity(nc, ident[:])
         nc.vector.memset(dummy[:], 0.0)
         nc.scalar.activation(out=dummy[:, 1:2], in_=dummy[:, 0:1], func=ACT.Tanh)
+        nc.vector.memset(zeros[:], 0.0)
         nc.vector.memset(w_scl[:].rearrange("p v n -> p (v n)").bitcast(I32), 0)
         nc.vector.memset(b_scl[:].bitcast(I32), 0)
-        nc.vector.memset(zeros[:], 0.0)
-        warm = new_bank("warm", "product", PRODUCT_BANKS)
-        for n in range(WARM_UP_MATMULS):
-            nc.tensor.matmul(warm[:], zeros[:, 0:P], zeros[:], start=True, stop=True)
+        warm = new_bank("warm", "warm")
+
+        def warm_up(count):
+            for n in range(count):
+                nc.tensor.matmul(warm[:], zeros[:, 0:P], zeros[:], start=True, stop=True)
+
+        warm_up(WARM_UP_MATMULS)
 
         load = nc.sync.dma_start
         x_rows = x_bytes.rearrange("(v p j) k -> v p j k", p=P, j=J)
@@ -282,121 +313,122 @@ def tile_stochasticconfigurationcandidatescores_w4_kernel(
             width = FP4_BYTES * NODE_HALF
             load(out=w_wrd[b][:].bitcast(I32), in_=w_rows[:, :, b * width : (b + 1) * width].bitcast(I32))
 
+        def load_scales(tile, rows):
+            for quadrant in range(4):
+                load(
+                    out=tile[32 * quadrant : 32 * quadrant + 4].bitcast(I32),
+                    in_=rows[4 * quadrant : 4 * quadrant + 4].bitcast(I32),
+                )
+
         load_x(0)
         load_x(1)
         load(out=x_scl[:], in_=x_scale.rearrange("o (v p j) -> p (o v) j", p=P, j=J))
         load_x(2)
-        load_w(0)
-        for quadrant in range(4):
-            load(
-                out=w_scl[32 * quadrant : 32 * quadrant + 4, :, :].bitcast(I32),
-                in_=w_scales[:, 4 * quadrant : 4 * quadrant + 4, :].rearrange("v r n -> r v n").bitcast(I32),
-            )
-        load_x(3)
-        load(out=gain_q[:], in_=gain.rearrange("(v p j) -> p v j", p=P, j=J))
         load(out=hid[0][:], in_=hid_rows[0])
-        load_w(1)
-        load(out=b_wrd[:].bitcast(I32), in_=beta_words[0].bitcast(I32))
-        for quadrant in range(4):
-            load(
-                out=b_scl[32 * quadrant : 32 * quadrant + 4, :].bitcast(I32),
-                in_=beta_scales[0][4 * quadrant : 4 * quadrant + 4, :].bitcast(I32),
-            )
+        load_x(3)
+        load_w(0)
+        load_scales(w_scl, w_scales.rearrange("v r n -> r v n"))
+        load_x(4)
         load(out=hid[1][:], in_=hid_rows[1])
+        load(out=b_wrd[:].bitcast(I32), in_=beta_words[0].bitcast(I32))
+        load_scales(b_scl, beta_scales[0])
+        load_w(1)
         load(out=tgt[0][:], in_=tgt_rows[0])
+        load(out=gain_q[:], in_=gain.rearrange("(v p j) -> p v j", p=P, j=J))
         load(out=tgt[1][:], in_=tgt_rows[1])
         load(out=tau_b[:], in_=tau.partition_broadcast(P))
 
         with tc.manual_schedule():
-            for r in range(-3, ROW_TILES + 2):
-                if r + 3 == 0:
-                    x_widen(nc.vector.tensor_copy, 0, 0, 512)
-                    x_widen(nc.scalar.copy, 0, 512, D)
-                elif r + 3 == 1:
-                    x_widen(nc.vector.tensor_copy, 1, 0, D)
-                elif r + 3 < ROW_TILES:
-                    x_widen(nc.scalar.copy, r + 3, 0, D)
-                if 0 <= r + 1 < ROW_TILES:
-                    x_turn(r + 1)
-                if 0 <= r - 5 < 4:
-                    g_turn(r - 5)
-                    g_copy_out(r - 5)
-                if 0 <= r < ROW_TILES:
-                    x_scale_out(r, 0)
-                if 0 <= r - 1 < SINGLE_ROW_TILES:
-                    x_quantise(r - 1)
-                elif SINGLE_ROW_TILES < r <= ROW_TILES and r % 2 == 0:
-                    x_quantise_pair(r // 2 - 1)
-                if 0 <= r < ROW_TILES:
-                    x_scale_out(r, 1)
-                if 0 <= r - 2:
-                    preact(r - 2, 0)
-                    tanh(r - 2, 0)
-                if 0 <= r - 5 < 2:
-                    preact(r - 5, 1)
-                    tanh(r - 5, 1)
-                if r == 7:
-                    apply_gain(0, 0, 0)
-                if r == 8:
+            x_widen(nc.vector.tensor_copy, 0, 0, BANK)
+            x_widen(nc.vector.tensor_copy, 0, BANK, D)
+            x_widen(nc.vector.tensor_copy, 1, 0, D)
+            x_widen(nc.scalar.copy, 2, 0, D)
+            x_widen(nc.scalar.copy, 3, 0, D)
+            x_turn(0)
+            x_turn(1)
+            warm_up(2)
+            x_turn(2)
+            x_scale_out(0)
+            g_in(0)
+            x_turn(3)
+            x_widen(nc.scalar.copy, 4, 0, D)
+            for r in range(1, ROW_TILES + 1):
+                if r < ROW_TILES:
+                    x_scale_out(r)
+                if r == ROW_TILES:
                     g_quantise(0)
-
-            beta_product(0, 0)
-            beta_product(0, 1)
-            for step in range(0, 8, 2):
-                pair = (divmod(step, 4), divmod(step + 1, 4))
-                ahead = (step + 2, step + 3) if step < 6 else ()
-                for k in ahead:
-                    preact(k, 1)
-                for k in ahead:
-                    beta_product(*divmod(k, 4))
-                for k in ahead:
-                    tanh(k, 1)
-                for v, nb in pair:
-                    h_turn(0, v, nb)
-                if step < 6:
-                    apply_gain(0, *divmod(step // 2 + 1, 2))
-                if step == 0:
+                x_quantise(r - 1)
+                if r + 4 < ROW_TILES:
+                    x_widen(nc.scalar.copy, r + 4, 0, D)
+                if r == ROW_TILES:
+                    beta_product(0, 0)
+                    beta_product(0, 1)
+                nodes(r - 1, 0)
+                if r + 3 < ROW_TILES:
+                    x_turn(r + 3)
+                elif r < ROW_TILES:
+                    g_in(r - 4)
+            apply_gain(0, 0)
+            beta_product(0, 2)
+            for k in range(4):
+                v, qb = divmod(2 * k, 4)
+                residual(v, qb)
+                nodes(2 * k, 1)
+                if k == 0:
                     g_quantise(1)
-                for v, qb in pair:
-                    residual(v, qb)
-                for v, nb in pair:
-                    energy(0, v, nb)
-                if step == 4:
+                if 2 * k + 3 < 8:
+                    beta_product(*divmod(2 * k + 3, 4))
+                residual(v, qb + 1)
+                nodes(2 * k + 1, 1)
+                if 2 * k + 4 < 8:
+                    beta_product(*divmod(2 * k + 4, 4))
+                i, u = ((0, 0), (0, 1), (2, 0), (2, 1))[k]
+                node_energy(i, u)
+                node_energy(i + 1, u)
+                if k < 3:
+                    apply_gain(*divmod(k + 1, 2))
+                if k == 1:
                     e_quantise(0)
-                else:
-                    if step > 0:
-                        hs_quantise(0, step // 4, 0, NODE_HALF)
+                if k == 2:
+                    hs_quantise(0)
+                    energy_sum(0)
+            apply_gain(2, 0)
             e_quantise(1)
-
-            for step in range(0, 8, 2):
-                pair = (divmod(step, 4), divmod(step + 1, 4))
-                for v, nb in pair:
-                    h_turn(1, v, nb)
-                blocks = (step - 2, step - 1) if step in (2, 4) else ()
-                for nb in blocks:
-                    correlate(0, nb)
-                for v, nb in pair:
-                    energy(1, v, nb)
-                for nb in blocks:
-                    square(0, nb)
-            apply_gain(1, 0, 0)
-            apply_gain(1, 0, 1)
+            correlation_squared(0)
+            node_energy(4, 0)
+            node_energy(5, 0)
+            correlation_squared(1)
             energy_inverse(0)
-            apply_gain(1, 1, 0)
-            hs_quantise(1, 0, 0, NODE_HALF)
-            apply_gain(1, 1, 1)
-            hs_quantise(1, 1, 0, 256)
-            hs_quantise(1, 1, 256, NODE_HALF)
-
-            for nb in (0, 1):
-                correlate(1, nb)
-                square(1, nb)
-            for nb in (0, 1, 2):
-                score(0, nb)
+            hs_quantise(1)
+            energy_sum(1)
+            node_energy(4, 1)
+            node_energy(5, 1)
+            correlation_squared(2)
+            apply_gain(2, 1)
             energy_inverse(1)
-            score(0, 3)
-            for nb in range(4):
-                if nb + 2 < 4:
-                    correlate(1, nb + 2)
-                    square(1, nb + 2)
-                score(1, nb, parts=LAST_BLOCK_PARTS if nb == 3 else 1)
+            node_energy(6, 0)
+            node_energy(7, 0)
+            correlation_squared(3)
+            apply_gain(3, 0)
+            hs_quantise(2)
+            score(0)
+            node_energy(6, 1)
+            node_energy(7, 1)
+            correlation_squared(4)
+            apply_gain(3, 1)
+            hs_quantise_half(3, 0)
+            energy_sum(2)
+            hs_quantise_half(3, 1)
+            energy_inverse(2)
+            correlation_squared(5)
+            correlation_squared(6)
+            correlation_squared(7)
+            score(1)
+            score(2)
+            score(3)
+            energy_sum(3)
+            score(4)
+            energy_inverse(3)
+            score(5)
+            score(6)
+            score(7, parts=LAST_BLOCK_PARTS)

@@ -22,7 +22,7 @@ J = 4
 BANK = 512
 ROW_TILES = N // P
 NODE_HALF = F // 2
-NODE_QUARTER = F // 4
+RUN = 4
 FP4_BYTES = 2
 
 X_LOADS = (1, 1, 2, 2, 2)
@@ -31,11 +31,12 @@ LAST_BLOCK_PARTS = 2
 
 BANK_RINGS = {
     "warm": (7,),
+    "spread": (4, 5),
     "turn in": (0, 1, 2, 3),
     "preact": (4, 5),
     "beta": (6, 7, 3),
     "turn h": (0, 1, 2),
-    "corr": (6, 7, 3),
+    "corr": (6, 7, 3, 4),
 }
 
 
@@ -61,7 +62,8 @@ def tile_stochasticconfigurationcandidatescores_w4_kernel(
         gain_q = sbuf("gain_q", [P, 2, J], BF16)
         tau_b = sbuf("tau_b", [P, Q], BF16)
 
-        x_wide = [sbuf("x_wide%d" % r, [P, D], BF16) for r in range(ROW_TILES)]
+        scale_b = sbuf("scale_b", [P, D], F32)
+        x_wide = [sbuf("x_wide%d" % i, [P, n, D], BF16) for i, n in enumerate(X_LOADS)]
         x_val = [sbuf("x_val%d" % i, [P, 2, 2, P, J], BF16) for i in range(4)]
         x_cod = [sbuf("x_cod%d" % i, [P, 2, 2, P], U32) for i in range(4)]
         x_csc = [sbuf("x_csc%d" % i, [P, 2, 2, P], U8) for i in range(4)]
@@ -73,12 +75,12 @@ def tile_stochasticconfigurationcandidatescores_w4_kernel(
         e_csc = [sbuf("e_csc%d" % v, [P, Q], U8) for v in range(2)]
         chunks = [(b, v) for b in range(2) for v in range(2)]
         h = {k: sbuf("h%d%d" % k, [P, J, NODE_HALF], F32) for k in chunks}
-        hs_val = [sbuf("hs_val%d" % n, [P, 2, NODE_QUARTER, J], BF16) for n in range(4)]
-        hs_cod = [sbuf("hs_cod%d" % n, [P, 2, NODE_QUARTER], U32) for n in range(4)]
-        hs_csc = [sbuf("hs_csc%d" % n, [P, 2, NODE_QUARTER], U8) for n in range(4)]
-        hh_part = [sbuf("hh_part%d" % n, [P, 2, 2], F32) for n in range(4)]
-        hh_sum = [sbuf("hh_sum%d" % n, [P, 2], F32) for n in range(4)]
-        hh_inv = [sbuf("hh_inv%d" % n, [P, 2], F32) for n in range(4)]
+        hs_val = [sbuf("hs_val%d" % b, [P, 2, NODE_HALF, J], BF16) for b in range(2)]
+        hs_cod = [sbuf("hs_cod%d" % b, [P, 2, NODE_HALF], U32) for b in range(2)]
+        hs_csc = [sbuf("hs_csc%d" % b, [P, 2, NODE_HALF], U8) for b in range(2)]
+        hh_part = [sbuf("hh_part%d" % b, [P, 4, 2], F32) for b in range(2)]
+        hh_sum = [sbuf("hh_sum%d" % b, [P, 4], F32) for b in range(2)]
+        hh_inv = [sbuf("hh_inv%d" % b, [P, 4], F32) for b in range(2)]
         squares = [sbuf("squares%d" % v, [P, BANK], BF16) for v in range(2)]
         c_sq = [sbuf("c_sq%d" % i, [P, Q], F32) for i in range(8)]
         res = [sbuf("res%d" % i, [P, Q], F32) for i in range(8)]
@@ -100,13 +102,35 @@ def tile_stochasticconfigurationcandidatescores_w4_kernel(
 
         x_place = [(i, n) for i, count in enumerate(X_LOADS) for n in range(count)]
 
-        def x_widen(copy, r, k0, k1):
+        def x_widen(copy, i, k0, k1):
+            copy(
+                x_wide[i][:].rearrange("p n k -> p (n k)")[:, k0:k1],
+                x_raw[i][:].rearrange("p n k -> p (n k)")[:, k0:k1].bitcast(FP8),
+            )
+
+        def scale_spread(v):
+            bank = new_bank(("s", v), "spread")
+            for j in range(J):
+                nc.tensor.transpose(
+                    bank[:, j * P : (j + 1) * P], x_scl[:, v, j : j + 1].to_broadcast([P, P]), ident[:]
+                )
+
+        def scale_copy_out(copy, v):
+            copy(
+                scale_b[:, v * BANK : (v + 1) * BANK].rearrange("p (k j) -> p k j", j=J),
+                banks["s", v][:].rearrange("p (j k) -> p k j", j=J),
+            )
+
+        def x_apply_scale(r, k0, k1):
             i, n = x_place[r]
-            copy(x_wide[r][:, k0:k1], x_raw[i][:, n, k0:k1].bitcast(FP8))
+            nc.vector.tensor_tensor(
+                out=x_wide[i][:, n, k0:k1], in0=x_raw[i][:, n, k0:k1].bitcast(FP8), in1=scale_b[:, k0:k1], op=ALU.mult
+            )
 
         def x_turn(r):
             bank = new_bank(("x", r), "turn in")
-            words = x_wide[r][:].bitcast(F32)
+            i, n = x_place[r]
+            words = x_wide[i][:, n, :].bitcast(F32)
             for v in range(2):
                 for u in range(2):
                     at = (2 * u + v) * P
@@ -122,12 +146,29 @@ def tile_stochasticconfigurationcandidatescores_w4_kernel(
                 op=ALU.mult,
             )
 
+        def x_copy_out(r):
+            nc.scalar.copy(
+                x_val[r // 2][:, r % 2].bitcast(F32),
+                banks["x", r][:].rearrange("p (u v r) -> p v r u", u=2, v=2),
+            )
+
+        def x_in(r):
+            x_turn(r)
+            x_copy_out(r)
+
         def x_quantise(r):
             i, n = r // 2, r % 2
             nc.vector.quantize_mx(
                 out=x_cod[i][:, n].rearrange("p v r -> p (v r)").bitcast(FP8X4),
                 scales=x_csc[i][:, n].rearrange("p v r -> p (v r)"),
                 in_=x_val[i][:, n].rearrange("p v r j -> p (v r j)"),
+            )
+
+        def x_quantise_pair(i):
+            nc.vector.quantize_mx(
+                out=x_cod[i][:].rearrange("p n v r -> p (n v r)").bitcast(FP8X4),
+                scales=x_csc[i][:].rearrange("p n v r -> p (n v r)"),
+                in_=x_val[i][:].rearrange("p n v r j -> p (n v r j)"),
             )
 
         def preact(r, b):
@@ -192,9 +233,9 @@ def tile_stochasticconfigurationcandidatescores_w4_kernel(
         def residual(v, qb):
             cols = slice(qb * P, (qb + 1) * P)
             nc.vector.tensor_tensor(
-                out=e_val[v][:, cols, :].rearrange("p (c i) j -> p c j i", i=4),
-                in0=tgt[v][:, :, cols].rearrange("p j (c i) -> p c j i", i=4),
-                in1=banks["gb", v, qb][:].rearrange("p (j c i) -> p c j i", j=J, i=4),
+                out=e_val[v][:, cols, :].rearrange("p (c i) j -> p c j i", i=RUN),
+                in0=tgt[v][:, :, cols].rearrange("p j (c i) -> p c j i", i=RUN),
+                in1=banks["gb", v, qb][:].rearrange("p (j c i) -> p c j i", j=J, i=RUN),
                 op=ALU.subtract,
             )
 
@@ -214,50 +255,42 @@ def tile_stochasticconfigurationcandidatescores_w4_kernel(
                 out=squares[i % 2][:],
                 in_=banks["h", i, v][:],
                 func=ACT.Square,
-                accum_out=hh_part[i // 2][:, i % 2, v : v + 1],
+                accum_out=hh_part[i // 4][:, i % 4, v : v + 1],
             )
 
         def node_energy(i, v):
             h_turn(i, v)
             energy(i, v)
 
-        def energy_sum(n):
-            nc.vector.tensor_tensor(out=hh_sum[n][:], in0=hh_part[n][:, :, 0], in1=hh_part[n][:, :, 1], op=ALU.add)
+        def energy_sum(b):
+            nc.vector.tensor_tensor(out=hh_sum[b][:], in0=hh_part[b][:, :, 0], in1=hh_part[b][:, :, 1], op=ALU.add)
 
-        def energy_inverse(n):
-            nc.vector.reciprocal(out=hh_inv[n][:], in_=hh_sum[n][:])
+        def energy_inverse(b):
+            nc.vector.reciprocal(out=hh_inv[b][:], in_=hh_sum[b][:])
 
-        def apply_gain(n, v):
-            at = n % 2 * NODE_QUARTER
+        def apply_gain(b, v, n0, n1):
             nc.vector.tensor_tensor(
-                out=hs_val[n][:, v].rearrange("p (c i) j -> p c j i", i=4),
-                in0=h[n // 2, v][:, :, at : at + NODE_QUARTER].rearrange("p j (c i) -> p c j i", i=4),
-                in1=gain_q[:, v, :].unsqueeze(1).unsqueeze(3).to_broadcast([P, NODE_QUARTER // 4, J, 4]),
+                out=hs_val[b][:, v, n0:n1].rearrange("p (c i) j -> p c j i", i=RUN),
+                in0=h[b, v][:, :, n0:n1].rearrange("p j (c i) -> p c j i", i=RUN),
+                in1=gain_q[:, v, :].unsqueeze(1).unsqueeze(3).to_broadcast([P, (n1 - n0) // RUN, J, RUN]),
                 op=ALU.mult,
             )
 
-        def hs_quantise(n):
+        def hs_quantise(b, n0, n1):
             nc.vector.quantize_mx(
-                out=hs_cod[n][:].rearrange("p v f -> p (v f)").bitcast(FP8X4),
-                scales=hs_csc[n][:].rearrange("p v f -> p (v f)"),
-                in_=hs_val[n][:].rearrange("p v f j -> p (v f j)"),
-            )
-
-        def hs_quantise_half(n, v):
-            nc.vector.quantize_mx(
-                out=hs_cod[n][:, v].bitcast(FP8X4),
-                scales=hs_csc[n][:, v],
-                in_=hs_val[n][:, v].rearrange("p f j -> p (f j)"),
+                out=hs_cod[b][:].rearrange("p v f -> p (v f)")[:, n0:n1].bitcast(FP8X4),
+                scales=hs_csc[b][:].rearrange("p v f -> p (v f)")[:, n0:n1],
+                in_=hs_val[b][:].rearrange("p v f j -> p (v f j)")[:, J * n0 : J * n1],
             )
 
         def correlate(i):
             bank = new_bank(("c", i), "corr")
-            cols = slice(i % 2 * P, (i % 2 + 1) * P)
+            cols = slice(i % 4 * P, (i % 4 + 1) * P)
             for v in range(2):
                 nc.tensor.matmul_mx(
                     out=bank[:],
-                    lhsT=hs_cod[i // 2][:, v, cols].bitcast(FP8X4),
-                    lhsT_scale=hs_csc[i // 2][:, v, cols],
+                    lhsT=hs_cod[i // 4][:, v, cols].bitcast(FP8X4),
+                    lhsT_scale=hs_csc[i // 4][:, v, cols],
                     rhs=e_cod[v][:].bitcast(FP8X4),
                     rhs_scale=e_csc[v][:],
                     start=(v == 0),
@@ -278,7 +311,7 @@ def tile_stochasticconfigurationcandidatescores_w4_kernel(
                 nc.vector.scalar_tensor_tensor(
                     out=res[i][:, cols],
                     in0=c_sq[i][:, cols],
-                    scalar=hh_inv[i // 2][:, i % 2 : i % 2 + 1],
+                    scalar=hh_inv[i // 4][:, i % 4 : i % 4 + 1],
                     in1=tau_b[:, cols],
                     op0=ALU.mult,
                     op1=ALU.subtract,
@@ -321,20 +354,20 @@ def tile_stochasticconfigurationcandidatescores_w4_kernel(
                 )
 
         load_x(0)
-        load_x(1)
         load(out=x_scl[:], in_=x_scale.rearrange("o (v p j) -> p (o v) j", p=P, j=J))
-        load_x(2)
+        load_x(1)
         load(out=hid[0][:], in_=hid_rows[0])
-        load_x(3)
+        load_x(2)
         load_w(0)
         load_scales(w_scl, w_scales.rearrange("v r n -> r v n"))
-        load_x(4)
+        load_x(3)
+        load_w(1)
         load(out=hid[1][:], in_=hid_rows[1])
+        load_x(4)
         load(out=b_wrd[:].bitcast(I32), in_=beta_words[0].bitcast(I32))
         load_scales(b_scl, beta_scales[0])
-        load_w(1)
-        load(out=tgt[0][:], in_=tgt_rows[0])
         load(out=gain_q[:], in_=gain.rearrange("(v p j) -> p v j", p=P, j=J))
+        load(out=tgt[0][:], in_=tgt_rows[0])
         load(out=tgt[1][:], in_=tgt_rows[1])
         load(out=tau_b[:], in_=tau.partition_broadcast(P))
 
@@ -342,93 +375,114 @@ def tile_stochasticconfigurationcandidatescores_w4_kernel(
             x_widen(nc.vector.tensor_copy, 0, 0, BANK)
             x_widen(nc.vector.tensor_copy, 0, BANK, D)
             x_widen(nc.vector.tensor_copy, 1, 0, D)
-            x_widen(nc.scalar.copy, 2, 0, D)
-            x_widen(nc.scalar.copy, 3, 0, D)
+            scale_spread(0)
+            scale_copy_out(nc.scalar.copy, 0)
             x_turn(0)
+            scale_spread(1)
+            scale_copy_out(nc.scalar.copy, 1)
             x_turn(1)
-            warm_up(2)
-            x_turn(2)
             x_scale_out(0)
+            warm_up(2)
             g_in(0)
-            x_turn(3)
-            x_widen(nc.scalar.copy, 4, 0, D)
-            for r in range(1, ROW_TILES + 1):
-                if r < ROW_TILES:
-                    x_scale_out(r)
-                if r == ROW_TILES:
-                    g_quantise(0)
-                x_quantise(r - 1)
-                if r + 4 < ROW_TILES:
-                    x_widen(nc.scalar.copy, r + 4, 0, D)
-                if r == ROW_TILES:
-                    beta_product(0, 0)
-                    beta_product(0, 1)
-                nodes(r - 1, 0)
-                if r + 3 < ROW_TILES:
-                    x_turn(r + 3)
-                elif r < ROW_TILES:
-                    g_in(r - 4)
-            apply_gain(0, 0)
+            g_in(1)
+            x_scale_out(1)
+            x_quantise(0)
+            nodes(0, 0)
+            x_apply_scale(2, 0, D)
+            x_quantise(1)
+            x_in(2)
+            nodes(1, 0)
+            x_apply_scale(3, 0, D)
+            nodes(0, 1)
+            x_in(3)
+            x_apply_scale(4, 0, D)
+            nodes(1, 1)
+            x_in(4)
+            g_in(2)
+            x_apply_scale(5, 0, D)
+            x_in(5)
+            x_quantise_pair(1)
+            nodes(2, 0)
+            nodes(3, 0)
+            x_apply_scale(6, 0, D)
+            x_in(6)
+            g_in(3)
+            x_apply_scale(7, 0, D)
+            nodes(2, 1)
+            x_in(7)
+            x_quantise_pair(2)
+            g_quantise(0)
+            nodes(4, 0)
+            nodes(5, 0)
+            beta_product(0, 0)
+            beta_product(0, 1)
             beta_product(0, 2)
-            for k in range(4):
-                v, qb = divmod(2 * k, 4)
-                residual(v, qb)
-                nodes(2 * k, 1)
-                if k == 0:
-                    g_quantise(1)
-                if 2 * k + 3 < 8:
-                    beta_product(*divmod(2 * k + 3, 4))
-                residual(v, qb + 1)
-                nodes(2 * k + 1, 1)
-                if 2 * k + 4 < 8:
-                    beta_product(*divmod(2 * k + 4, 4))
-                i, u = ((0, 0), (0, 1), (2, 0), (2, 1))[k]
-                node_energy(i, u)
-                node_energy(i + 1, u)
-                if k < 3:
-                    apply_gain(*divmod(k + 1, 2))
-                if k == 1:
-                    e_quantise(0)
-                if k == 2:
-                    hs_quantise(0)
-                    energy_sum(0)
-            apply_gain(2, 0)
-            e_quantise(1)
-            correlation_squared(0)
+            node_energy(0, 0)
+            node_energy(1, 0)
+            apply_gain(0, 0, 0, NODE_HALF)
+            x_quantise_pair(3)
+            g_quantise(1)
+            nodes(6, 0)
+            nodes(7, 0)
+            residual(0, 0)
+            beta_product(0, 3)
+            residual(0, 1)
+            beta_product(1, 0)
+            node_energy(2, 0)
+            node_energy(3, 0)
+            nodes(3, 1)
+            residual(0, 2)
+            beta_product(1, 1)
+            residual(0, 3)
+            beta_product(1, 2)
+            node_energy(0, 1)
+            node_energy(1, 1)
+            nodes(4, 1)
+            residual(1, 0)
+            beta_product(1, 3)
+            node_energy(2, 1)
+            node_energy(3, 1)
+            nodes(5, 1)
+            nodes(6, 1)
+            apply_gain(0, 1, 0, NODE_HALF)
+            residual(1, 1)
+            e_quantise(0)
+            residual(1, 2)
+            residual(1, 3)
             node_energy(4, 0)
             node_energy(5, 0)
-            correlation_squared(1)
-            energy_inverse(0)
-            hs_quantise(1)
-            energy_sum(1)
-            node_energy(4, 1)
-            node_energy(5, 1)
-            correlation_squared(2)
-            apply_gain(2, 1)
-            energy_inverse(1)
+            nodes(7, 1)
+            hs_quantise(0, 0, 2 * NODE_HALF)
+            e_quantise(1)
             node_energy(6, 0)
             node_energy(7, 0)
-            correlation_squared(3)
-            apply_gain(3, 0)
-            hs_quantise(2)
-            score(0)
+            correlation_squared(0)
+            apply_gain(1, 0, 0, NODE_HALF)
+            energy_sum(0)
+            node_energy(4, 1)
+            node_energy(5, 1)
+            correlation_squared(1)
+            apply_gain(1, 1, 0, 256)
+            energy_inverse(0)
+            hs_quantise(1, 0, NODE_HALF)
             node_energy(6, 1)
             node_energy(7, 1)
+            correlation_squared(2)
+            correlation_squared(3)
+            score(0)
+            hs_quantise(1, NODE_HALF, NODE_HALF + 256)
+            apply_gain(1, 1, 256, NODE_HALF)
             correlation_squared(4)
-            apply_gain(3, 1)
-            hs_quantise_half(3, 0)
-            energy_sum(2)
-            hs_quantise_half(3, 1)
-            energy_inverse(2)
             correlation_squared(5)
+            score(1)
+            hs_quantise(1, NODE_HALF + 256, 2 * NODE_HALF)
             correlation_squared(6)
             correlation_squared(7)
-            score(1)
+            energy_sum(1)
             score(2)
+            energy_inverse(1)
             score(3)
-            energy_sum(3)
             score(4)
-            energy_inverse(3)
             score(5)
             score(6)
             score(7, parts=LAST_BLOCK_PARTS)

@@ -26,18 +26,9 @@ RUN = 4
 FP4_BYTES = 2
 
 X_LOADS = (1, 1, 2, 2, 2)
+X_GROUPS = (1, 1, 2, 4)
 WARM_UP_MATMULS = 3
 LAST_BLOCK_PARTS = 2
-
-BANK_RINGS = {
-    "warm": (7,),
-    "spread": (4, 5),
-    "turn in": (0, 1, 2, 3),
-    "preact": (4, 5),
-    "beta": (6, 7, 3),
-    "turn h": (0, 1, 2),
-    "corr": (6, 7, 3, 4),
-}
 
 
 def tile_stochasticconfigurationcandidatescores_w4_kernel(
@@ -64,12 +55,12 @@ def tile_stochasticconfigurationcandidatescores_w4_kernel(
 
         scale_b = sbuf("scale_b", [P, D], F32)
         x_wide = [sbuf("x_wide%d" % i, [P, n, D], BF16) for i, n in enumerate(X_LOADS)]
-        x_val = [sbuf("x_val%d" % i, [P, 2, 2, P, J], BF16) for i in range(4)]
-        x_cod = [sbuf("x_cod%d" % i, [P, 2, 2, P], U32) for i in range(4)]
-        x_csc = [sbuf("x_csc%d" % i, [P, 2, 2, P], U8) for i in range(4)]
-        g_val = [sbuf("g_val%d" % v, [P, J, P, J], BF16) for v in range(2)]
-        g_cod = [sbuf("g_cod%d" % v, [P, J, P], U32) for v in range(2)]
-        g_csc = [sbuf("g_csc%d" % v, [P, J, P], U8) for v in range(2)]
+        x_val = [sbuf("x_val%d" % i, [P, n, 2, P, J], BF16) for i, n in enumerate(X_GROUPS)]
+        x_cod = [sbuf("x_cod%d" % i, [P, n, 2, P], U32) for i, n in enumerate(X_GROUPS)]
+        x_csc = [sbuf("x_csc%d" % i, [P, n, 2, P], U8) for i, n in enumerate(X_GROUPS)]
+        g_val = sbuf("g_val", [P, ROW_TILES, P, J], BF16)
+        g_cod = sbuf("g_cod", [P, ROW_TILES, P], U32)
+        g_csc = sbuf("g_csc", [P, ROW_TILES, P], U8)
         e_val = [sbuf("e_val%d" % v, [P, Q, J], BF16) for v in range(2)]
         e_cod = [sbuf("e_cod%d" % v, [P, Q], U32) for v in range(2)]
         e_csc = [sbuf("e_csc%d" % v, [P, Q], U8) for v in range(2)]
@@ -91,16 +82,13 @@ def tile_stochasticconfigurationcandidatescores_w4_kernel(
 
         banks = {}
 
-        taken = {kind: [] for kind in BANK_RINGS}
-
-        def new_bank(key, kind):
-            ring = BANK_RINGS[kind]
-            number = ring[len(taken[kind]) % len(ring)]
-            taken[kind].append(key)
+        def new_bank(key, number):
             banks[key] = psum.tile([P, BANK], F32, name="bank%d" % number, tag="bank%d" % number, bufs=1)
             return banks[key]
 
         x_place = [(i, n) for i, count in enumerate(X_LOADS) for n in range(count)]
+
+        x_group = [(i, n) for i, count in enumerate(X_GROUPS) for n in range(count)]
 
         def x_widen(copy, i, k0, k1):
             copy(
@@ -108,8 +96,8 @@ def tile_stochasticconfigurationcandidatescores_w4_kernel(
                 x_raw[i][:].rearrange("p n k -> p (n k)")[:, k0:k1].bitcast(FP8),
             )
 
-        def scale_spread(v):
-            bank = new_bank(("s", v), "spread")
+        def scale_spread(v, number):
+            bank = new_bank(("s", v), number)
             for j in range(J):
                 nc.tensor.transpose(
                     bank[:, j * P : (j + 1) * P], x_scl[:, v, j : j + 1].to_broadcast([P, P]), ident[:]
@@ -127,8 +115,8 @@ def tile_stochasticconfigurationcandidatescores_w4_kernel(
                 out=x_wide[i][:, n, k0:k1], in0=x_raw[i][:, n, k0:k1].bitcast(FP8), in1=scale_b[:, k0:k1], op=ALU.mult
             )
 
-        def x_turn(r):
-            bank = new_bank(("x", r), "turn in")
+        def x_turn(r, number):
+            bank = new_bank(("x", r), number)
             i, n = x_place[r]
             words = x_wide[i][:, n, :].bitcast(F32)
             for v in range(2):
@@ -140,7 +128,7 @@ def tile_stochasticconfigurationcandidatescores_w4_kernel(
 
         def x_scale_out(r):
             nc.vector.tensor_tensor(
-                out=x_val[r // 2][:, r % 2].rearrange("p v r (u e) -> p v r u e", u=2),
+                out=x_val[x_group[r][0]][:, x_group[r][1]].rearrange("p v r (u e) -> p v r u e", u=2),
                 in0=banks["x", r][:].bitcast(BF16).rearrange("p (u v r e) -> p v r u e", u=2, v=2, e=2),
                 in1=x_scl[:].rearrange("p v (u e) -> p v u e", u=2).unsqueeze(2).to_broadcast([P, 2, P, 2, 2]),
                 op=ALU.mult,
@@ -148,36 +136,29 @@ def tile_stochasticconfigurationcandidatescores_w4_kernel(
 
         def x_copy_out(r):
             nc.scalar.copy(
-                x_val[r // 2][:, r % 2].bitcast(F32),
+                x_val[x_group[r][0]][:, x_group[r][1]].bitcast(F32),
                 banks["x", r][:].rearrange("p (u v r) -> p v r u", u=2, v=2),
             )
 
-        def x_in(r):
-            x_turn(r)
+        def x_in(r, number):
+            x_turn(r, number)
             x_copy_out(r)
 
-        def x_quantise(r):
-            i, n = r // 2, r % 2
-            nc.vector.quantize_mx(
-                out=x_cod[i][:, n].rearrange("p v r -> p (v r)").bitcast(FP8X4),
-                scales=x_csc[i][:, n].rearrange("p v r -> p (v r)"),
-                in_=x_val[i][:, n].rearrange("p v r j -> p (v r j)"),
-            )
-
-        def x_quantise_pair(i):
+        def x_quantise(i):
             nc.vector.quantize_mx(
                 out=x_cod[i][:].rearrange("p n v r -> p (n v r)").bitcast(FP8X4),
                 scales=x_csc[i][:].rearrange("p n v r -> p (n v r)"),
                 in_=x_val[i][:].rearrange("p n v r j -> p (n v r j)"),
             )
 
-        def preact(r, b):
-            bank = new_bank(("xw", r, b), "preact")
+        def preact(r, b, number):
+            bank = new_bank(("xw", r, b), number)
+            i, n = x_group[r]
             for v in range(2):
                 nc.tensor.matmul_mx(
                     out=bank[:],
-                    lhsT=x_cod[r // 2][:, r % 2, v, :].bitcast(FP8X4),
-                    lhsT_scale=x_csc[r // 2][:, r % 2, v, :],
+                    lhsT=x_cod[i][:, n, v, :].bitcast(FP8X4),
+                    lhsT_scale=x_csc[i][:, n, v, :],
                     rhs=w_wrd[b][:, v, :].bitcast(FP4X4),
                     rhs_scale=w_scl[:, v, b * NODE_HALF : (b + 1) * NODE_HALF],
                     start=(v == 0),
@@ -187,12 +168,12 @@ def tile_stochasticconfigurationcandidatescores_w4_kernel(
         def tanh(r, b):
             nc.scalar.activation(out=h[b, r // J][:, r % J, :], in_=banks["xw", r, b][:], func=ACT.Tanh)
 
-        def nodes(r, b):
-            preact(r, b)
+        def nodes(r, b, number):
+            preact(r, b, number)
             tanh(r, b)
 
-        def g_turn(i):
-            bank = new_bank(("g", i), "turn in")
+        def g_turn(i, number):
+            bank = new_bank(("g", i), number)
             for n in range(2):
                 words = hid[i // 2][:, 2 * (i % 2) + n, :].bitcast(F32)
                 for u in range(2):
@@ -200,30 +181,29 @@ def tile_stochasticconfigurationcandidatescores_w4_kernel(
                     nc.tensor.transpose(bank[:, at : at + P], words[:, u:256:2], ident[:])
 
         def g_copy_out(i):
-            n = 2 * (i % 2)
             nc.scalar.copy(
-                g_val[i // 2][:, n : n + 2].bitcast(F32),
+                g_val[:, 2 * i : 2 * i + 2].bitcast(F32),
                 banks["g", i][:].rearrange("p (n u r) -> p n r u", n=2, u=2),
             )
 
-        def g_in(i):
-            g_turn(i)
+        def g_in(i, number):
+            g_turn(i, number)
             g_copy_out(i)
 
-        def g_quantise(v):
+        def g_quantise():
             nc.vector.quantize_mx(
-                out=g_cod[v][:].rearrange("p n r -> p (n r)").bitcast(FP8X4),
-                scales=g_csc[v][:].rearrange("p n r -> p (n r)"),
-                in_=g_val[v][:].rearrange("p n r j -> p (n r j)"),
+                out=g_cod[:].rearrange("p n r -> p (n r)").bitcast(FP8X4),
+                scales=g_csc[:].rearrange("p n r -> p (n r)"),
+                in_=g_val[:].rearrange("p n r j -> p (n r j)"),
             )
 
-        def beta_product(v, qb):
-            bank = new_bank(("gb", v, qb), "beta")
+        def beta_product(v, qb, number):
+            bank = new_bank(("gb", v, qb), number)
             for j in range(J):
                 nc.tensor.matmul_mx(
                     out=bank[:, j * P : (j + 1) * P],
-                    lhsT=g_cod[v][:, j, :].bitcast(FP8X4),
-                    lhsT_scale=g_csc[v][:, j, :],
+                    lhsT=g_cod[:, J * v + j, :].bitcast(FP8X4),
+                    lhsT_scale=g_csc[:, J * v + j, :],
                     rhs=b_wrd[:, qb * P * FP4_BYTES : (qb + 1) * P * FP4_BYTES].bitcast(FP4X4),
                     rhs_scale=b_scl[:, qb * P : (qb + 1) * P],
                     start=True,
@@ -244,8 +224,8 @@ def tile_stochasticconfigurationcandidatescores_w4_kernel(
                 out=e_cod[v][:].bitcast(FP8X4), scales=e_csc[v][:], in_=e_val[v][:].rearrange("p q j -> p (q j)")
             )
 
-        def h_turn(i, v):
-            bank = new_bank(("h", i, v), "turn h")
+        def h_turn(i, v, number):
+            bank = new_bank(("h", i, v), number)
             at = i % 4 * P
             for j in range(J):
                 nc.tensor.transpose(bank[:, j * P : (j + 1) * P], h[i // 4, v][:, j, at : at + P], ident[:])
@@ -258,8 +238,8 @@ def tile_stochasticconfigurationcandidatescores_w4_kernel(
                 accum_out=hh_part[i // 4][:, i % 4, v : v + 1],
             )
 
-        def node_energy(i, v):
-            h_turn(i, v)
+        def node_energy(i, v, number):
+            h_turn(i, v, number)
             energy(i, v)
 
         def energy_sum(b):
@@ -283,8 +263,8 @@ def tile_stochasticconfigurationcandidatescores_w4_kernel(
                 in_=hs_val[b][:].rearrange("p v f j -> p (v f j)")[:, J * n0 : J * n1],
             )
 
-        def correlate(i):
-            bank = new_bank(("c", i), "corr")
+        def correlate(i, number):
+            bank = new_bank(("c", i), number)
             cols = slice(i % 4 * P, (i % 4 + 1) * P)
             for v in range(2):
                 nc.tensor.matmul_mx(
@@ -300,8 +280,8 @@ def tile_stochasticconfigurationcandidatescores_w4_kernel(
         def square(i):
             nc.scalar.activation(out=c_sq[i][:], in_=banks["c", i][:], func=ACT.Square)
 
-        def correlation_squared(i):
-            correlate(i)
+        def correlation_squared(i, number):
+            correlate(i, number)
             square(i)
 
         def score(i, parts=1):
@@ -324,7 +304,7 @@ def tile_stochasticconfigurationcandidatescores_w4_kernel(
         nc.vector.memset(zeros[:], 0.0)
         nc.vector.memset(w_scl[:].rearrange("p v n -> p (v n)").bitcast(I32), 0)
         nc.vector.memset(b_scl[:].bitcast(I32), 0)
-        warm = new_bank("warm", "warm")
+        warm = new_bank("warm", 7)
 
         def warm_up(count):
             for n in range(count):
@@ -356,13 +336,13 @@ def tile_stochasticconfigurationcandidatescores_w4_kernel(
         load_x(0)
         load(out=x_scl[:], in_=x_scale.rearrange("o (v p j) -> p (o v) j", p=P, j=J))
         load_x(1)
-        load(out=hid[0][:], in_=hid_rows[0])
         load_x(2)
+        load(out=hid[0][:], in_=hid_rows[0])
         load_w(0)
         load_scales(w_scl, w_scales.rearrange("v r n -> r v n"))
-        load_x(3)
         load_w(1)
         load(out=hid[1][:], in_=hid_rows[1])
+        load_x(3)
         load_x(4)
         load(out=b_wrd[:].bitcast(I32), in_=beta_words[0].bitcast(I32))
         load_scales(b_scl, beta_scales[0])
@@ -375,109 +355,108 @@ def tile_stochasticconfigurationcandidatescores_w4_kernel(
             x_widen(nc.vector.tensor_copy, 0, 0, BANK)
             x_widen(nc.vector.tensor_copy, 0, BANK, D)
             x_widen(nc.vector.tensor_copy, 1, 0, D)
-            scale_spread(0)
+            x_widen(nc.scalar.copy, 2, 0, D)
+            x_widen(nc.scalar.copy, 2, D, 2 * D)
+            scale_spread(0, 4)
+            x_turn(0, 0)
+            scale_spread(1, 5)
             scale_copy_out(nc.scalar.copy, 0)
-            x_turn(0)
-            scale_spread(1)
             scale_copy_out(nc.scalar.copy, 1)
-            x_turn(1)
+            x_turn(1, 1)
+            x_turn(2, 2)
             x_scale_out(0)
-            warm_up(2)
-            g_in(0)
-            g_in(1)
+            g_in(0, 6)
+            x_turn(3, 3)
+            g_in(1, 7)
             x_scale_out(1)
             x_quantise(0)
-            nodes(0, 0)
-            x_apply_scale(2, 0, D)
+            nodes(0, 0, 4)
+            nodes(0, 1, 5)
+            x_scale_out(2)
             x_quantise(1)
-            x_in(2)
-            nodes(1, 0)
-            x_apply_scale(3, 0, D)
-            nodes(0, 1)
-            x_in(3)
+            nodes(1, 0, 6)
+            nodes(1, 1, 7)
+            g_in(2, 0)
+            g_in(3, 1)
+            x_scale_out(3)
             x_apply_scale(4, 0, D)
-            nodes(1, 1)
-            x_in(4)
-            g_in(2)
+            x_in(4, 2)
+            x_quantise(2)
+            nodes(2, 0, 4)
+            nodes(3, 0, 5)
+            nodes(2, 1, 6)
             x_apply_scale(5, 0, D)
-            x_in(5)
-            x_quantise_pair(1)
-            nodes(2, 0)
-            nodes(3, 0)
+            x_in(5, 3)
             x_apply_scale(6, 0, D)
-            x_in(6)
-            g_in(3)
+            x_in(6, 0)
+            nodes(3, 1, 7)
             x_apply_scale(7, 0, D)
-            nodes(2, 1)
-            x_in(7)
-            x_quantise_pair(2)
-            g_quantise(0)
-            nodes(4, 0)
-            nodes(5, 0)
-            beta_product(0, 0)
-            beta_product(0, 1)
-            beta_product(0, 2)
-            node_energy(0, 0)
-            node_energy(1, 0)
+            x_in(7, 1)
+            node_energy(0, 0, 2)
+            node_energy(1, 0, 4)
+            g_quantise()
+            beta_product(0, 0, 6)
+            beta_product(0, 1, 5)
+            beta_product(0, 2, 7)
+            node_energy(2, 0, 3)
+            node_energy(3, 0, 0)
+            node_energy(4, 0, 1)
+            node_energy(5, 0, 2)
             apply_gain(0, 0, 0, NODE_HALF)
-            x_quantise_pair(3)
-            g_quantise(1)
-            nodes(6, 0)
-            nodes(7, 0)
+            x_quantise(3)
+            nodes(4, 0, 4)
+            nodes(5, 0, 3)
             residual(0, 0)
-            beta_product(0, 3)
+            beta_product(0, 3, 6)
+            nodes(6, 0, 0)
             residual(0, 1)
-            beta_product(1, 0)
-            node_energy(2, 0)
-            node_energy(3, 0)
-            nodes(3, 1)
+            beta_product(1, 0, 5)
+            nodes(7, 0, 1)
             residual(0, 2)
-            beta_product(1, 1)
+            beta_product(1, 1, 7)
+            node_energy(6, 0, 2)
+            node_energy(7, 0, 4)
+            apply_gain(1, 0, 0, NODE_HALF)
+            nodes(4, 1, 3)
+            nodes(5, 1, 0)
             residual(0, 3)
-            beta_product(1, 2)
-            node_energy(0, 1)
-            node_energy(1, 1)
-            nodes(4, 1)
+            beta_product(1, 2, 6)
             residual(1, 0)
-            beta_product(1, 3)
-            node_energy(2, 1)
-            node_energy(3, 1)
-            nodes(5, 1)
-            nodes(6, 1)
-            apply_gain(0, 1, 0, NODE_HALF)
+            beta_product(1, 3, 5)
+            node_energy(0, 1, 1)
+            node_energy(1, 1, 2)
+            node_energy(2, 1, 4)
+            nodes(6, 1, 3)
+            nodes(7, 1, 0)
+            node_energy(3, 1, 1)
             residual(1, 1)
             e_quantise(0)
+            apply_gain(0, 1, 0, NODE_HALF)
             residual(1, 2)
             residual(1, 3)
-            node_energy(4, 0)
-            node_energy(5, 0)
-            nodes(7, 1)
             hs_quantise(0, 0, 2 * NODE_HALF)
             e_quantise(1)
-            node_energy(6, 0)
-            node_energy(7, 0)
-            correlation_squared(0)
-            apply_gain(1, 0, 0, NODE_HALF)
+            node_energy(4, 1, 2)
+            node_energy(5, 1, 4)
+            correlation_squared(0, 7)
+            correlation_squared(1, 6)
+            node_energy(6, 1, 3)
+            node_energy(7, 1, 0)
+            correlation_squared(2, 5)
+            correlation_squared(3, 1)
+            hs_quantise(1, 0, NODE_HALF)
             energy_sum(0)
-            node_energy(4, 1)
-            node_energy(5, 1)
-            correlation_squared(1)
             apply_gain(1, 1, 0, 256)
             energy_inverse(0)
-            hs_quantise(1, 0, NODE_HALF)
-            node_energy(6, 1)
-            node_energy(7, 1)
-            correlation_squared(2)
-            correlation_squared(3)
-            score(0)
-            hs_quantise(1, NODE_HALF, NODE_HALF + 256)
             apply_gain(1, 1, 256, NODE_HALF)
-            correlation_squared(4)
-            correlation_squared(5)
-            score(1)
+            hs_quantise(1, NODE_HALF, NODE_HALF + 256)
+            correlation_squared(4, 2)
+            correlation_squared(5, 3)
+            score(0)
             hs_quantise(1, NODE_HALF + 256, 2 * NODE_HALF)
-            correlation_squared(6)
-            correlation_squared(7)
+            correlation_squared(6, 4)
+            correlation_squared(7, 0)
+            score(1)
             energy_sum(1)
             score(2)
             energy_inverse(1)

@@ -19,6 +19,7 @@ FLOPS = 2 * N * D * F + 2 * N * L * Q + 2 * N * F * Q
 
 P = 128
 J = 4
+PSUM_BANKS = 8
 BANK = 512
 ROW_TILES = N // P
 NODE_HALF = F // 2
@@ -26,8 +27,9 @@ RUN = 4
 FP4_BYTES = 2
 
 X_LOADS = (1, 1, 2, 2, 2)
-X_GROUPS = (1, 1, 2, 4)
+X_GROUPS = (1, 1, 2, 2, 2)
 WARM_UP_MATMULS = 3
+GPSIMD_NODES = 128
 LAST_BLOCK_PARTS = 2
 
 
@@ -51,6 +53,7 @@ def tile_stochasticconfigurationcandidatescores_w4_kernel(
         hid = [sbuf("hid%d" % v, [P, J, L], BF16) for v in range(2)]
         tgt = [sbuf("tgt%d" % v, [P, J, Q], BF16) for v in range(2)]
         gain_q = sbuf("gain_q", [P, 2, J], BF16)
+        gain_f = [sbuf("gain_f%d" % v, [P, J], F32) for v in range(2)]
         tau_b = sbuf("tau_b", [P, Q], BF16)
 
         scale_b = sbuf("scale_b", [P, D], F32)
@@ -82,9 +85,18 @@ def tile_stochasticconfigurationcandidatescores_w4_kernel(
 
         banks = {}
 
-        def new_bank(key, number):
-            banks[key] = psum.tile([P, BANK], F32, name="bank%d" % number, tag="bank%d" % number, bufs=1)
-            return banks[key]
+        free = list(range(PSUM_BANKS))
+
+        def new_bank(key):
+            number = free.pop(0)
+            tile = psum.tile([P, BANK], F32, name="bank%d" % number, tag="bank%d" % number, bufs=1)
+            banks[key] = (number, tile)
+            return tile
+
+        def read_bank(key):
+            number, tile = banks.pop(key)
+            free.append(number)
+            return tile
 
         x_place = [(i, n) for i, count in enumerate(X_LOADS) for n in range(count)]
 
@@ -96,8 +108,8 @@ def tile_stochasticconfigurationcandidatescores_w4_kernel(
                 x_raw[i][:].rearrange("p n k -> p (n k)")[:, k0:k1].bitcast(FP8),
             )
 
-        def scale_spread(v, number):
-            bank = new_bank(("s", v), number)
+        def scale_spread(v):
+            bank = new_bank(("s", v))
             for j in range(J):
                 nc.tensor.transpose(
                     bank[:, j * P : (j + 1) * P], x_scl[:, v, j : j + 1].to_broadcast([P, P]), ident[:]
@@ -106,7 +118,7 @@ def tile_stochasticconfigurationcandidatescores_w4_kernel(
         def scale_copy_out(copy, v):
             copy(
                 scale_b[:, v * BANK : (v + 1) * BANK].rearrange("p (k j) -> p k j", j=J),
-                banks["s", v][:].rearrange("p (j k) -> p k j", j=J),
+                read_bank(("s", v))[:].rearrange("p (j k) -> p k j", j=J),
             )
 
         def x_apply_scale(r, k0, k1):
@@ -115,8 +127,8 @@ def tile_stochasticconfigurationcandidatescores_w4_kernel(
                 out=x_wide[i][:, n, k0:k1], in0=x_raw[i][:, n, k0:k1].bitcast(FP8), in1=scale_b[:, k0:k1], op=ALU.mult
             )
 
-        def x_turn(r, number):
-            bank = new_bank(("x", r), number)
+        def x_turn(r):
+            bank = new_bank(("x", r))
             i, n = x_place[r]
             words = x_wide[i][:, n, :].bitcast(F32)
             for v in range(2):
@@ -129,7 +141,7 @@ def tile_stochasticconfigurationcandidatescores_w4_kernel(
         def x_scale_out(r):
             nc.vector.tensor_tensor(
                 out=x_val[x_group[r][0]][:, x_group[r][1]].rearrange("p v r (u e) -> p v r u e", u=2),
-                in0=banks["x", r][:].bitcast(BF16).rearrange("p (u v r e) -> p v r u e", u=2, v=2, e=2),
+                in0=read_bank(("x", r))[:].bitcast(BF16).rearrange("p (u v r e) -> p v r u e", u=2, v=2, e=2),
                 in1=x_scl[:].rearrange("p v (u e) -> p v u e", u=2).unsqueeze(2).to_broadcast([P, 2, P, 2, 2]),
                 op=ALU.mult,
             )
@@ -137,11 +149,11 @@ def tile_stochasticconfigurationcandidatescores_w4_kernel(
         def x_copy_out(r):
             nc.scalar.copy(
                 x_val[x_group[r][0]][:, x_group[r][1]].bitcast(F32),
-                banks["x", r][:].rearrange("p (u v r) -> p v r u", u=2, v=2),
+                read_bank(("x", r))[:].rearrange("p (u v r) -> p v r u", u=2, v=2),
             )
 
-        def x_in(r, number):
-            x_turn(r, number)
+        def x_in(r):
+            x_turn(r)
             x_copy_out(r)
 
         def x_quantise(i):
@@ -151,8 +163,8 @@ def tile_stochasticconfigurationcandidatescores_w4_kernel(
                 in_=x_val[i][:].rearrange("p n v r j -> p (n v r j)"),
             )
 
-        def preact(r, b, number):
-            bank = new_bank(("xw", r, b), number)
+        def preact(r, b):
+            bank = new_bank(("xw", r, b))
             i, n = x_group[r]
             for v in range(2):
                 nc.tensor.matmul_mx(
@@ -166,14 +178,14 @@ def tile_stochasticconfigurationcandidatescores_w4_kernel(
                 )
 
         def tanh(r, b):
-            nc.scalar.activation(out=h[b, r // J][:, r % J, :], in_=banks["xw", r, b][:], func=ACT.Tanh)
+            nc.scalar.activation(out=h[b, r // J][:, r % J, :], in_=read_bank(("xw", r, b))[:], func=ACT.Tanh)
 
-        def nodes(r, b, number):
-            preact(r, b, number)
+        def nodes(r, b):
+            preact(r, b)
             tanh(r, b)
 
-        def g_turn(i, number):
-            bank = new_bank(("g", i), number)
+        def g_turn(i):
+            bank = new_bank(("g", i))
             for n in range(2):
                 words = hid[i // 2][:, 2 * (i % 2) + n, :].bitcast(F32)
                 for u in range(2):
@@ -183,11 +195,11 @@ def tile_stochasticconfigurationcandidatescores_w4_kernel(
         def g_copy_out(i):
             nc.scalar.copy(
                 g_val[:, 2 * i : 2 * i + 2].bitcast(F32),
-                banks["g", i][:].rearrange("p (n u r) -> p n r u", n=2, u=2),
+                read_bank(("g", i))[:].rearrange("p (n u r) -> p n r u", n=2, u=2),
             )
 
-        def g_in(i, number):
-            g_turn(i, number)
+        def g_in(i):
+            g_turn(i)
             g_copy_out(i)
 
         def g_quantise():
@@ -197,8 +209,8 @@ def tile_stochasticconfigurationcandidatescores_w4_kernel(
                 in_=g_val[:].rearrange("p n r j -> p (n r j)"),
             )
 
-        def beta_product(v, qb, number):
-            bank = new_bank(("gb", v, qb), number)
+        def beta_product(v, qb):
+            bank = new_bank(("gb", v, qb))
             for j in range(J):
                 nc.tensor.matmul_mx(
                     out=bank[:, j * P : (j + 1) * P],
@@ -215,7 +227,7 @@ def tile_stochasticconfigurationcandidatescores_w4_kernel(
             nc.vector.tensor_tensor(
                 out=e_val[v][:, cols, :].rearrange("p (c i) j -> p c j i", i=RUN),
                 in0=tgt[v][:, :, cols].rearrange("p j (c i) -> p c j i", i=RUN),
-                in1=banks["gb", v, qb][:].rearrange("p (j c i) -> p c j i", j=J, i=RUN),
+                in1=read_bank(("gb", v, qb))[:].rearrange("p (j c i) -> p c j i", j=J, i=RUN),
                 op=ALU.subtract,
             )
 
@@ -224,8 +236,8 @@ def tile_stochasticconfigurationcandidatescores_w4_kernel(
                 out=e_cod[v][:].bitcast(FP8X4), scales=e_csc[v][:], in_=e_val[v][:].rearrange("p q j -> p (q j)")
             )
 
-        def h_turn(i, v, number):
-            bank = new_bank(("h", i, v), number)
+        def h_turn(i, v):
+            bank = new_bank(("h", i, v))
             at = i % 4 * P
             for j in range(J):
                 nc.tensor.transpose(bank[:, j * P : (j + 1) * P], h[i // 4, v][:, j, at : at + P], ident[:])
@@ -233,13 +245,13 @@ def tile_stochasticconfigurationcandidatescores_w4_kernel(
         def energy(i, v):
             nc.scalar.activation(
                 out=squares[i % 2][:],
-                in_=banks["h", i, v][:],
+                in_=read_bank(("h", i, v))[:],
                 func=ACT.Square,
                 accum_out=hh_part[i // 4][:, i % 4, v : v + 1],
             )
 
-        def node_energy(i, v, number):
-            h_turn(i, v, number)
+        def node_energy(i, v):
+            h_turn(i, v)
             energy(i, v)
 
         def energy_sum(b):
@@ -248,11 +260,12 @@ def tile_stochasticconfigurationcandidatescores_w4_kernel(
         def energy_inverse(b):
             nc.vector.reciprocal(out=hh_inv[b][:], in_=hh_sum[b][:])
 
-        def apply_gain(b, v, n0, n1):
-            nc.vector.tensor_tensor(
+        def apply_gain(b, v, n0, n1, engine=nc.vector, gains=None):
+            gains = gain_q[:, v, :] if gains is None else gains[:]
+            engine.tensor_tensor(
                 out=hs_val[b][:, v, n0:n1].rearrange("p (c i) j -> p c j i", i=RUN),
                 in0=h[b, v][:, :, n0:n1].rearrange("p j (c i) -> p c j i", i=RUN),
-                in1=gain_q[:, v, :].unsqueeze(1).unsqueeze(3).to_broadcast([P, (n1 - n0) // RUN, J, RUN]),
+                in1=gains.unsqueeze(1).unsqueeze(3).to_broadcast([P, (n1 - n0) // RUN, J, RUN]),
                 op=ALU.mult,
             )
 
@@ -263,8 +276,8 @@ def tile_stochasticconfigurationcandidatescores_w4_kernel(
                 in_=hs_val[b][:].rearrange("p v f j -> p (v f j)")[:, J * n0 : J * n1],
             )
 
-        def correlate(i, number):
-            bank = new_bank(("c", i), number)
+        def correlate(i):
+            bank = new_bank(("c", i))
             cols = slice(i % 4 * P, (i % 4 + 1) * P)
             for v in range(2):
                 nc.tensor.matmul_mx(
@@ -278,10 +291,10 @@ def tile_stochasticconfigurationcandidatescores_w4_kernel(
                 )
 
         def square(i):
-            nc.scalar.activation(out=c_sq[i][:], in_=banks["c", i][:], func=ACT.Square)
+            nc.scalar.activation(out=c_sq[i][:], in_=read_bank(("c", i))[:], func=ACT.Square)
 
-        def correlation_squared(i, number):
-            correlate(i, number)
+        def correlation_squared(i):
+            correlate(i)
             square(i)
 
         def score(i, parts=1):
@@ -304,13 +317,14 @@ def tile_stochasticconfigurationcandidatescores_w4_kernel(
         nc.vector.memset(zeros[:], 0.0)
         nc.vector.memset(w_scl[:].rearrange("p v n -> p (v n)").bitcast(I32), 0)
         nc.vector.memset(b_scl[:].bitcast(I32), 0)
-        warm = new_bank("warm", 7)
+        warm = new_bank("warm")
 
         def warm_up(count):
             for n in range(count):
                 nc.tensor.matmul(warm[:], zeros[:, 0:P], zeros[:], start=True, stop=True)
 
         warm_up(WARM_UP_MATMULS)
+        read_bank("warm")
 
         load = nc.sync.dma_start
         x_rows = x_bytes.rearrange("(v p j) k -> v p j k", p=P, j=J)
@@ -341,8 +355,8 @@ def tile_stochasticconfigurationcandidatescores_w4_kernel(
         load_w(0)
         load_scales(w_scl, w_scales.rearrange("v r n -> r v n"))
         load_w(1)
-        load(out=hid[1][:], in_=hid_rows[1])
         load_x(3)
+        load(out=hid[1][:], in_=hid_rows[1])
         load_x(4)
         load(out=b_wrd[:].bitcast(I32), in_=beta_words[0].bitcast(I32))
         load_scales(b_scl, beta_scales[0])
@@ -357,108 +371,114 @@ def tile_stochasticconfigurationcandidatescores_w4_kernel(
             x_widen(nc.vector.tensor_copy, 1, 0, D)
             x_widen(nc.scalar.copy, 2, 0, D)
             x_widen(nc.scalar.copy, 2, D, 2 * D)
-            scale_spread(0, 4)
-            x_turn(0, 0)
-            scale_spread(1, 5)
+            scale_spread(0)
+            x_turn(0)
+            scale_spread(1)
             scale_copy_out(nc.scalar.copy, 0)
             scale_copy_out(nc.scalar.copy, 1)
-            x_turn(1, 1)
-            x_turn(2, 2)
+            x_turn(1)
+            x_turn(2)
             x_scale_out(0)
-            g_in(0, 6)
-            x_turn(3, 3)
-            g_in(1, 7)
+            g_in(0)
+            x_turn(3)
+            g_in(1)
             x_scale_out(1)
             x_quantise(0)
-            nodes(0, 0, 4)
-            nodes(0, 1, 5)
+            nodes(0, 0)
+            nodes(0, 1)
             x_scale_out(2)
             x_quantise(1)
-            nodes(1, 0, 6)
-            nodes(1, 1, 7)
-            g_in(2, 0)
-            g_in(3, 1)
+            nodes(1, 0)
+            nodes(1, 1)
+            g_in(2)
+            g_in(3)
             x_scale_out(3)
             x_apply_scale(4, 0, D)
-            x_in(4, 2)
+            x_in(4)
             x_quantise(2)
-            nodes(2, 0, 4)
-            nodes(3, 0, 5)
-            nodes(2, 1, 6)
+            nodes(2, 0)
+            nodes(3, 0)
             x_apply_scale(5, 0, D)
-            x_in(5, 3)
+            x_in(5)
+            nodes(2, 1)
             x_apply_scale(6, 0, D)
-            x_in(6, 0)
-            nodes(3, 1, 7)
+            x_in(6)
+            nodes(3, 1)
             x_apply_scale(7, 0, D)
-            x_in(7, 1)
-            node_energy(0, 0, 2)
-            node_energy(1, 0, 4)
+            x_in(7)
             g_quantise()
-            beta_product(0, 0, 6)
-            beta_product(0, 1, 5)
-            beta_product(0, 2, 7)
-            node_energy(2, 0, 3)
-            node_energy(3, 0, 0)
-            node_energy(4, 0, 1)
-            node_energy(5, 0, 2)
-            apply_gain(0, 0, 0, NODE_HALF)
             x_quantise(3)
-            nodes(4, 0, 4)
-            nodes(5, 0, 3)
+            beta_product(0, 0)
+            beta_product(0, 1)
+            nodes(4, 0)
+            nodes(5, 0)
+            node_energy(0, 0)
+            node_energy(1, 0)
+            beta_product(0, 2)
+            apply_gain(0, 0, 0, NODE_HALF)
+            nc.vector.tensor_copy(gain_f[0][:], gain_q[:, 0, :])
+            x_quantise(4)
+            apply_gain(1, 0, NODE_HALF - GPSIMD_NODES, NODE_HALF, nc.gpsimd, gain_f[0])
+            nodes(6, 0)
+            nodes(7, 0)
             residual(0, 0)
-            beta_product(0, 3, 6)
-            nodes(6, 0, 0)
+            beta_product(0, 3)
+            node_energy(2, 0)
+            node_energy(3, 0)
             residual(0, 1)
-            beta_product(1, 0, 5)
-            nodes(7, 0, 1)
+            beta_product(1, 0)
             residual(0, 2)
-            beta_product(1, 1, 7)
-            node_energy(6, 0, 2)
-            node_energy(7, 0, 4)
-            apply_gain(1, 0, 0, NODE_HALF)
-            nodes(4, 1, 3)
-            nodes(5, 1, 0)
+            beta_product(1, 1)
+            nodes(4, 1)
+            node_energy(0, 1)
+            node_energy(1, 1)
+            node_energy(2, 1)
+            hs_quantise(0, 0, NODE_HALF)
             residual(0, 3)
-            beta_product(1, 2, 6)
+            beta_product(1, 2)
+            beta_product(1, 3)
+            node_energy(3, 1)
+            node_energy(4, 0)
+            nodes(5, 1)
+            node_energy(5, 0)
+            node_energy(6, 0)
+            nodes(6, 1)
+            nc.vector.tensor_copy(gain_f[1][:], gain_q[:, 1, :])
+            apply_gain(0, 1, 0, NODE_HALF - GPSIMD_NODES)
+            apply_gain(0, 1, NODE_HALF - GPSIMD_NODES, NODE_HALF, nc.gpsimd, gain_f[1])
             residual(1, 0)
-            beta_product(1, 3, 5)
-            node_energy(0, 1, 1)
-            node_energy(1, 1, 2)
-            node_energy(2, 1, 4)
-            nodes(6, 1, 3)
-            nodes(7, 1, 0)
-            node_energy(3, 1, 1)
+            node_energy(7, 0)
+            nodes(7, 1)
             residual(1, 1)
-            e_quantise(0)
-            apply_gain(0, 1, 0, NODE_HALF)
             residual(1, 2)
             residual(1, 3)
-            hs_quantise(0, 0, 2 * NODE_HALF)
+            e_quantise(0)
+            hs_quantise(0, NODE_HALF, 2 * NODE_HALF)
             e_quantise(1)
-            node_energy(4, 1, 2)
-            node_energy(5, 1, 4)
-            correlation_squared(0, 7)
-            correlation_squared(1, 6)
-            node_energy(6, 1, 3)
-            node_energy(7, 1, 0)
-            correlation_squared(2, 5)
-            correlation_squared(3, 1)
-            hs_quantise(1, 0, NODE_HALF)
+            correlation_squared(0)
+            correlation_squared(1)
+            node_energy(4, 1)
+            node_energy(5, 1)
+            correlation_squared(2)
+            node_energy(6, 1)
+            node_energy(7, 1)
+            correlation_squared(3)
             energy_sum(0)
-            apply_gain(1, 1, 0, 256)
+            apply_gain(1, 0, 0, NODE_HALF - GPSIMD_NODES)
             energy_inverse(0)
-            apply_gain(1, 1, 256, NODE_HALF)
-            hs_quantise(1, NODE_HALF, NODE_HALF + 256)
-            correlation_squared(4, 2)
-            correlation_squared(5, 3)
+            hs_quantise(1, 0, NODE_HALF)
             score(0)
-            hs_quantise(1, NODE_HALF + 256, 2 * NODE_HALF)
-            correlation_squared(6, 4)
-            correlation_squared(7, 0)
+            apply_gain(1, 1, 0, 256)
             score(1)
+            hs_quantise(1, NODE_HALF, NODE_HALF + 256)
+            correlation_squared(4)
+            correlation_squared(5)
+            apply_gain(1, 1, 256, NODE_HALF)
             energy_sum(1)
             score(2)
+            hs_quantise(1, NODE_HALF + 256, 2 * NODE_HALF)
+            correlation_squared(6)
+            correlation_squared(7)
             energy_inverse(1)
             score(3)
             score(4)

@@ -53,17 +53,16 @@ def tile_stochasticconfigurationcandidatescores_w4_kernel(
         hid = [sbuf("hid%d" % v, [P, J, L], BF16) for v in range(2)]
         tgt = [sbuf("tgt%d" % v, [P, J, Q], BF16) for v in range(2)]
         gain_q = sbuf("gain_q", [P, 2, J], BF16)
-        gain_f = [sbuf("gain_f%d" % v, [P, J], F32) for v in range(2)]
+        gain_f = [sbuf("gain_f%d" % n, [P, J], F32) for n in range(8)]
         tau_b = sbuf("tau_b", [P, Q], BF16)
 
-        scale_b = sbuf("scale_b", [P, D], F32)
-        x_wide = [sbuf("x_wide%d" % i, [P, n, D], BF16) for i, n in enumerate(X_LOADS)]
+        x_wide = [sbuf("x_wide%d" % r, [P, D], BF16) for r in range(ROW_TILES)]
         x_val = [sbuf("x_val%d" % i, [P, n, 2, P, J], BF16) for i, n in enumerate(X_GROUPS)]
         x_cod = [sbuf("x_cod%d" % i, [P, n, 2, P], U32) for i, n in enumerate(X_GROUPS)]
         x_csc = [sbuf("x_csc%d" % i, [P, n, 2, P], U8) for i, n in enumerate(X_GROUPS)]
-        g_val = sbuf("g_val", [P, ROW_TILES, P, J], BF16)
-        g_cod = sbuf("g_cod", [P, ROW_TILES, P], U32)
-        g_csc = sbuf("g_csc", [P, ROW_TILES, P], U8)
+        g_val = [sbuf("g_val%d" % v, [P, J, P, J], BF16) for v in range(2)]
+        g_cod = [sbuf("g_cod%d" % v, [P, J, P], U32) for v in range(2)]
+        g_csc = [sbuf("g_csc%d" % v, [P, J, P], U8) for v in range(2)]
         e_val = [sbuf("e_val%d" % v, [P, Q, J], BF16) for v in range(2)]
         e_cod = [sbuf("e_cod%d" % v, [P, Q], U32) for v in range(2)]
         e_csc = [sbuf("e_csc%d" % v, [P, Q], U8) for v in range(2)]
@@ -80,6 +79,8 @@ def tile_stochasticconfigurationcandidatescores_w4_kernel(
         res = [sbuf("res%d" % i, [P, Q], F32) for i in range(8)]
 
         ident = sbuf("ident", [P, P], F32)
+        ident_b = sbuf("ident_b", [P, P], BF16)
+        ones = sbuf("ones", [P, 1], F32)
         zeros = sbuf("zeros", [P, BANK], BF16)
         dummy = sbuf("dummy", [P, 2], F32)
 
@@ -102,35 +103,31 @@ def tile_stochasticconfigurationcandidatescores_w4_kernel(
 
         x_group = [(i, n) for i, count in enumerate(X_GROUPS) for n in range(count)]
 
-        def x_widen(copy, i, k0, k1):
-            copy(
-                x_wide[i][:].rearrange("p n k -> p (n k)")[:, k0:k1],
-                x_raw[i][:].rearrange("p n k -> p (n k)")[:, k0:k1].bitcast(FP8),
-            )
-
-        def scale_spread(v):
-            bank = new_bank(("s", v))
-            for j in range(J):
-                nc.tensor.transpose(
-                    bank[:, j * P : (j + 1) * P], x_scl[:, v, j : j + 1].to_broadcast([P, P]), ident[:]
-                )
-
-        def scale_copy_out(copy, v):
-            copy(
-                scale_b[:, v * BANK : (v + 1) * BANK].rearrange("p (k j) -> p k j", j=J),
-                read_bank(("s", v))[:].rearrange("p (j k) -> p k j", j=J),
-            )
-
-        def x_apply_scale(r, k0, k1):
+        def x_widen(copy, r, k0=0, k1=D):
             i, n = x_place[r]
-            nc.vector.tensor_tensor(
-                out=x_wide[i][:, n, k0:k1], in0=x_raw[i][:, n, k0:k1].bitcast(FP8), in1=scale_b[:, k0:k1], op=ALU.mult
+            copy(x_wide[r][:, k0:k1], x_raw[i][:, n, k0:k1].bitcast(FP8))
+
+        def x_widen_split(r, m0=0, m1=D // J):
+            i, n = x_place[r]
+            nc.vector.tensor_scalar(
+                out=x_wide[r][:].rearrange("p (u m e) -> p m u e", u=2, e=2)[:, m0:m1],
+                in0=x_raw[i][:, n, J * m0 : J * m1].bitcast(FP8),
+                scalar1=ones[:],
+                scalar2=None,
+                op0=ALU.mult,
             )
+
+        def x_turn_split(r):
+            bank = new_bank(("x", r))
+            words = x_wide[r][:].bitcast(F32)
+            for v in range(2):
+                for u in range(2):
+                    at = (2 * u + v) * P
+                    nc.tensor.transpose(bank[:, at : at + P], words[:, at : at + P], ident[:])
 
         def x_turn(r):
             bank = new_bank(("x", r))
-            i, n = x_place[r]
-            words = x_wide[i][:, n, :].bitcast(F32)
+            words = x_wide[r][:].bitcast(F32)
             for v in range(2):
                 for u in range(2):
                     at = (2 * u + v) * P
@@ -145,16 +142,6 @@ def tile_stochasticconfigurationcandidatescores_w4_kernel(
                 in1=x_scl[:].rearrange("p v (u e) -> p v u e", u=2).unsqueeze(2).to_broadcast([P, 2, P, 2, 2]),
                 op=ALU.mult,
             )
-
-        def x_copy_out(r):
-            nc.scalar.copy(
-                x_val[x_group[r][0]][:, x_group[r][1]].bitcast(F32),
-                read_bank(("x", r))[:].rearrange("p (u v r) -> p v r u", u=2, v=2),
-            )
-
-        def x_in(r):
-            x_turn(r)
-            x_copy_out(r)
 
         def x_quantise(i):
             nc.vector.quantize_mx(
@@ -184,6 +171,11 @@ def tile_stochasticconfigurationcandidatescores_w4_kernel(
             preact(r, b)
             tanh(r, b)
 
+        def constants():
+            bank = new_bank("const")[:].bitcast(BF16)
+            nc.tensor.matmul(bank[:, 0:Q], ident_b[:], tau_b[:], start=True, stop=True)
+            nc.tensor.matmul(bank[:, Q : Q + 2 * J], ident_b[:], gain_q[:].rearrange("p v j -> p (v j)"), start=True, stop=True)
+
         def g_turn(i):
             bank = new_bank(("g", i))
             for n in range(2):
@@ -194,7 +186,7 @@ def tile_stochasticconfigurationcandidatescores_w4_kernel(
 
         def g_copy_out(i):
             nc.scalar.copy(
-                g_val[:, 2 * i : 2 * i + 2].bitcast(F32),
+                g_val[i // 2][:, 2 * (i % 2) : 2 * (i % 2) + 2].bitcast(F32),
                 read_bank(("g", i))[:].rearrange("p (n u r) -> p n r u", n=2, u=2),
             )
 
@@ -202,11 +194,11 @@ def tile_stochasticconfigurationcandidatescores_w4_kernel(
             g_turn(i)
             g_copy_out(i)
 
-        def g_quantise():
+        def g_quantise(v):
             nc.vector.quantize_mx(
-                out=g_cod[:].rearrange("p n r -> p (n r)").bitcast(FP8X4),
-                scales=g_csc[:].rearrange("p n r -> p (n r)"),
-                in_=g_val[:].rearrange("p n r j -> p (n r j)"),
+                out=g_cod[v][:].rearrange("p n r -> p (n r)").bitcast(FP8X4),
+                scales=g_csc[v][:].rearrange("p n r -> p (n r)"),
+                in_=g_val[v][:].rearrange("p n r j -> p (n r j)"),
             )
 
         def beta_product(v, qb):
@@ -214,8 +206,8 @@ def tile_stochasticconfigurationcandidatescores_w4_kernel(
             for j in range(J):
                 nc.tensor.matmul_mx(
                     out=bank[:, j * P : (j + 1) * P],
-                    lhsT=g_cod[:, J * v + j, :].bitcast(FP8X4),
-                    lhsT_scale=g_csc[:, J * v + j, :],
+                    lhsT=g_cod[v][:, j, :].bitcast(FP8X4),
+                    lhsT_scale=g_csc[v][:, j, :],
                     rhs=b_wrd[:, qb * P * FP4_BYTES : (qb + 1) * P * FP4_BYTES].bitcast(FP4X4),
                     rhs_scale=b_scl[:, qb * P : (qb + 1) * P],
                     start=True,
@@ -260,14 +252,22 @@ def tile_stochasticconfigurationcandidatescores_w4_kernel(
         def energy_inverse(b):
             nc.vector.reciprocal(out=hh_inv[b][:], in_=hh_sum[b][:])
 
-        def apply_gain(b, v, n0, n1, engine=nc.vector, gains=None):
-            gains = gain_q[:, v, :] if gains is None else gains[:]
+        def apply_gain(engine, gains, b, v, n0, n1):
             engine.tensor_tensor(
                 out=hs_val[b][:, v, n0:n1].rearrange("p (c i) j -> p c j i", i=RUN),
                 in0=h[b, v][:, :, n0:n1].rearrange("p j (c i) -> p c j i", i=RUN),
                 in1=gains.unsqueeze(1).unsqueeze(3).to_broadcast([P, (n1 - n0) // RUN, J, RUN]),
                 op=ALU.mult,
             )
+
+        def gain_vector(b, v, n0, n1):
+            gains = banks["const"][1][:].bitcast(BF16)[:, Q + J * v : Q + J * (v + 1)]
+            apply_gain(nc.vector, gains, b, v, n0, n1)
+
+        def gain_gpsimd(b, v, n0, n1):
+            gains = gain_f.pop()
+            nc.vector.tensor_copy(gains[:], gain_q[:, v, :])
+            apply_gain(nc.gpsimd, gains[:], b, v, n0, n1)
 
         def hs_quantise(b, n0, n1):
             nc.vector.quantize_mx(
@@ -276,25 +276,25 @@ def tile_stochasticconfigurationcandidatescores_w4_kernel(
                 in_=hs_val[b][:].rearrange("p v f j -> p (v f j)")[:, J * n0 : J * n1],
             )
 
-        def correlate(i):
-            bank = new_bank(("c", i))
+        def correlate(i, v):
+            bank = new_bank(("c", i)) if v == 0 else banks["c", i][1]
             cols = slice(i % 4 * P, (i % 4 + 1) * P)
-            for v in range(2):
-                nc.tensor.matmul_mx(
-                    out=bank[:],
-                    lhsT=hs_cod[i // 4][:, v, cols].bitcast(FP8X4),
-                    lhsT_scale=hs_csc[i // 4][:, v, cols],
-                    rhs=e_cod[v][:].bitcast(FP8X4),
-                    rhs_scale=e_csc[v][:],
-                    start=(v == 0),
-                    stop=(v == 1),
-                )
+            nc.tensor.matmul_mx(
+                out=bank[:],
+                lhsT=hs_cod[i // 4][:, v, cols].bitcast(FP8X4),
+                lhsT_scale=hs_csc[i // 4][:, v, cols],
+                rhs=e_cod[v][:].bitcast(FP8X4),
+                rhs_scale=e_csc[v][:],
+                start=(v == 0),
+                stop=(v == 1),
+            )
 
         def square(i):
             nc.scalar.activation(out=c_sq[i][:], in_=read_bank(("c", i))[:], func=ACT.Square)
 
         def correlation_squared(i):
-            correlate(i)
+            correlate(i, 0)
+            correlate(i, 1)
             square(i)
 
         def score(i, parts=1):
@@ -305,7 +305,7 @@ def tile_stochasticconfigurationcandidatescores_w4_kernel(
                     out=res[i][:, cols],
                     in0=c_sq[i][:, cols],
                     scalar=hh_inv[i // 4][:, i % 4 : i % 4 + 1],
-                    in1=tau_b[:, cols],
+                    in1=banks["const"][1][:].bitcast(BF16)[:, cols],
                     op0=ALU.mult,
                     op1=ALU.subtract,
                 )
@@ -314,6 +314,8 @@ def tile_stochasticconfigurationcandidatescores_w4_kernel(
         make_identity(nc, ident[:])
         nc.vector.memset(dummy[:], 0.0)
         nc.scalar.activation(out=dummy[:, 1:2], in_=dummy[:, 0:1], func=ACT.Tanh)
+        nc.scalar.copy(ident_b[:], ident[:])
+        nc.vector.memset(ones[:], 1.0)
         nc.vector.memset(zeros[:], 0.0)
         nc.vector.memset(w_scl[:].rearrange("p v n -> p (v n)").bitcast(I32), 0)
         nc.vector.memset(b_scl[:].bitcast(I32), 0)
@@ -323,8 +325,7 @@ def tile_stochasticconfigurationcandidatescores_w4_kernel(
             for n in range(count):
                 nc.tensor.matmul(warm[:], zeros[:, 0:P], zeros[:], start=True, stop=True)
 
-        warm_up(WARM_UP_MATMULS)
-        read_bank("warm")
+        warm_up(3)
 
         load = nc.sync.dma_start
         x_rows = x_bytes.rearrange("(v p j) k -> v p j k", p=P, j=J)
@@ -351,134 +352,142 @@ def tile_stochasticconfigurationcandidatescores_w4_kernel(
         load(out=x_scl[:], in_=x_scale.rearrange("o (v p j) -> p (o v) j", p=P, j=J))
         load_x(1)
         load_x(2)
-        load(out=hid[0][:], in_=hid_rows[0])
+        load_x(3)
         load_w(0)
         load_scales(w_scl, w_scales.rearrange("v r n -> r v n"))
-        load_w(1)
-        load_x(3)
-        load(out=hid[1][:], in_=hid_rows[1])
         load_x(4)
+        load_w(1)
+        load(out=hid[0][:], in_=hid_rows[0])
+        load(out=gain_q[:], in_=gain.rearrange("(v p j) -> p v j", p=P, j=J))
+        load(out=tau_b[:], in_=tau.partition_broadcast(P))
+        load(out=hid[1][:], in_=hid_rows[1])
         load(out=b_wrd[:].bitcast(I32), in_=beta_words[0].bitcast(I32))
         load_scales(b_scl, beta_scales[0])
-        load(out=gain_q[:], in_=gain.rearrange("(v p j) -> p v j", p=P, j=J))
         load(out=tgt[0][:], in_=tgt_rows[0])
         load(out=tgt[1][:], in_=tgt_rows[1])
-        load(out=tau_b[:], in_=tau.partition_broadcast(P))
 
         with tc.manual_schedule():
-            x_widen(nc.vector.tensor_copy, 0, 0, BANK)
-            x_widen(nc.vector.tensor_copy, 0, BANK, D)
-            x_widen(nc.vector.tensor_copy, 1, 0, D)
-            x_widen(nc.scalar.copy, 2, 0, D)
-            x_widen(nc.scalar.copy, 2, D, 2 * D)
-            scale_spread(0)
-            x_turn(0)
-            scale_spread(1)
-            scale_copy_out(nc.scalar.copy, 0)
-            scale_copy_out(nc.scalar.copy, 1)
-            x_turn(1)
-            x_turn(2)
+            x_widen_split(0, 0, P)
+            x_widen_split(0, P, 2 * P)
+            x_widen_split(1)
+            x_widen_split(2)
+            x_widen(nc.scalar.copy, 4)
+            x_widen(nc.scalar.copy, 5)
+            x_widen(nc.scalar.copy, 6)
+            x_turn_split(0)
+            warm_up(1)
+            x_turn_split(1)
+            warm_up(1)
+            x_turn_split(2)
+            warm_up(1)
+            read_bank("warm")
             x_scale_out(0)
-            g_in(0)
-            x_turn(3)
-            g_in(1)
-            x_scale_out(1)
+            x_widen_split(3)
             x_quantise(0)
+            x_turn(4)
+            x_turn_split(3)
+            x_scale_out(1)
             nodes(0, 0)
             nodes(0, 1)
+            x_widen(nc.scalar.copy, 7)
             x_scale_out(2)
             x_quantise(1)
+            x_turn(5)
+            x_turn(6)
             nodes(1, 0)
             nodes(1, 1)
-            g_in(2)
-            g_in(3)
             x_scale_out(3)
-            x_apply_scale(4, 0, D)
-            x_in(4)
+            x_scale_out(4)
             x_quantise(2)
+            g_in(0)
+            g_in(1)
+            constants()
             nodes(2, 0)
             nodes(3, 0)
-            x_apply_scale(5, 0, D)
-            x_in(5)
             nodes(2, 1)
-            x_apply_scale(6, 0, D)
-            x_in(6)
             nodes(3, 1)
-            x_apply_scale(7, 0, D)
-            x_in(7)
-            g_quantise()
+            x_scale_out(5)
+            x_scale_out(6)
             x_quantise(3)
-            beta_product(0, 0)
-            beta_product(0, 1)
+            g_quantise(0)
+            x_turn(7)
+            g_in(2)
+            gain_gpsimd(0, 0, 320, 512)
+            x_scale_out(7)
             nodes(4, 0)
             nodes(5, 0)
+            gain_vector(0, 0, 0, 320)
+            g_in(3)
             node_energy(0, 0)
             node_energy(1, 0)
-            beta_product(0, 2)
-            apply_gain(0, 0, 0, NODE_HALF)
-            nc.vector.tensor_copy(gain_f[0][:], gain_q[:, 0, :])
+            node_energy(2, 0)
             x_quantise(4)
-            apply_gain(1, 0, NODE_HALF - GPSIMD_NODES, NODE_HALF, nc.gpsimd, gain_f[0])
+            beta_product(0, 0)
+            beta_product(0, 1)
+            g_quantise(1)
+            gain_gpsimd(1, 0, 320, 512)
+            residual(0, 0)
+            residual(0, 1)
+            beta_product(0, 2)
+            beta_product(0, 3)
             nodes(6, 0)
             nodes(7, 0)
-            residual(0, 0)
-            beta_product(0, 3)
-            node_energy(2, 0)
-            node_energy(3, 0)
-            residual(0, 1)
-            beta_product(1, 0)
             residual(0, 2)
-            beta_product(1, 1)
-            nodes(4, 1)
-            node_energy(0, 1)
-            node_energy(1, 1)
-            node_energy(2, 1)
-            hs_quantise(0, 0, NODE_HALF)
             residual(0, 3)
-            beta_product(1, 2)
-            beta_product(1, 3)
-            node_energy(3, 1)
+            hs_quantise(0, 0, NODE_HALF)
+            node_energy(3, 0)
             node_energy(4, 0)
-            nodes(5, 1)
             node_energy(5, 0)
             node_energy(6, 0)
-            nodes(6, 1)
-            nc.vector.tensor_copy(gain_f[1][:], gain_q[:, 1, :])
-            apply_gain(0, 1, 0, NODE_HALF - GPSIMD_NODES)
-            apply_gain(0, 1, NODE_HALF - GPSIMD_NODES, NODE_HALF, nc.gpsimd, gain_f[1])
+            beta_product(1, 0)
+            beta_product(1, 1)
+            e_quantise(0)
+            gain_gpsimd(0, 1, 128, 512)
+            gain_vector(1, 0, 0, 320)
             residual(1, 0)
-            node_energy(7, 0)
-            nodes(7, 1)
             residual(1, 1)
+            beta_product(1, 2)
+            beta_product(1, 3)
+            nodes(4, 1)
+            nodes(5, 1)
             residual(1, 2)
             residual(1, 3)
-            e_quantise(0)
-            hs_quantise(0, NODE_HALF, 2 * NODE_HALF)
-            e_quantise(1)
-            correlation_squared(0)
-            correlation_squared(1)
+            nodes(6, 1)
+            nodes(7, 1)
+            gain_vector(0, 1, 0, 128)
+            node_energy(7, 0)
+            node_energy(0, 1)
+            node_energy(1, 1)
+            correlate(0, 0)
+            correlate(1, 0)
+            node_energy(2, 1)
+            node_energy(3, 1)
             node_energy(4, 1)
-            node_energy(5, 1)
+            e_quantise(1)
+            hs_quantise(0, NODE_HALF, 2 * NODE_HALF)
+            hs_quantise(1, 0, NODE_HALF)
+            gain_gpsimd(1, 1, 384, 512)
+            correlate(0, 1)
+            correlate(1, 1)
+            square(0)
+            square(1)
             correlation_squared(2)
+            gain_vector(1, 1, 0, 384)
+            node_energy(5, 1)
             node_energy(6, 1)
             node_energy(7, 1)
-            correlation_squared(3)
             energy_sum(0)
-            apply_gain(1, 0, 0, NODE_HALF - GPSIMD_NODES)
+            hs_quantise(1, NODE_HALF, 2 * NODE_HALF)
             energy_inverse(0)
-            hs_quantise(1, 0, NODE_HALF)
-            score(0)
-            apply_gain(1, 1, 0, 256)
-            score(1)
-            hs_quantise(1, NODE_HALF, NODE_HALF + 256)
+            correlation_squared(3)
             correlation_squared(4)
             correlation_squared(5)
-            apply_gain(1, 1, 256, NODE_HALF)
-            energy_sum(1)
-            score(2)
-            hs_quantise(1, NODE_HALF + 256, 2 * NODE_HALF)
             correlation_squared(6)
             correlation_squared(7)
+            score(0)
+            score(1)
+            score(2)
+            energy_sum(1)
             energy_inverse(1)
             score(3)
             score(4)

@@ -50,10 +50,10 @@ def tile_stochasticconfigurationcandidatescores_w4_kernel(
         w_scl = sbuf("w_scl", [P, 2, F], U8)
         b_wrd = sbuf("b_wrd", [P, FP4_BYTES * Q], U8)
         b_scl = sbuf("b_scl", [P, Q], U8)
-        hid = [sbuf("hid%d" % v, [P, J, L], BF16) for v in range(2)]
+        hid = [sbuf("hid%d" % i, [P, 2, L], BF16) for i in range(4)]
         tgt = [sbuf("tgt%d" % v, [P, J, Q], BF16) for v in range(2)]
         gain_q = sbuf("gain_q", [P, 2, J], BF16)
-        gain_f = [sbuf("gain_f%d" % n, [P, J], F32) for n in range(8)]
+        gain_f = sbuf("gain_f", [P, 2, J], F32)
         tau_b = sbuf("tau_b", [P, Q], BF16)
 
         x_wide = [sbuf("x_wide%d" % r, [P, D], BF16) for r in range(ROW_TILES)]
@@ -68,7 +68,9 @@ def tile_stochasticconfigurationcandidatescores_w4_kernel(
         e_csc = [sbuf("e_csc%d" % v, [P, Q], U8) for v in range(2)]
         chunks = [(b, v) for b in range(2) for v in range(2)]
         h = {k: sbuf("h%d%d" % k, [P, J, NODE_HALF], F32) for k in chunks}
-        hs_val = [sbuf("hs_val%d" % b, [P, 2, NODE_HALF, J], BF16) for b in range(2)]
+        g_as_nodes = [tile[:].rearrange("p n r j -> p (n r) j") for tile in g_val]
+        hs_val = {(0, 0): g_as_nodes[0], (1, 0): g_as_nodes[1], (0, 1): g_as_nodes[1], (1, 1): g_as_nodes[1]}
+
         hs_cod = [sbuf("hs_cod%d" % b, [P, 2, NODE_HALF], U32) for b in range(2)]
         hs_csc = [sbuf("hs_csc%d" % b, [P, 2, NODE_HALF], U8) for b in range(2)]
         hh_part = [sbuf("hh_part%d" % b, [P, 4, 2], F32) for b in range(2)]
@@ -171,21 +173,23 @@ def tile_stochasticconfigurationcandidatescores_w4_kernel(
             preact(r, b)
             tanh(r, b)
 
-        def constants():
-            bank = new_bank("const")[:].bitcast(BF16)
-            nc.tensor.matmul(bank[:, 0:Q], ident_b[:], tau_b[:], start=True, stop=True)
-            nc.tensor.matmul(bank[:, Q : Q + 2 * J], ident_b[:], gain_q[:].rearrange("p v j -> p (v j)"), start=True, stop=True)
+        def gains_to_psum():
+            bank = new_bank("gains")
+            nc.tensor.matmul(bank[:, 0 : 2 * J], ident_b[:], gain_q[:].rearrange("p v j -> p (v j)"), start=True, stop=True)
+
+        def tau_to_psum():
+            nc.tensor.matmul(new_bank("tau")[:], ident_b[:], tau_b[:], start=True, stop=True)
 
         def g_turn(i):
             bank = new_bank(("g", i))
             for n in range(2):
-                words = hid[i // 2][:, 2 * (i % 2) + n, :].bitcast(F32)
+                words = hid[i][:, n, :].bitcast(F32)
                 for u in range(2):
                     at = (2 * n + u) * P
                     nc.tensor.transpose(bank[:, at : at + P], words[:, u:256:2], ident[:])
 
-        def g_copy_out(i):
-            nc.scalar.copy(
+        def g_copy_out(i, copy=nc.scalar.copy):
+            copy(
                 g_val[i // 2][:, 2 * (i % 2) : 2 * (i % 2) + 2].bitcast(F32),
                 read_bank(("g", i))[:].rearrange("p (n u r) -> p n r u", n=2, u=2),
             )
@@ -236,44 +240,43 @@ def tile_stochasticconfigurationcandidatescores_w4_kernel(
 
         def energy(i, v):
             nc.scalar.activation(
-                out=squares[i % 2][:],
+                out=squares[0][:],
                 in_=read_bank(("h", i, v))[:],
                 func=ACT.Square,
                 accum_out=hh_part[i // 4][:, i % 4, v : v + 1],
             )
+            squares.reverse()
 
         def node_energy(i, v):
             h_turn(i, v)
             energy(i, v)
 
         def energy_sum(b):
-            nc.vector.tensor_tensor(out=hh_sum[b][:], in0=hh_part[b][:, :, 0], in1=hh_part[b][:, :, 1], op=ALU.add)
+            nc.vector.tensor_reduce(out=hh_sum[b][:], in_=hh_part[b][:], axis=mybir.AxisListType.X, op=ALU.add)
 
         def energy_inverse(b):
             nc.vector.reciprocal(out=hh_inv[b][:], in_=hh_sum[b][:])
 
         def apply_gain(engine, gains, b, v, n0, n1):
             engine.tensor_tensor(
-                out=hs_val[b][:, v, n0:n1].rearrange("p (c i) j -> p c j i", i=RUN),
+                out=hs_val[b, v][:, n0:n1].rearrange("p (c i) j -> p c j i", i=RUN),
                 in0=h[b, v][:, :, n0:n1].rearrange("p j (c i) -> p c j i", i=RUN),
                 in1=gains.unsqueeze(1).unsqueeze(3).to_broadcast([P, (n1 - n0) // RUN, J, RUN]),
                 op=ALU.mult,
             )
 
         def gain_vector(b, v, n0, n1):
-            gains = banks["const"][1][:].bitcast(BF16)[:, Q + J * v : Q + J * (v + 1)]
+            gains = banks["gains"][1][:, J * v : J * (v + 1)]
             apply_gain(nc.vector, gains, b, v, n0, n1)
 
         def gain_gpsimd(b, v, n0, n1):
-            gains = gain_f.pop()
-            nc.vector.tensor_copy(gains[:], gain_q[:, v, :])
-            apply_gain(nc.gpsimd, gains[:], b, v, n0, n1)
+            apply_gain(nc.gpsimd, gain_f[:, v, :], b, v, n0, n1)
 
-        def hs_quantise(b, n0, n1):
+        def hs_quantise(b, v, n0=0, n1=NODE_HALF):
             nc.vector.quantize_mx(
-                out=hs_cod[b][:].rearrange("p v f -> p (v f)")[:, n0:n1].bitcast(FP8X4),
-                scales=hs_csc[b][:].rearrange("p v f -> p (v f)")[:, n0:n1],
-                in_=hs_val[b][:].rearrange("p v f j -> p (v f j)")[:, J * n0 : J * n1],
+                out=hs_cod[b][:, v, n0:n1].bitcast(FP8X4),
+                scales=hs_csc[b][:, v, n0:n1],
+                in_=hs_val[b, v][:, n0:n1].rearrange("p f j -> p (f j)"),
             )
 
         def correlate(i, v):
@@ -305,7 +308,7 @@ def tile_stochasticconfigurationcandidatescores_w4_kernel(
                     out=res[i][:, cols],
                     in0=c_sq[i][:, cols],
                     scalar=hh_inv[i // 4][:, i % 4 : i % 4 + 1],
-                    in1=banks["const"][1][:].bitcast(BF16)[:, cols],
+                    in1=banks["tau"][1][:, cols],
                     op0=ALU.mult,
                     op1=ALU.subtract,
                 )
@@ -337,6 +340,9 @@ def tile_stochasticconfigurationcandidatescores_w4_kernel(
             r = sum(X_LOADS[:i])
             load(out=x_raw[i][:], in_=x_rows[r // J][:, r % J : r % J + X_LOADS[i], :])
 
+        def load_g(i):
+            load(out=hid[i][:], in_=hid_rows[i // 2][:, 2 * (i % 2) : 2 * (i % 2) + 2, :])
+
         def load_w(b):
             width = FP4_BYTES * NODE_HALF
             load(out=w_wrd[b][:].bitcast(I32), in_=w_rows[:, :, b * width : (b + 1) * width].bitcast(I32))
@@ -349,83 +355,93 @@ def tile_stochasticconfigurationcandidatescores_w4_kernel(
                 )
 
         load_x(0)
-        load(out=x_scl[:], in_=x_scale.rearrange("o (v p j) -> p (o v) j", p=P, j=J))
         load_x(1)
         load_x(2)
+        load(out=x_scl[:], in_=x_scale.rearrange("o (v p j) -> p (o v) j", p=P, j=J))
+        load_g(0)
         load_x(3)
         load_w(0)
         load_scales(w_scl, w_scales.rearrange("v r n -> r v n"))
         load_x(4)
         load_w(1)
-        load(out=hid[0][:], in_=hid_rows[0])
+        load_g(1)
         load(out=gain_q[:], in_=gain.rearrange("(v p j) -> p v j", p=P, j=J))
-        load(out=tau_b[:], in_=tau.partition_broadcast(P))
-        load(out=hid[1][:], in_=hid_rows[1])
+        load_g(2)
+        load_g(3)
         load(out=b_wrd[:].bitcast(I32), in_=beta_words[0].bitcast(I32))
         load_scales(b_scl, beta_scales[0])
         load(out=tgt[0][:], in_=tgt_rows[0])
         load(out=tgt[1][:], in_=tgt_rows[1])
+        load(out=tau_b[:], in_=tau.partition_broadcast(P))
 
         with tc.manual_schedule():
             x_widen_split(0, 0, P)
             x_widen_split(0, P, 2 * P)
             x_widen_split(1)
-            x_widen_split(2)
-            x_widen(nc.scalar.copy, 4)
-            x_widen(nc.scalar.copy, 5)
-            x_widen(nc.scalar.copy, 6)
+            x_widen(nc.scalar.copy, 2)
+            x_widen(nc.scalar.copy, 3)
             x_turn_split(0)
             warm_up(1)
             x_turn_split(1)
             warm_up(1)
-            x_turn_split(2)
+            x_turn(2)
+            g_turn(0)
             warm_up(1)
             read_bank("warm")
+            x_widen(nc.scalar.copy, 4)
+            g_copy_out(0)
+            x_widen(nc.scalar.copy, 5)
             x_scale_out(0)
-            x_widen_split(3)
-            x_quantise(0)
-            x_turn(4)
-            x_turn_split(3)
             x_scale_out(1)
+            x_quantise(0)
+            x_turn(3)
             nodes(0, 0)
             nodes(0, 1)
-            x_widen(nc.scalar.copy, 7)
+            x_widen(nc.scalar.copy, 6)
             x_scale_out(2)
             x_quantise(1)
+            x_turn(4)
             x_turn(5)
-            x_turn(6)
             nodes(1, 0)
             nodes(1, 1)
             x_scale_out(3)
             x_scale_out(4)
             x_quantise(2)
-            g_in(0)
+            x_widen(nc.scalar.copy, 7)
             g_in(1)
-            constants()
+            x_turn(6)
+            gains_to_psum()
             nodes(2, 0)
             nodes(3, 0)
             nodes(2, 1)
-            nodes(3, 1)
             x_scale_out(5)
             x_scale_out(6)
+            nc.vector.tensor_copy(gain_f[:], gain_q[:])
             x_quantise(3)
             g_quantise(0)
             x_turn(7)
-            g_in(2)
-            gain_gpsimd(0, 0, 320, 512)
-            x_scale_out(7)
-            nodes(4, 0)
-            nodes(5, 0)
-            gain_vector(0, 0, 0, 320)
-            g_in(3)
+            nodes(3, 1)
             node_energy(0, 0)
             node_energy(1, 0)
+            g_turn(2)
+            g_turn(3)
+            gain_gpsimd(0, 0, 256, 512)
+            x_scale_out(7)
+            gain_vector(0, 0, 0, 256)
+            g_copy_out(2, nc.vector.tensor_copy)
+            g_copy_out(3, nc.vector.tensor_copy)
+            nodes(4, 0)
+            nodes(5, 0)
             node_energy(2, 0)
+            node_energy(3, 0)
+            node_energy(4, 0)
+            node_energy(5, 0)
             x_quantise(4)
             beta_product(0, 0)
             beta_product(0, 1)
+            hs_quantise(0, 0)
             g_quantise(1)
-            gain_gpsimd(1, 0, 320, 512)
+            gain_gpsimd(1, 0, 224, 512)
             residual(0, 0)
             residual(0, 1)
             beta_product(0, 2)
@@ -434,61 +450,65 @@ def tile_stochasticconfigurationcandidatescores_w4_kernel(
             nodes(7, 0)
             residual(0, 2)
             residual(0, 3)
-            hs_quantise(0, 0, NODE_HALF)
-            node_energy(3, 0)
-            node_energy(4, 0)
-            node_energy(5, 0)
+            gain_vector(1, 0, 0, 224)
             node_energy(6, 0)
+            node_energy(7, 0)
+            node_energy(0, 1)
+            node_energy(1, 1)
             beta_product(1, 0)
             beta_product(1, 1)
             e_quantise(0)
-            gain_gpsimd(0, 1, 128, 512)
-            gain_vector(1, 0, 0, 320)
+            hs_quantise(1, 0)
+            gain_gpsimd(0, 1, 224, 512)
             residual(1, 0)
             residual(1, 1)
+            nodes(4, 1)
             beta_product(1, 2)
             beta_product(1, 3)
-            nodes(4, 1)
             nodes(5, 1)
             residual(1, 2)
             residual(1, 3)
             nodes(6, 1)
             nodes(7, 1)
-            gain_vector(0, 1, 0, 128)
-            node_energy(7, 0)
-            node_energy(0, 1)
-            node_energy(1, 1)
-            correlate(0, 0)
-            correlate(1, 0)
+            gain_vector(0, 1, 0, 224)
             node_energy(2, 1)
             node_energy(3, 1)
+            correlate(0, 0)
+            correlate(1, 0)
             node_energy(4, 1)
+            node_energy(5, 1)
+            tau_to_psum()
             e_quantise(1)
-            hs_quantise(0, NODE_HALF, 2 * NODE_HALF)
-            hs_quantise(1, 0, NODE_HALF)
-            gain_gpsimd(1, 1, 384, 512)
+            hs_quantise(0, 1)
+            gain_gpsimd(1, 1, 320, 512)
+            energy_sum(0)
             correlate(0, 1)
             correlate(1, 1)
             square(0)
             square(1)
-            correlation_squared(2)
-            gain_vector(1, 1, 0, 384)
-            node_energy(5, 1)
+            gain_vector(1, 1, 0, 160)
+            energy_inverse(0)
+            gain_vector(1, 1, 160, 320)
+            read_bank("gains")
             node_energy(6, 1)
             node_energy(7, 1)
-            energy_sum(0)
-            hs_quantise(1, NODE_HALF, 2 * NODE_HALF)
-            energy_inverse(0)
+            correlation_squared(2)
             correlation_squared(3)
-            correlation_squared(4)
-            correlation_squared(5)
-            correlation_squared(6)
-            correlation_squared(7)
+            correlate(4, 0)
+            correlate(5, 0)
             score(0)
             score(1)
-            score(2)
+            hs_quantise(1, 1, 0, 256)
+            hs_quantise(1, 1, 256, 512)
             energy_sum(1)
             energy_inverse(1)
+            correlate(4, 1)
+            square(4)
+            correlate(5, 1)
+            square(5)
+            correlation_squared(6)
+            correlation_squared(7)
+            score(2)
             score(3)
             score(4)
             score(5)

@@ -292,8 +292,12 @@ def tile_stochasticconfigurationcandidatescores_w4_kernel(
                 stop=(v == 1),
             )
 
-        def square(i):
-            nc.scalar.activation(out=c_sq[i][:], in_=read_bank(("c", i))[:], func=ACT.Square)
+        def square(i, parts=1):
+            bank = read_bank(("c", i))
+            width = Q // parts
+            for part in range(parts):
+                cols = slice(part * width, (part + 1) * width)
+                nc.scalar.activation(out=c_sq[i][:, cols], in_=bank[:, cols], func=ACT.Square)
 
         def correlation_squared(i):
             correlate(i, 0)
@@ -358,8 +362,8 @@ def tile_stochasticconfigurationcandidatescores_w4_kernel(
         load_x(1)
         load_x(2)
         load(out=x_scl[:], in_=x_scale.rearrange("o (v p j) -> p (o v) j", p=P, j=J))
-        load_g(0)
         load_x(3)
+        load_g(0)
         load_w(0)
         load_scales(w_scl, w_scales.rearrange("v r n -> r v n"))
         load_x(4)
@@ -378,39 +382,39 @@ def tile_stochasticconfigurationcandidatescores_w4_kernel(
             x_widen_split(0, 0, P)
             x_widen_split(0, P, 2 * P)
             x_widen_split(1)
-            x_widen(nc.scalar.copy, 2)
+            x_widen_split(2)
             x_widen(nc.scalar.copy, 3)
+            x_widen(nc.scalar.copy, 4)
+            x_widen(nc.scalar.copy, 5)
             x_turn_split(0)
             warm_up(1)
             x_turn_split(1)
             warm_up(1)
-            x_turn(2)
-            g_turn(0)
+            x_turn_split(2)
+            x_turn(3)
             warm_up(1)
             read_bank("warm")
-            x_widen(nc.scalar.copy, 4)
-            g_copy_out(0)
-            x_widen(nc.scalar.copy, 5)
+            g_in(0)
+            x_turn(4)
             x_scale_out(0)
             x_scale_out(1)
             x_quantise(0)
-            x_turn(3)
+            x_widen(nc.scalar.copy, 6)
             nodes(0, 0)
             nodes(0, 1)
-            x_widen(nc.scalar.copy, 6)
+            x_widen(nc.scalar.copy, 7)
             x_scale_out(2)
             x_quantise(1)
-            x_turn(4)
             x_turn(5)
+            g_turn(1)
             nodes(1, 0)
             nodes(1, 1)
             x_scale_out(3)
             x_scale_out(4)
             x_quantise(2)
-            x_widen(nc.scalar.copy, 7)
-            g_in(1)
+            g_copy_out(1)
             x_turn(6)
-            gains_to_psum()
+            x_turn(7)
             nodes(2, 0)
             nodes(3, 0)
             nodes(2, 1)
@@ -419,10 +423,10 @@ def tile_stochasticconfigurationcandidatescores_w4_kernel(
             nc.vector.tensor_copy(gain_f[:], gain_q[:])
             x_quantise(3)
             g_quantise(0)
-            x_turn(7)
             nodes(3, 1)
             node_energy(0, 0)
             node_energy(1, 0)
+            gains_to_psum()
             g_turn(2)
             g_turn(3)
             gain_gpsimd(0, 0, 256, 512)
@@ -507,7 +511,9 @@ def tile_stochasticconfigurationcandidatescores_w4_kernel(
             correlate(5, 1)
             square(5)
             correlation_squared(6)
-            correlation_squared(7)
+            correlate(7, 0)
+            correlate(7, 1)
+            square(7, parts=LAST_BLOCK_PARTS)
             score(2)
             score(3)
             score(4)

@@ -52,7 +52,8 @@ def tile_stochasticconfigurationcandidatescores_w4_kernel(
         b_scl = sbuf("b_scl", [P, Q], U8)
         hid = [sbuf("hid%d" % i, [P, 2, L], BF16) for i in range(4)]
         tgt = [sbuf("tgt%d" % v, [P, J, Q], BF16) for v in range(2)]
-        gain_q = sbuf("gain_q", [P, 2, J], BF16)
+        gain_pad = sbuf("gain_pad", [P, P], BF16)
+        gain_q = gain_pad[:, 0 : 2 * J].rearrange("p (v j) -> p v j", j=J)
         gain_f = sbuf("gain_f", [P, 2, J], F32)
         tau_b = sbuf("tau_b", [P, Q], BF16)
 
@@ -175,7 +176,7 @@ def tile_stochasticconfigurationcandidatescores_w4_kernel(
 
         def gains_to_psum():
             bank = new_bank("gains")
-            nc.tensor.matmul(bank[:, 0 : 2 * J], ident_b[:], gain_q[:].rearrange("p v j -> p (v j)"), start=True, stop=True)
+            nc.tensor.matmul(bank[:, 0:P], ident_b[:], gain_pad[:], start=True, stop=True)
 
         def tau_to_psum():
             nc.tensor.matmul(new_bank("tau")[:], ident_b[:], tau_b[:], start=True, stop=True)
@@ -319,6 +320,7 @@ def tile_stochasticconfigurationcandidatescores_w4_kernel(
                 nc.sync.dma_start(out=out[i * P : (i + 1) * P, cols], in_=res[i][:, cols])
 
         make_identity(nc, ident[:])
+        nc.scalar.dma_start(out=x_scl[:], in_=x_scale.rearrange("o (v p j) -> p (o v) j", p=P, j=J))
         nc.vector.memset(dummy[:], 0.0)
         nc.scalar.activation(out=dummy[:, 1:2], in_=dummy[:, 0:1], func=ACT.Tanh)
         nc.scalar.copy(ident_b[:], ident[:])
@@ -326,6 +328,7 @@ def tile_stochasticconfigurationcandidatescores_w4_kernel(
         nc.vector.memset(zeros[:], 0.0)
         nc.vector.memset(w_scl[:].rearrange("p v n -> p (v n)").bitcast(I32), 0)
         nc.vector.memset(b_scl[:].bitcast(I32), 0)
+        nc.vector.memset(gain_pad[:], 0.0)
         warm = new_bank("warm")
 
         def warm_up(count):
@@ -361,7 +364,6 @@ def tile_stochasticconfigurationcandidatescores_w4_kernel(
         load_x(0)
         load_x(1)
         load_x(2)
-        load(out=x_scl[:], in_=x_scale.rearrange("o (v p j) -> p (o v) j", p=P, j=J))
         load_x(3)
         load_g(0)
         load_w(0)
@@ -415,34 +417,32 @@ def tile_stochasticconfigurationcandidatescores_w4_kernel(
             g_copy_out(1)
             x_turn(6)
             x_turn(7)
+            nc.scalar.copy(gain_f[:], gain_q[:])
             nodes(2, 0)
             nodes(3, 0)
             nodes(2, 1)
             x_scale_out(5)
             x_scale_out(6)
-            nc.vector.tensor_copy(gain_f[:], gain_q[:])
             x_quantise(3)
             g_quantise(0)
             nodes(3, 1)
             node_energy(0, 0)
             node_energy(1, 0)
             gains_to_psum()
-            g_turn(2)
-            g_turn(3)
-            gain_gpsimd(0, 0, 256, 512)
+            g_in(2)
+            g_in(3)
+            gain_gpsimd(0, 0, 320, 512)
             x_scale_out(7)
-            gain_vector(0, 0, 0, 256)
-            g_copy_out(2, nc.vector.tensor_copy)
-            g_copy_out(3, nc.vector.tensor_copy)
+            gain_vector(0, 0, 0, 320)
             nodes(4, 0)
             nodes(5, 0)
+            beta_product(0, 0)
+            beta_product(0, 1)
             node_energy(2, 0)
             node_energy(3, 0)
             node_energy(4, 0)
             node_energy(5, 0)
             x_quantise(4)
-            beta_product(0, 0)
-            beta_product(0, 1)
             hs_quantise(0, 0)
             g_quantise(1)
             gain_gpsimd(1, 0, 224, 512)
@@ -484,15 +484,15 @@ def tile_stochasticconfigurationcandidatescores_w4_kernel(
             tau_to_psum()
             e_quantise(1)
             hs_quantise(0, 1)
-            gain_gpsimd(1, 1, 320, 512)
+            gain_gpsimd(1, 1, 288, 512)
             energy_sum(0)
             correlate(0, 1)
             correlate(1, 1)
             square(0)
             square(1)
-            gain_vector(1, 1, 0, 160)
+            gain_vector(1, 1, 0, 144)
             energy_inverse(0)
-            gain_vector(1, 1, 160, 320)
+            gain_vector(1, 1, 144, 288)
             read_bank("gains")
             node_energy(6, 1)
             node_energy(7, 1)
@@ -505,7 +505,6 @@ def tile_stochasticconfigurationcandidatescores_w4_kernel(
             hs_quantise(1, 1, 0, 256)
             hs_quantise(1, 1, 256, 512)
             energy_sum(1)
-            energy_inverse(1)
             correlate(4, 1)
             square(4)
             correlate(5, 1)
@@ -515,6 +514,7 @@ def tile_stochasticconfigurationcandidatescores_w4_kernel(
             correlate(7, 1)
             square(7, parts=LAST_BLOCK_PARTS)
             score(2)
+            energy_inverse(1)
             score(3)
             score(4)
             score(5)

@@ -174,12 +174,10 @@ def tile_stochasticconfigurationcandidatescores_w4_kernel(
             preact(r, b)
             tanh(r, b)
 
-        def gains_to_psum():
-            bank = new_bank("gains")
-            nc.tensor.matmul(bank[:, 0:P], ident_b[:], gain_pad[:], start=True, stop=True)
-
-        def tau_to_psum():
-            nc.tensor.matmul(new_bank("tau")[:], ident_b[:], tau_b[:], start=True, stop=True)
+        def constants_to_psum():
+            bank = new_bank("constants")[:].bitcast(BF16)
+            nc.tensor.matmul(bank[:, 0:Q], ident_b[:], tau_b[:], start=True, stop=True)
+            nc.tensor.matmul(bank[:, Q : Q + P], ident_b[:], gain_pad[:], start=True, stop=True)
 
         def g_turn(i):
             bank = new_bank(("g", i))
@@ -188,6 +186,27 @@ def tile_stochasticconfigurationcandidatescores_w4_kernel(
                 for u in range(2):
                     at = (2 * n + u) * P
                     nc.tensor.transpose(bank[:, at : at + P], words[:, u:256:2], ident[:])
+
+        def g_split_place(i):
+            return x_val[i - 1][:].rearrange("p n v r j -> p (n v r j)")[:, 0 : 2 * L]
+
+        def g_split(i):
+            nc.gpsimd.tensor_scalar(
+                out=g_split_place(i).rearrange("p (u m e) -> p u m e", u=2, e=2),
+                in0=hid[i][:].rearrange("p n (q u e) -> p u (n q) e", u=2, e=2),
+                scalar1=1.0,
+                scalar2=0.0,
+                op0=ALU.mult,
+                op1=ALU.add,
+            )
+
+        def g_turn_split(i):
+            bank = new_bank(("g", i))
+            words = g_split_place(i).bitcast(F32)
+            for n in range(2):
+                for u in range(2):
+                    at = (2 * n + u) * P
+                    nc.tensor.transpose(bank[:, at : at + P], words[:, (2 * u + n) * P : (2 * u + n + 1) * P], ident[:])
 
         def g_copy_out(i, copy=nc.scalar.copy):
             copy(
@@ -267,7 +286,7 @@ def tile_stochasticconfigurationcandidatescores_w4_kernel(
             )
 
         def gain_vector(b, v, n0, n1):
-            gains = banks["gains"][1][:, J * v : J * (v + 1)]
+            gains = banks["constants"][1][:].bitcast(BF16)[:, Q + J * v : Q + J * (v + 1)]
             apply_gain(nc.vector, gains, b, v, n0, n1)
 
         def gain_gpsimd(b, v, n0, n1):
@@ -313,7 +332,7 @@ def tile_stochasticconfigurationcandidatescores_w4_kernel(
                     out=res[i][:, cols],
                     in0=c_sq[i][:, cols],
                     scalar=hh_inv[i // 4][:, i % 4 : i % 4 + 1],
-                    in1=banks["tau"][1][:, cols],
+                    in1=banks["constants"][1][:].bitcast(BF16)[:, cols],
                     op0=ALU.mult,
                     op1=ALU.subtract,
                 )
@@ -335,7 +354,7 @@ def tile_stochasticconfigurationcandidatescores_w4_kernel(
             for n in range(count):
                 nc.tensor.matmul(warm[:], zeros[:, 0:P], zeros[:], start=True, stop=True)
 
-        warm_up(3)
+        warm_up(2)
 
         load = nc.sync.dma_start
         x_rows = x_bytes.rearrange("(v p j) k -> v p j k", p=P, j=J)
@@ -374,11 +393,11 @@ def tile_stochasticconfigurationcandidatescores_w4_kernel(
         load(out=gain_q[:], in_=gain.rearrange("(v p j) -> p v j", p=P, j=J))
         load_g(2)
         load_g(3)
+        load(out=tau_b[:], in_=tau.partition_broadcast(P))
         load(out=b_wrd[:].bitcast(I32), in_=beta_words[0].bitcast(I32))
         load_scales(b_scl, beta_scales[0])
         load(out=tgt[0][:], in_=tgt_rows[0])
         load(out=tgt[1][:], in_=tgt_rows[1])
-        load(out=tau_b[:], in_=tau.partition_broadcast(P))
 
         with tc.manual_schedule():
             x_widen_split(0, 0, P)
@@ -394,7 +413,7 @@ def tile_stochasticconfigurationcandidatescores_w4_kernel(
             warm_up(1)
             x_turn_split(2)
             x_turn(3)
-            warm_up(1)
+            warm_up(2)
             read_bank("warm")
             g_in(0)
             x_turn(4)
@@ -414,6 +433,7 @@ def tile_stochasticconfigurationcandidatescores_w4_kernel(
             x_scale_out(3)
             x_scale_out(4)
             x_quantise(2)
+            g_split(3)
             g_copy_out(1)
             x_turn(6)
             x_turn(7)
@@ -428,9 +448,10 @@ def tile_stochasticconfigurationcandidatescores_w4_kernel(
             nodes(3, 1)
             node_energy(0, 0)
             node_energy(1, 0)
-            gains_to_psum()
+            constants_to_psum()
             g_in(2)
-            g_in(3)
+            g_turn_split(3)
+            g_copy_out(3)
             gain_gpsimd(0, 0, 320, 512)
             x_scale_out(7)
             gain_vector(0, 0, 0, 320)
@@ -477,13 +498,12 @@ def tile_stochasticconfigurationcandidatescores_w4_kernel(
             gain_vector(0, 1, 0, 224)
             node_energy(2, 1)
             node_energy(3, 1)
-            correlate(0, 0)
-            correlate(1, 0)
             node_energy(4, 1)
             node_energy(5, 1)
-            tau_to_psum()
             e_quantise(1)
             hs_quantise(0, 1)
+            correlate(0, 0)
+            correlate(1, 0)
             gain_gpsimd(1, 1, 288, 512)
             energy_sum(0)
             correlate(0, 1)
@@ -493,7 +513,6 @@ def tile_stochasticconfigurationcandidatescores_w4_kernel(
             gain_vector(1, 1, 0, 144)
             energy_inverse(0)
             gain_vector(1, 1, 144, 288)
-            read_bank("gains")
             node_energy(6, 1)
             node_energy(7, 1)
             correlation_squared(2)

@@ -27,7 +27,7 @@ RUN = 4
 FP4_BYTES = 2
 
 X_LOADS = (1, 1, 2, 2, 2)
-X_GROUPS = (1, 1, 2, 2, 2)
+X_GROUPS = (2, 2, 2, 2)
 WARM_UP_MATMULS = 3
 GPSIMD_NODES = 128
 LAST_BLOCK_PARTS = 2
@@ -57,8 +57,10 @@ def tile_stochasticconfigurationcandidatescores_w4_kernel(
         gain_f = sbuf("gain_f", [P, 2, J], F32)
         tau_b = sbuf("tau_b", [P, Q], BF16)
 
-        x_wide = [sbuf("x_wide%d" % r, [P, D], BF16) for r in range(ROW_TILES)]
         x_val = [sbuf("x_val%d" % i, [P, n, 2, P, J], BF16) for i, n in enumerate(X_GROUPS)]
+        x_wide = [sbuf("x_wide%d" % r, [P, D], BF16)[:] for r in range(ROW_TILES - 1)]
+        x_wide.append(x_val[0][:, 0].rearrange("p v r j -> p (v r j)"))
+        x_pairs = [sbuf("x_pairs%d" % r, [P, D // 2], F32) for r in range(ROW_TILES)]
         x_cod = [sbuf("x_cod%d" % i, [P, n, 2, P], U32) for i, n in enumerate(X_GROUPS)]
         x_csc = [sbuf("x_csc%d" % i, [P, n, 2, P], U8) for i, n in enumerate(X_GROUPS)]
         g_val = [sbuf("g_val%d" % v, [P, J, P, J], BF16) for v in range(2)]
@@ -113,7 +115,7 @@ def tile_stochasticconfigurationcandidatescores_w4_kernel(
         def x_widen_split(r, m0=0, m1=D // J):
             i, n = x_place[r]
             nc.vector.tensor_scalar(
-                out=x_wide[r][:].rearrange("p (u m e) -> p m u e", u=2, e=2)[:, m0:m1],
+                out=x_wide[r].rearrange("p (u m e) -> p m u e", u=2, e=2)[:, m0:m1],
                 in0=x_raw[i][:, n, J * m0 : J * m1].bitcast(FP8),
                 scalar1=ones[:],
                 scalar2=None,
@@ -122,15 +124,28 @@ def tile_stochasticconfigurationcandidatescores_w4_kernel(
 
         def x_turn_split(r):
             bank = new_bank(("x", r))
-            words = x_wide[r][:].bitcast(F32)
+            words = x_wide[r].bitcast(F32)
             for v in range(2):
                 for u in range(2):
                     at = (2 * u + v) * P
                     nc.tensor.transpose(bank[:, at : at + P], words[:, at : at + P], ident[:])
 
+        def x_split(r):
+            nc.scalar.copy(
+                x_pairs[r][:].rearrange("p (u m) -> p u m", u=2),
+                x_wide[r].bitcast(F32).rearrange("p (m u) -> p u m", u=2),
+            )
+
+        def x_turn_pairs(r):
+            bank = new_bank(("x", r))
+            for v in range(2):
+                for u in range(2):
+                    at = (2 * u + v) * P
+                    nc.tensor.transpose(bank[:, at : at + P], x_pairs[r][:, at : at + P], ident[:])
+
         def x_turn(r):
             bank = new_bank(("x", r))
-            words = x_wide[r][:].bitcast(F32)
+            words = x_wide[r].bitcast(F32)
             for v in range(2):
                 for u in range(2):
                     at = (2 * u + v) * P
@@ -188,7 +203,7 @@ def tile_stochasticconfigurationcandidatescores_w4_kernel(
                     nc.tensor.transpose(bank[:, at : at + P], words[:, u:256:2], ident[:])
 
         def g_split_place(i):
-            return x_val[i - 1][:].rearrange("p n v r j -> p (n v r j)")[:, 0 : 2 * L]
+            return x_val[i - 2][:].rearrange("p n v r j -> p (n v r j)")[:, 0 : 2 * L]
 
         def g_split(i):
             nc.gpsimd.tensor_scalar(
@@ -384,12 +399,12 @@ def tile_stochasticconfigurationcandidatescores_w4_kernel(
         load_x(1)
         load_x(2)
         load_x(3)
+        load_x(4)
         load_g(0)
+        load_g(1)
         load_w(0)
         load_scales(w_scl, w_scales.rearrange("v r n -> r v n"))
-        load_x(4)
         load_w(1)
-        load_g(1)
         load(out=gain_q[:], in_=gain.rearrange("(v p j) -> p v j", p=P, j=J))
         load_g(2)
         load_g(3)
@@ -403,53 +418,56 @@ def tile_stochasticconfigurationcandidatescores_w4_kernel(
             x_widen_split(0, 0, P)
             x_widen_split(0, P, 2 * P)
             x_widen_split(1)
-            x_widen_split(2)
+            x_widen(nc.scalar.copy, 2)
             x_widen(nc.scalar.copy, 3)
             x_widen(nc.scalar.copy, 4)
-            x_widen(nc.scalar.copy, 5)
+            x_widen(nc.gpsimd.tensor_copy, 5)
+            x_widen(nc.gpsimd.tensor_copy, 6)
             x_turn_split(0)
             warm_up(1)
             x_turn_split(1)
             warm_up(1)
-            x_turn_split(2)
+            x_turn(2)
+            g_turn(0)
             x_turn(3)
-            warm_up(2)
+            g_turn(1)
+            warm_up(1)
             read_bank("warm")
-            g_in(0)
             x_turn(4)
+            x_split(5)
             x_scale_out(0)
+            x_turn_pairs(5)
             x_scale_out(1)
+            x_scale_out(2)
             x_quantise(0)
-            x_widen(nc.scalar.copy, 6)
+            x_widen(nc.gpsimd.tensor_copy, 7)
+            g_copy_out(0)
+            x_split(6)
+            g_copy_out(1)
             nodes(0, 0)
             nodes(0, 1)
-            x_widen(nc.scalar.copy, 7)
-            x_scale_out(2)
-            x_quantise(1)
-            x_turn(5)
-            g_turn(1)
+            x_split(7)
             nodes(1, 0)
             nodes(1, 1)
             x_scale_out(3)
             x_scale_out(4)
-            x_quantise(2)
+            x_quantise(1)
             g_split(3)
-            g_copy_out(1)
-            x_turn(6)
-            x_turn(7)
+            x_turn_pairs(6)
+            g_in(2)
+            x_turn_pairs(7)
             nc.scalar.copy(gain_f[:], gain_q[:])
             nodes(2, 0)
             nodes(3, 0)
             nodes(2, 1)
             x_scale_out(5)
             x_scale_out(6)
-            x_quantise(3)
+            x_quantise(2)
             g_quantise(0)
             nodes(3, 1)
+            constants_to_psum()
             node_energy(0, 0)
             node_energy(1, 0)
-            constants_to_psum()
-            g_in(2)
             g_turn_split(3)
             g_copy_out(3)
             gain_gpsimd(0, 0, 320, 512)
@@ -463,7 +481,7 @@ def tile_stochasticconfigurationcandidatescores_w4_kernel(
             node_energy(3, 0)
             node_energy(4, 0)
             node_energy(5, 0)
-            x_quantise(4)
+            x_quantise(3)
             hs_quantise(0, 0)
             g_quantise(1)
             gain_gpsimd(1, 0, 224, 512)

@@ -286,15 +286,22 @@ def tile_stochasticconfigurationcandidatescores_w4_kernel(
             h_turn(i, v)
             energy(i, v)
 
-        def energy_sum(b):
-            nc.vector.tensor_reduce(out=hh_sum[b][:], in_=hh_part[b][:], axis=mybir.AxisListType.X, op=ALU.add)
+        def energy_sum(b, n0=0, n1=4):
+            nc.vector.tensor_reduce(
+                out=hh_sum[b][:, n0:n1], in_=hh_part[b][:, n0:n1], axis=mybir.AxisListType.X, op=ALU.add
+            )
 
-        def energy_inverse(b):
-            nc.vector.reciprocal(out=hh_inv[b][:], in_=hh_sum[b][:])
+        def energy_inverse(b, n0=0, n1=4):
+            nc.vector.reciprocal(out=hh_inv[b][:, n0:n1], in_=hh_sum[b][:, n0:n1])
+
+        def hs_place(b, v, n0, n1):
+            if (b, v) == (1, 1) and n1 <= NODE_HALF // 2:
+                return g_as_nodes[0][:, n0:n1]
+            return hs_val[b, v][:, n0:n1]
 
         def apply_gain(engine, gains, b, v, n0, n1):
             engine.tensor_tensor(
-                out=hs_val[b, v][:, n0:n1].rearrange("p (c i) j -> p c j i", i=RUN),
+                out=hs_place(b, v, n0, n1).rearrange("p (c i) j -> p c j i", i=RUN),
                 in0=h[b, v][:, :, n0:n1].rearrange("p j (c i) -> p c j i", i=RUN),
                 in1=gains.unsqueeze(1).unsqueeze(3).to_broadcast([P, (n1 - n0) // RUN, J, RUN]),
                 op=ALU.mult,
@@ -305,13 +312,18 @@ def tile_stochasticconfigurationcandidatescores_w4_kernel(
             apply_gain(nc.vector, gains, b, v, n0, n1)
 
         def gain_gpsimd(b, v, n0, n1):
-            apply_gain(nc.gpsimd, gain_f[:, v, :], b, v, n0, n1)
+            nc.gpsimd.tensor_tensor(
+                out=hs_place(b, v, n0, n1),
+                in0=h[b, v][:, :, n0:n1].rearrange("p j f -> p f j"),
+                in1=gain_f[:, v, :].unsqueeze(1).to_broadcast([P, n1 - n0, J]),
+                op=ALU.mult,
+            )
 
         def hs_quantise(b, v, n0=0, n1=NODE_HALF):
             nc.vector.quantize_mx(
                 out=hs_cod[b][:, v, n0:n1].bitcast(FP8X4),
                 scales=hs_csc[b][:, v, n0:n1],
-                in_=hs_val[b, v][:, n0:n1].rearrange("p f j -> p (f j)"),
+                in_=hs_place(b, v, n0, n1).rearrange("p f j -> p (f j)"),
             )
 
         def correlate(i, v):
@@ -523,25 +535,30 @@ def tile_stochasticconfigurationcandidatescores_w4_kernel(
             correlate(0, 0)
             correlate(1, 0)
             gain_gpsimd(1, 1, 288, 512)
-            energy_sum(0)
             correlate(0, 1)
             correlate(1, 1)
             square(0)
             square(1)
             gain_vector(1, 1, 0, 144)
+            energy_sum(0)
+            gain_vector(1, 1, 144, 256)
             energy_inverse(0)
-            gain_vector(1, 1, 144, 288)
-            node_energy(6, 1)
-            node_energy(7, 1)
+            gain_vector(1, 1, 256, 288)
             correlation_squared(2)
             correlation_squared(3)
+            node_energy(6, 1)
+            node_energy(7, 1)
             correlate(4, 0)
             correlate(5, 0)
             score(0)
             score(1)
             hs_quantise(1, 1, 0, 256)
             hs_quantise(1, 1, 256, 512)
-            energy_sum(1)
+            energy_sum(1, 0, 2)
+            score(2)
+            energy_inverse(1, 0, 2)
+            score(3)
+            energy_sum(1, 2, 4)
             correlate(4, 1)
             square(4)
             correlate(5, 1)
@@ -550,10 +567,8 @@ def tile_stochasticconfigurationcandidatescores_w4_kernel(
             correlate(7, 0)
             correlate(7, 1)
             square(7, parts=LAST_BLOCK_PARTS)
-            score(2)
-            energy_inverse(1)
-            score(3)
             score(4)
+            energy_inverse(1, 2, 4)
             score(5)
             score(6)
             score(7, parts=LAST_BLOCK_PARTS)

@@ -86,7 +86,6 @@ def tile_stochasticconfigurationcandidatescores_w4_kernel(
         ident = sbuf("ident", [P, P], F32)
         ident_b = sbuf("ident_b", [P, P], BF16)
         ones = sbuf("ones", [P, 1], F32)
-        zeros = sbuf("zeros", [P, BANK], BF16)
         dummy = sbuf("dummy", [P, 2], F32)
 
         banks = {}
@@ -371,17 +370,9 @@ def tile_stochasticconfigurationcandidatescores_w4_kernel(
         nc.scalar.activation(out=dummy[:, 1:2], in_=dummy[:, 0:1], func=ACT.Tanh)
         nc.scalar.copy(ident_b[:], ident[:])
         nc.vector.memset(ones[:], 1.0)
-        nc.vector.memset(zeros[:], 0.0)
         nc.vector.memset(w_scl[:].rearrange("p v n -> p (v n)").bitcast(I32), 0)
         nc.vector.memset(b_scl[:].bitcast(I32), 0)
         nc.vector.memset(gain_pad[:], 0.0)
-        warm = new_bank("warm")
-
-        def warm_up(count):
-            for n in range(count):
-                nc.tensor.matmul(warm[:], zeros[:, 0:P], zeros[:], start=True, stop=True)
-
-        warm_up(2)
 
         load = nc.sync.dma_start
         x_rows = x_bytes.rearrange("(v p j) k -> v p j k", p=P, j=J)
@@ -436,15 +427,11 @@ def tile_stochasticconfigurationcandidatescores_w4_kernel(
             x_widen(nc.gpsimd.tensor_copy, 5)
             x_widen(nc.gpsimd.tensor_copy, 6)
             x_turn_split(0)
-            warm_up(1)
             x_turn_split(1)
-            warm_up(1)
             x_turn(2)
             g_turn(0)
             x_turn(3)
             g_turn(1)
-            warm_up(1)
-            read_bank("warm")
             x_turn(4)
             x_split(5)
             x_scale_out(0)

@@ -31,6 +31,7 @@ X_GROUPS = (2, 2, 2, 2)
 WARM_UP_MATMULS = 3
 GPSIMD_NODES = 128
 LAST_BLOCK_PARTS = 2
+PART = 2048
 
 
 def tile_stochasticconfigurationcandidatescores_w4_kernel(
@@ -57,25 +58,35 @@ def tile_stochasticconfigurationcandidatescores_w4_kernel(
         gain_f = sbuf("gain_f", [P, 2, J], F32)
         tau_b = sbuf("tau_b", [P, Q], BF16)
 
-        x_val = [sbuf("x_val%d" % i, [P, n, 2, P, J], BF16) for i, n in enumerate(X_GROUPS)]
+        trio = sbuf("trio", [P, 3, PART], BF16)
+        duo = sbuf("duo", [P, 2, PART], BF16)
+        as_x = "p (n k r j) -> p n k r j"
+        x_val = [sbuf("x_val%d" % i, [P, 2, 2, P, J], BF16)[:] for i in range(2)]
+        x_val.extend(tile[:, 0].rearrange(as_x, n=2, k=2, j=J) for tile in (trio, duo))
+        joint_cod = [sbuf("joint_cod%d" % i, [P, 2, PART // J], U32) for i in range(4)]
+        joint_csc = [sbuf("joint_csc%d" % i, [P, 2, PART // J], U8) for i in range(4)]
         x_wide = [sbuf("x_wide%d" % r, [P, D], BF16)[:] for r in range(ROW_TILES - 1)]
         x_wide.append(x_val[0][:, 0].rearrange("p v r j -> p (v r j)"))
         x_pairs = [sbuf("x_pairs%d" % r, [P, D // 2], F32) for r in range(ROW_TILES)]
-        x_cod = [sbuf("x_cod%d" % i, [P, n, 2, P], U32) for i, n in enumerate(X_GROUPS)]
-        x_csc = [sbuf("x_csc%d" % i, [P, n, 2, P], U8) for i, n in enumerate(X_GROUPS)]
-        g_val = [sbuf("g_val%d" % v, [P, J, P, J], BF16) for v in range(2)]
-        g_cod = [sbuf("g_cod%d" % v, [P, J, P], U32) for v in range(2)]
-        g_csc = [sbuf("g_csc%d" % v, [P, J, P], U8) for v in range(2)]
-        e_val = [sbuf("e_val%d" % v, [P, Q, J], BF16) for v in range(2)]
-        e_cod = [sbuf("e_cod%d" % v, [P, Q], U32) for v in range(2)]
-        e_csc = [sbuf("e_csc%d" % v, [P, Q], U8) for v in range(2)]
+        x_cod = [sbuf("x_cod%d" % i, [P, 2, 2, P], U32)[:] for i in range(2)]
+        x_csc = [sbuf("x_csc%d" % i, [P, 2, 2, P], U8)[:] for i in range(2)]
+        x_cod.extend(tile[:, 0].rearrange("p (n k r) -> p n k r", n=2, k=2) for tile in joint_cod[:2])
+        x_csc.extend(tile[:, 0].rearrange("p (n k r) -> p n k r", n=2, k=2) for tile in joint_csc[:2])
+        g_val = [tile[:, 1].rearrange("p (n r j) -> p n r j", n=J, j=J) for tile in (trio, duo)]
+        g_cod = [tile[:, 1].rearrange("p (n r) -> p n r", n=J) for tile in joint_cod[:2]]
+        g_csc = [tile[:, 1].rearrange("p (n r) -> p n r", n=J) for tile in joint_csc[:2]]
+        e_val = [trio[:, 2 * v].rearrange("p (q j) -> p q j", j=J) for v in range(2)]
+        e_cod = [joint_cod[2 + v][:, v] for v in range(2)]
+        e_csc = [joint_csc[2 + v][:, v] for v in range(2)]
         chunks = [(b, v) for b in range(2) for v in range(2)]
         h = {k: sbuf("h%d%d" % k, [P, J, NODE_HALF], F32) for k in chunks}
-        g_as_nodes = [tile[:].rearrange("p n r j -> p (n r) j") for tile in g_val]
-        hs_val = {(0, 0): g_as_nodes[0], (1, 0): g_as_nodes[1], (0, 1): g_as_nodes[1], (1, 1): g_as_nodes[1]}
-
-        hs_cod = [sbuf("hs_cod%d" % b, [P, 2, NODE_HALF], U32) for b in range(2)]
-        hs_csc = [sbuf("hs_csc%d" % b, [P, 2, NODE_HALF], U8) for b in range(2)]
+        places = {(0, 0): trio[:, 1], (1, 0): trio[:, 1], (0, 1): trio[:, 0], (1, 1): trio[:, 2]}
+        hs_val = {k: place.rearrange("p (f j) -> p f j", j=J) for k, place in places.items()}
+        hs_spare = duo[:, 1].rearrange("p (f j) -> p f j", j=J)
+        hs_cod = {(0, 0): sbuf("hs_cod00", [P, NODE_HALF], U32)[:], (1, 1): sbuf("hs_cod11", [P, NODE_HALF], U32)[:]}
+        hs_csc = {(0, 0): sbuf("hs_csc00", [P, NODE_HALF], U8)[:], (1, 1): sbuf("hs_csc11", [P, NODE_HALF], U8)[:]}
+        hs_cod.update({(1, 0): joint_cod[2][:, 1], (0, 1): joint_cod[3][:, 0]})
+        hs_csc.update({(1, 0): joint_csc[2][:, 1], (0, 1): joint_csc[3][:, 0]})
         hh_part = [sbuf("hh_part%d" % b, [P, 4, 2], F32) for b in range(2)]
         hh_sum = [sbuf("hh_sum%d" % b, [P, 4], F32) for b in range(2)]
         hh_inv = [sbuf("hh_inv%d" % b, [P, 4], F32) for b in range(2)]
@@ -162,9 +173,9 @@ def tile_stochasticconfigurationcandidatescores_w4_kernel(
 
         def x_quantise(i):
             nc.vector.quantize_mx(
-                out=x_cod[i][:].rearrange("p n v r -> p (n v r)").bitcast(FP8X4),
-                scales=x_csc[i][:].rearrange("p n v r -> p (n v r)"),
-                in_=x_val[i][:].rearrange("p n v r j -> p (n v r j)"),
+                out=x_cod[i].rearrange("p n v r -> p (n v r)").bitcast(FP8X4),
+                scales=x_csc[i].rearrange("p n v r -> p (n v r)"),
+                in_=x_val[i].rearrange("p n v r j -> p (n v r j)"),
             )
 
         def preact(r, b):
@@ -188,10 +199,13 @@ def tile_stochasticconfigurationcandidatescores_w4_kernel(
             preact(r, b)
             tanh(r, b)
 
-        def constants_to_psum():
+        def gains_to_psum():
             bank = new_bank("constants")[:].bitcast(BF16)
-            nc.tensor.matmul(bank[:, 0:Q], ident_b[:], tau_b[:], start=True, stop=True)
             nc.tensor.matmul(bank[:, Q : Q + P], ident_b[:], gain_pad[:], start=True, stop=True)
+
+        def tau_to_psum():
+            bank = banks["constants"][1][:].bitcast(BF16)
+            nc.tensor.matmul(bank[:, 0:Q], ident_b[:], tau_b[:], start=True, stop=True)
 
         def g_turn(i):
             bank = new_bank(("g", i))
@@ -201,22 +215,28 @@ def tile_stochasticconfigurationcandidatescores_w4_kernel(
                     at = (2 * n + u) * P
                     nc.tensor.transpose(bank[:, at : at + P], words[:, u:256:2], ident[:])
 
-        def g_split_place(i):
-            return x_val[i - 2][:].rearrange("p n v r j -> p (n v r j)")[:, 0 : 2 * L]
+        sorted_place = x_val[1][:, 0].rearrange("p k r j -> p (k r j)")
 
-        def g_split(i):
+        def sort_gpsimd(rows):
             nc.gpsimd.tensor_scalar(
-                out=g_split_place(i).rearrange("p (u m e) -> p u m e", u=2, e=2),
-                in0=hid[i][:].rearrange("p n (q u e) -> p u (n q) e", u=2, e=2),
+                out=sorted_place.rearrange("p (u m e) -> p u m e", u=2, e=2),
+                in0=rows.rearrange("p (m u e) -> p u m e", u=2, e=2),
                 scalar1=1.0,
                 scalar2=0.0,
                 op0=ALU.mult,
                 op1=ALU.add,
             )
 
+        def x_split_gpsimd(r):
+            x_pairs[r] = sorted_place.bitcast(F32)
+            sort_gpsimd(x_wide[r])
+
+        def g_split(i):
+            sort_gpsimd(hid[i][:].rearrange("p n k -> p (n k)"))
+
         def g_turn_split(i):
             bank = new_bank(("g", i))
-            words = g_split_place(i).bitcast(F32)
+            words = sorted_place.bitcast(F32)
             for n in range(2):
                 for u in range(2):
                     at = (2 * n + u) * P
@@ -232,11 +252,23 @@ def tile_stochasticconfigurationcandidatescores_w4_kernel(
             g_turn(i)
             g_copy_out(i)
 
+        def joint_quantise(i, values):
+            nc.vector.quantize_mx(
+                out=joint_cod[i][:].rearrange("p a c -> p (a c)").bitcast(FP8X4),
+                scales=joint_csc[i][:].rearrange("p a c -> p (a c)"),
+                in_=values.rearrange("p a c -> p (a c)"),
+            )
+
+        def e_quantise(v):
+            nc.vector.quantize_mx(
+                out=e_cod[v].bitcast(FP8X4), scales=e_csc[v], in_=e_val[v].rearrange("p q j -> p (q j)")
+            )
+
         def g_quantise(v):
             nc.vector.quantize_mx(
-                out=g_cod[v][:].rearrange("p n r -> p (n r)").bitcast(FP8X4),
-                scales=g_csc[v][:].rearrange("p n r -> p (n r)"),
-                in_=g_val[v][:].rearrange("p n r j -> p (n r j)"),
+                out=g_cod[v].rearrange("p n r -> p (n r)").bitcast(FP8X4),
+                scales=g_csc[v].rearrange("p n r -> p (n r)"),
+                in_=g_val[v].rearrange("p n r j -> p (n r j)"),
             )
 
         def beta_product(v, qb):
@@ -259,11 +291,6 @@ def tile_stochasticconfigurationcandidatescores_w4_kernel(
                 in0=tgt[v][:, :, cols].rearrange("p j (c i) -> p c j i", i=RUN),
                 in1=read_bank(("gb", v, qb))[:].rearrange("p (j c i) -> p c j i", j=J, i=RUN),
                 op=ALU.subtract,
-            )
-
-        def e_quantise(v):
-            nc.vector.quantize_mx(
-                out=e_cod[v][:].bitcast(FP8X4), scales=e_csc[v][:], in_=e_val[v][:].rearrange("p q j -> p (q j)")
             )
 
         def h_turn(i, v):
@@ -295,7 +322,7 @@ def tile_stochasticconfigurationcandidatescores_w4_kernel(
 
         def hs_place(b, v, n0, n1):
             if (b, v) == (1, 1) and n1 <= NODE_HALF // 2:
-                return g_as_nodes[0][:, n0:n1]
+                return hs_spare[:, n0:n1]
             return hs_val[b, v][:, n0:n1]
 
         def apply_gain(engine, gains, b, v, n0, n1):
@@ -320,8 +347,8 @@ def tile_stochasticconfigurationcandidatescores_w4_kernel(
 
         def hs_quantise(b, v, n0=0, n1=NODE_HALF):
             nc.vector.quantize_mx(
-                out=hs_cod[b][:, v, n0:n1].bitcast(FP8X4),
-                scales=hs_csc[b][:, v, n0:n1],
+                out=hs_cod[b, v][:, n0:n1].bitcast(FP8X4),
+                scales=hs_csc[b, v][:, n0:n1],
                 in_=hs_place(b, v, n0, n1).rearrange("p f j -> p (f j)"),
             )
 
@@ -330,10 +357,10 @@ def tile_stochasticconfigurationcandidatescores_w4_kernel(
             cols = slice(i % 4 * P, (i % 4 + 1) * P)
             nc.tensor.matmul_mx(
                 out=bank[:],
-                lhsT=hs_cod[i // 4][:, v, cols].bitcast(FP8X4),
-                lhsT_scale=hs_csc[i // 4][:, v, cols],
-                rhs=e_cod[v][:].bitcast(FP8X4),
-                rhs_scale=e_csc[v][:],
+                lhsT=hs_cod[i // 4, v][:, cols].bitcast(FP8X4),
+                lhsT_scale=hs_csc[i // 4, v][:, cols],
+                rhs=e_cod[v].bitcast(FP8X4),
+                rhs_scale=e_csc[v],
                 start=(v == 0),
                 stop=(v == 1),
             )
@@ -364,12 +391,12 @@ def tile_stochasticconfigurationcandidatescores_w4_kernel(
                 )
                 nc.sync.dma_start(out=out[i * P : (i + 1) * P, cols], in_=res[i][:, cols])
 
+        nc.vector.memset(dummy[:], 0.0)
+        nc.vector.memset(ones[:], 1.0)
         make_identity(nc, ident[:])
         nc.scalar.dma_start(out=x_scl[:], in_=x_scale.rearrange("o (v p j) -> p (o v) j", p=P, j=J))
-        nc.vector.memset(dummy[:], 0.0)
         nc.scalar.activation(out=dummy[:, 1:2], in_=dummy[:, 0:1], func=ACT.Tanh)
         nc.scalar.copy(ident_b[:], ident[:])
-        nc.vector.memset(ones[:], 1.0)
         nc.vector.memset(w_scl[:].rearrange("p v n -> p (v n)").bitcast(I32), 0)
         nc.vector.memset(b_scl[:].bitcast(I32), 0)
         nc.vector.memset(gain_pad[:], 0.0)
@@ -405,17 +432,17 @@ def tile_stochasticconfigurationcandidatescores_w4_kernel(
         load_x(4)
         load_g(0)
         load_g(1)
-        load_w(0)
         load_scales(w_scl, w_scales.rearrange("v r n -> r v n"))
+        load_w(0)
         load_w(1)
-        load(out=gain_q[:], in_=gain.rearrange("(v p j) -> p v j", p=P, j=J))
-        load_g(2)
         load_g(3)
-        load(out=tau_b[:], in_=tau.partition_broadcast(P))
+        load_g(2)
+        load(out=gain_q[:], in_=gain.rearrange("(v p j) -> p v j", p=P, j=J))
         load(out=b_wrd[:].bitcast(I32), in_=beta_words[0].bitcast(I32))
         load_scales(b_scl, beta_scales[0])
         load(out=tgt[0][:], in_=tgt_rows[0])
         load(out=tgt[1][:], in_=tgt_rows[1])
+        load(out=tau_b[:], in_=tau.partition_broadcast(P))
 
         with tc.manual_schedule():
             x_widen_split(0, 0, P)
@@ -461,17 +488,16 @@ def tile_stochasticconfigurationcandidatescores_w4_kernel(
             nodes(2, 1)
             x_scale_out(5)
             x_scale_out(6)
-            x_quantise(2)
-            g_quantise(0)
+            joint_quantise(0, trio[:, 0:2])
             nodes(3, 1)
-            constants_to_psum()
+            gains_to_psum()
             node_energy(0, 0)
             node_energy(1, 0)
             g_turn_split(3)
             g_copy_out(3)
-            gain_gpsimd(0, 0, 320, 512)
+            gain_gpsimd(0, 0, 304, 512)
             x_scale_out(7)
-            gain_vector(0, 0, 0, 320)
+            gain_vector(0, 0, 0, 304)
             nodes(4, 0)
             nodes(5, 0)
             beta_product(0, 0)
@@ -483,7 +509,7 @@ def tile_stochasticconfigurationcandidatescores_w4_kernel(
             x_quantise(3)
             hs_quantise(0, 0)
             g_quantise(1)
-            gain_gpsimd(1, 0, 224, 512)
+            gain_gpsimd(1, 0, 208, 512)
             residual(0, 0)
             residual(0, 1)
             beta_product(0, 2)
@@ -492,7 +518,7 @@ def tile_stochasticconfigurationcandidatescores_w4_kernel(
             nodes(7, 0)
             residual(0, 2)
             residual(0, 3)
-            gain_vector(1, 0, 0, 224)
+            gain_vector(1, 0, 0, 208)
             node_energy(6, 0)
             node_energy(7, 0)
             node_energy(0, 1)
@@ -501,7 +527,7 @@ def tile_stochasticconfigurationcandidatescores_w4_kernel(
             beta_product(1, 1)
             e_quantise(0)
             hs_quantise(1, 0)
-            gain_gpsimd(0, 1, 224, 512)
+            gain_gpsimd(0, 1, 208, 512)
             residual(1, 0)
             residual(1, 1)
             nodes(4, 1)
@@ -512,40 +538,39 @@ def tile_stochasticconfigurationcandidatescores_w4_kernel(
             residual(1, 3)
             nodes(6, 1)
             nodes(7, 1)
-            gain_vector(0, 1, 0, 224)
+            gain_vector(0, 1, 0, 208)
             node_energy(2, 1)
             node_energy(3, 1)
             node_energy(4, 1)
             node_energy(5, 1)
             e_quantise(1)
             hs_quantise(0, 1)
+            tau_to_psum()
             correlate(0, 0)
             correlate(1, 0)
-            gain_gpsimd(1, 1, 288, 512)
+            gain_gpsimd(1, 1, 256, 512)
             correlate(0, 1)
             correlate(1, 1)
             square(0)
             square(1)
-            gain_vector(1, 1, 0, 144)
             energy_sum(0)
-            gain_vector(1, 1, 144, 256)
+            gain_vector(1, 1, 0, 128)
             energy_inverse(0)
-            gain_vector(1, 1, 256, 288)
-            correlation_squared(2)
-            correlation_squared(3)
+            gain_vector(1, 1, 128, 256)
             node_energy(6, 1)
             node_energy(7, 1)
+            correlation_squared(2)
+            correlation_squared(3)
             correlate(4, 0)
             correlate(5, 0)
             score(0)
             score(1)
             hs_quantise(1, 1, 0, 256)
             hs_quantise(1, 1, 256, 512)
-            energy_sum(1, 0, 2)
+            energy_sum(1)
             score(2)
-            energy_inverse(1, 0, 2)
+            energy_inverse(1)
             score(3)
-            energy_sum(1, 2, 4)
             correlate(4, 1)
             square(4)
             correlate(5, 1)
@@ -555,7 +580,6 @@ def tile_stochasticconfigurationcandidatescores_w4_kernel(
             correlate(7, 1)
             square(7, parts=LAST_BLOCK_PARTS)
             score(4)
-            energy_inverse(1, 2, 4)
             score(5)
             score(6)
             score(7, parts=LAST_BLOCK_PARTS)

@@ -199,13 +199,10 @@ def tile_stochasticconfigurationcandidatescores_w4_kernel(
             preact(r, b)
             tanh(r, b)
 
-        def gains_to_psum():
+        def constants_to_psum():
             bank = new_bank("constants")[:].bitcast(BF16)
-            nc.tensor.matmul(bank[:, Q : Q + P], ident_b[:], gain_pad[:], start=True, stop=True)
-
-        def tau_to_psum():
-            bank = banks["constants"][1][:].bitcast(BF16)
             nc.tensor.matmul(bank[:, 0:Q], ident_b[:], tau_b[:], start=True, stop=True)
+            nc.tensor.matmul(bank[:, Q : Q + P], ident_b[:], gain_pad[:], start=True, stop=True)
 
         def g_turn(i):
             bank = new_bank(("g", i))
@@ -234,9 +231,17 @@ def tile_stochasticconfigurationcandidatescores_w4_kernel(
         def g_split(i):
             sort_gpsimd(hid[i][:].rearrange("p n k -> p (n k)"))
 
+        g_pairs = sbuf("g_pairs", [P, L], F32)
+
+        def g_split_scalar(i):
+            nc.scalar.copy(
+                g_pairs[:].rearrange("p (u m) -> p u m", u=2),
+                hid[i][:].bitcast(F32).rearrange("p n (q u) -> p u (n q)", u=2),
+            )
+
         def g_turn_split(i):
             bank = new_bank(("g", i))
-            words = sorted_place.bitcast(F32)
+            words = g_pairs[:] if i == 2 else sorted_place.bitcast(F32)
             for n in range(2):
                 for u in range(2):
                     at = (2 * n + u) * P
@@ -432,17 +437,17 @@ def tile_stochasticconfigurationcandidatescores_w4_kernel(
         load_x(4)
         load_g(0)
         load_g(1)
-        load_scales(w_scl, w_scales.rearrange("v r n -> r v n"))
         load_w(0)
-        load_w(1)
-        load_g(3)
+        load_scales(w_scl, w_scales.rearrange("v r n -> r v n"))
         load_g(2)
+        load_w(1)
         load(out=gain_q[:], in_=gain.rearrange("(v p j) -> p v j", p=P, j=J))
+        load_g(3)
+        load(out=tau_b[:], in_=tau.partition_broadcast(P))
         load(out=b_wrd[:].bitcast(I32), in_=beta_words[0].bitcast(I32))
         load_scales(b_scl, beta_scales[0])
         load(out=tgt[0][:], in_=tgt_rows[0])
         load(out=tgt[1][:], in_=tgt_rows[1])
-        load(out=tau_b[:], in_=tau.partition_broadcast(P))
 
         with tc.manual_schedule():
             x_widen_split(0, 0, P)
@@ -470,17 +475,19 @@ def tile_stochasticconfigurationcandidatescores_w4_kernel(
             g_copy_out(0)
             x_split(6)
             g_copy_out(1)
+            g_split_scalar(2)
             nodes(0, 0)
-            nodes(0, 1)
-            x_split(7)
             nodes(1, 0)
+            x_split(7)
+            nodes(0, 1)
             nodes(1, 1)
             x_scale_out(3)
             x_scale_out(4)
             x_quantise(1)
             g_split(3)
             x_turn_pairs(6)
-            g_in(2)
+            g_turn_split(2)
+            g_copy_out(2)
             x_turn_pairs(7)
             nc.scalar.copy(gain_f[:], gain_q[:])
             nodes(2, 0)
@@ -490,7 +497,7 @@ def tile_stochasticconfigurationcandidatescores_w4_kernel(
             x_scale_out(6)
             joint_quantise(0, trio[:, 0:2])
             nodes(3, 1)
-            gains_to_psum()
+            constants_to_psum()
             node_energy(0, 0)
             node_energy(1, 0)
             g_turn_split(3)
@@ -545,7 +552,6 @@ def tile_stochasticconfigurationcandidatescores_w4_kernel(
             node_energy(5, 1)
             e_quantise(1)
             hs_quantise(0, 1)
-            tau_to_psum()
             correlate(0, 0)
             correlate(1, 0)
             gain_gpsimd(1, 1, 256, 512)
@@ -557,20 +563,21 @@ def tile_stochasticconfigurationcandidatescores_w4_kernel(
             gain_vector(1, 1, 0, 128)
             energy_inverse(0)
             gain_vector(1, 1, 128, 256)
-            node_energy(6, 1)
-            node_energy(7, 1)
             correlation_squared(2)
             correlation_squared(3)
+            node_energy(6, 1)
+            node_energy(7, 1)
             correlate(4, 0)
             correlate(5, 0)
             score(0)
             score(1)
             hs_quantise(1, 1, 0, 256)
             hs_quantise(1, 1, 256, 512)
-            energy_sum(1)
+            energy_sum(1, 0, 2)
             score(2)
-            energy_inverse(1)
+            energy_inverse(1, 0, 2)
             score(3)
+            energy_sum(1, 2, 4)
             correlate(4, 1)
             square(4)
             correlate(5, 1)
@@ -580,6 +587,7 @@ def tile_stochasticconfigurationcandidatescores_w4_kernel(
             correlate(7, 1)
             square(7, parts=LAST_BLOCK_PARTS)
             score(4)
+            energy_inverse(1, 2, 4)
             score(5)
             score(6)
             score(7, parts=LAST_BLOCK_PARTS)

@@ -399,7 +399,6 @@ def tile_stochasticconfigurationcandidatescores_w4_kernel(
         nc.vector.memset(dummy[:], 0.0)
         nc.vector.memset(ones[:], 1.0)
         make_identity(nc, ident[:])
-        nc.scalar.dma_start(out=x_scl[:], in_=x_scale.rearrange("o (v p j) -> p (o v) j", p=P, j=J))
         nc.scalar.activation(out=dummy[:, 1:2], in_=dummy[:, 0:1], func=ACT.Tanh)
         nc.scalar.copy(ident_b[:], ident[:])
         nc.vector.memset(w_scl[:].rearrange("p v n -> p (v n)").bitcast(I32), 0)
@@ -432,6 +431,7 @@ def tile_stochasticconfigurationcandidatescores_w4_kernel(
 
         load_x(0)
         load_x(1)
+        load(out=x_scl[:], in_=x_scale.rearrange("o (v p j) -> p (o v) j", p=P, j=J))
         load_x(2)
         load_x(3)
         load_x(4)

from contextlib import ExitStack

import concourse.mybir as mybir
from concourse.masks import make_identity

F32 = mybir.dt.float32
BF16 = mybir.dt.bfloat16
I32 = mybir.dt.int32
U32 = mybir.dt.uint32
U8 = mybir.dt.uint8
FP8 = mybir.dt.float8_e4m3fn
FP8X4 = mybir.dt.float8_e4m3fn_x4
FP4X4 = mybir.dt.float4_e2m1fn_x4
ACT = mybir.ActivationFunctionType
ALU = mybir.AluOpType

N, D, F, L, Q = 1024, 1024, 1024, 512, 512
FLOPS = 2 * N * D * F + 2 * N * L * Q + 2 * N * F * Q

P = 128
J = 4
PSUM_BANKS = 8
BANK = 512
ROW_TILES = N // P
NODE_HALF = F // 2
RUN = 4
FP4_BYTES = 2

X_LOADS = (1, 1, 2, 2, 2)
X_GROUPS = (2, 2, 2, 2)
WARM_UP_MATMULS = 3
GPSIMD_NODES = 128
LAST_BLOCK_PARTS = 2
PART = 2048


def tile_stochasticconfigurationcandidatescores_w4_kernel(
    tc, x_bytes, x_scale, w_words, w_scales, gain, target, hidden, beta_words, beta_scales, tau, out
):
    nc = tc.nc
    with ExitStack() as ctx:
        keep = ctx.enter_context(tc.tile_pool(name="keep", bufs=1))
        psum = ctx.enter_context(tc.psum_pool(name="psum", bufs=1))

        def sbuf(name, shape, dtype):
            return keep.tile(shape, dtype, name=name, align_bytes=64)

        x_raw = [sbuf("x_raw%d" % i, [P, n, D], U8) for i, n in enumerate(X_LOADS)]
        x_scl = sbuf("x_scl", [P, 2, J], F32)
        w_wrd = [sbuf("w_wrd%d" % b, [P, 2, FP4_BYTES * NODE_HALF], U8) for b in range(2)]
        w_scl = sbuf("w_scl", [P, 2, F], U8)
        b_wrd = sbuf("b_wrd", [P, FP4_BYTES * Q], U8)
        b_scl = sbuf("b_scl", [P, Q], U8)
        hid = [sbuf("hid%d" % i, [P, 2, L], BF16) for i in range(4)]
        tgt = [sbuf("tgt%d" % v, [P, J, Q], BF16) for v in range(2)]
        gain_pad = sbuf("gain_pad", [P, P], BF16)
        gain_q = gain_pad[:, 0 : 2 * J].rearrange("p (v j) -> p v j", j=J)
        gain_f = sbuf("gain_f", [P, 2, J], F32)
        tau_b = sbuf("tau_b", [P, Q], BF16)

        trio = sbuf("trio", [P, 3, PART], BF16)
        duo = sbuf("duo", [P, 2, PART], BF16)
        as_x = "p (n k r j) -> p n k r j"
        x_val = [sbuf("x_val%d" % i, [P, 2, 2, P, J], BF16)[:] for i in range(2)]
        x_val.extend(tile[:, 0].rearrange(as_x, n=2, k=2, j=J) for tile in (trio, duo))
        joint_cod = [sbuf("joint_cod%d" % i, [P, 2, PART // J], U32) for i in range(4)]
        joint_csc = [sbuf("joint_csc%d" % i, [P, 2, PART // J], U8) for i in range(4)]
        x_wide = [sbuf("x_wide%d" % r, [P, D], BF16)[:] for r in range(ROW_TILES - 1)]
        x_wide.append(x_val[0][:, 0].rearrange("p v r j -> p (v r j)"))
        x_pairs = [sbuf("x_pairs%d" % r, [P, D // 2], F32) for r in range(ROW_TILES)]
        x_cod = [sbuf("x_cod%d" % i, [P, 2, 2, P], U32)[:] for i in range(2)]
        x_csc = [sbuf("x_csc%d" % i, [P, 2, 2, P], U8)[:] for i in range(2)]
        x_cod.extend(tile[:, 0].rearrange("p (n k r) -> p n k r", n=2, k=2) for tile in joint_cod[:2])
        x_csc.extend(tile[:, 0].rearrange("p (n k r) -> p n k r", n=2, k=2) for tile in joint_csc[:2])
        g_val = [tile[:, 1].rearrange("p (n r j) -> p n r j", n=J, j=J) for tile in (trio, duo)]
        g_cod = [tile[:, 1].rearrange("p (n r) -> p n r", n=J) for tile in joint_cod[:2]]
        g_csc = [tile[:, 1].rearrange("p (n r) -> p n r", n=J) for tile in joint_csc[:2]]
        e_val = [trio[:, 2 * v].rearrange("p (q j) -> p q j", j=J) for v in range(2)]
        e_cod = [joint_cod[2 + v][:, v] for v in range(2)]
        e_csc = [joint_csc[2 + v][:, v] for v in range(2)]
        chunks = [(b, v) for b in range(2) for v in range(2)]
        h = {k: sbuf("h%d%d" % k, [P, J, NODE_HALF], F32) for k in chunks}
        places = {(0, 0): trio[:, 1], (1, 0): trio[:, 1], (0, 1): trio[:, 0], (1, 1): trio[:, 2]}
        hs_val = {k: place.rearrange("p (f j) -> p f j", j=J) for k, place in places.items()}
        hs_spare = duo[:, 1].rearrange("p (f j) -> p f j", j=J)
        hs_cod = {(0, 0): sbuf("hs_cod00", [P, NODE_HALF], U32)[:], (1, 1): sbuf("hs_cod11", [P, NODE_HALF], U32)[:]}
        hs_csc = {(0, 0): sbuf("hs_csc00", [P, NODE_HALF], U8)[:], (1, 1): sbuf("hs_csc11", [P, NODE_HALF], U8)[:]}
        hs_cod.update({(1, 0): joint_cod[2][:, 1], (0, 1): joint_cod[3][:, 0]})
        hs_csc.update({(1, 0): joint_csc[2][:, 1], (0, 1): joint_csc[3][:, 0]})
        hh_part = [sbuf("hh_part%d" % b, [P, 4, 2], F32) for b in range(2)]
        hh_sum = [sbuf("hh_sum%d" % b, [P, 4], F32) for b in range(2)]
        hh_inv = [sbuf("hh_inv%d" % b, [P, 4], F32) for b in range(2)]
        squares = [sbuf("squares%d" % v, [P, BANK], BF16) for v in range(2)]
        c_sq = [sbuf("c_sq%d" % i, [P, Q], F32) for i in range(8)]
        res = [sbuf("res%d" % i, [P, Q], F32) for i in range(8)]

        ident = sbuf("ident", [P, P], F32)
        ident_b = sbuf("ident_b", [P, P], BF16)
        ones = sbuf("ones", [P, 1], F32)
        dummy = sbuf("dummy", [P, 2], F32)

        banks = {}

        free = list(range(PSUM_BANKS))

        def new_bank(key):
            number = free.pop(0)
            tile = psum.tile([P, BANK], F32, name="bank%d" % number, tag="bank%d" % number, bufs=1)
            banks[key] = (number, tile)
            return tile

        def read_bank(key):
            number, tile = banks.pop(key)
            free.append(number)
            return tile

        x_place = [(i, n) for i, count in enumerate(X_LOADS) for n in range(count)]

        x_group = [(i, n) for i, count in enumerate(X_GROUPS) for n in range(count)]

        def x_widen(copy, r, k0=0, k1=D):
            i, n = x_place[r]
            copy(x_wide[r][:, k0:k1], x_raw[i][:, n, k0:k1].bitcast(FP8))

        def x_widen_split(r, m0=0, m1=D // J):
            i, n = x_place[r]
            nc.vector.tensor_scalar(
                out=x_wide[r].rearrange("p (u m e) -> p m u e", u=2, e=2)[:, m0:m1],
                in0=x_raw[i][:, n, J * m0 : J * m1].bitcast(FP8),
                scalar1=ones[:],
                scalar2=None,
                op0=ALU.mult,
            )

        def x_turn_split(r):
            bank = new_bank(("x", r))
            words = x_wide[r].bitcast(F32)
            for v in range(2):
                for u in range(2):
                    at = (2 * u + v) * P
                    nc.tensor.transpose(bank[:, at : at + P], words[:, at : at + P], ident[:])

        def x_split(r):
            nc.scalar.copy(
                x_pairs[r][:].rearrange("p (u m) -> p u m", u=2),
                x_wide[r].bitcast(F32).rearrange("p (m u) -> p u m", u=2),
            )

        def x_turn_pairs(r):
            bank = new_bank(("x", r))
            for v in range(2):
                for u in range(2):
                    at = (2 * u + v) * P
                    nc.tensor.transpose(bank[:, at : at + P], x_pairs[r][:, at : at + P], ident[:])

        def x_turn(r):
            bank = new_bank(("x", r))
            words = x_wide[r].bitcast(F32)
            for v in range(2):
                for u in range(2):
                    at = (2 * u + v) * P
                    nc.tensor.transpose(
                        bank[:, at : at + P], words[:, 256 * v + u : 256 * (v + 1) : 2], ident[:]
                    )

        def x_scale_out(r):
            nc.vector.tensor_tensor(
                out=x_val[x_group[r][0]][:, x_group[r][1]].rearrange("p v r (u e) -> p v r u e", u=2),
                in0=read_bank(("x", r))[:].bitcast(BF16).rearrange("p (u v r e) -> p v r u e", u=2, v=2, e=2),
                in1=x_scl[:].rearrange("p v (u e) -> p v u e", u=2).unsqueeze(2).to_broadcast([P, 2, P, 2, 2]),
                op=ALU.mult,
            )

        def x_quantise(i):
            nc.vector.quantize_mx(
                out=x_cod[i].rearrange("p n v r -> p (n v r)").bitcast(FP8X4),
                scales=x_csc[i].rearrange("p n v r -> p (n v r)"),
                in_=x_val[i].rearrange("p n v r j -> p (n v r j)"),
            )

        def preact(r, b):
            bank = new_bank(("xw", r, b))
            i, n = x_group[r]
            for v in range(2):
                nc.tensor.matmul_mx(
                    out=bank[:],
                    lhsT=x_cod[i][:, n, v, :].bitcast(FP8X4),
                    lhsT_scale=x_csc[i][:, n, v, :],
                    rhs=w_wrd[b][:, v, :].bitcast(FP4X4),
                    rhs_scale=w_scl[:, v, b * NODE_HALF : (b + 1) * NODE_HALF],
                    start=(v == 0),
                    stop=(v == 1),
                )

        def tanh(r, b):
            nc.scalar.activation(out=h[b, r // J][:, r % J, :], in_=read_bank(("xw", r, b))[:], func=ACT.Tanh)

        def nodes(r, b):
            preact(r, b)
            tanh(r, b)

        def constants_to_psum():
            bank = new_bank("constants")[:].bitcast(BF16)
            nc.tensor.matmul(bank[:, 0:Q], ident_b[:], tau_b[:], start=True, stop=True)
            nc.tensor.matmul(bank[:, Q : Q + P], ident_b[:], gain_pad[:], start=True, stop=True)

        def g_turn(i):
            bank = new_bank(("g", i))
            for n in range(2):
                words = hid[i][:, n, :].bitcast(F32)
                for u in range(2):
                    at = (2 * n + u) * P
                    nc.tensor.transpose(bank[:, at : at + P], words[:, u:256:2], ident[:])

        sorted_place = x_val[1][:, 0].rearrange("p k r j -> p (k r j)")

        def sort_gpsimd(rows):
            nc.gpsimd.tensor_scalar(
                out=sorted_place.rearrange("p (u m e) -> p u m e", u=2, e=2),
                in0=rows.rearrange("p (m u e) -> p u m e", u=2, e=2),
                scalar1=1.0,
                scalar2=0.0,
                op0=ALU.mult,
                op1=ALU.add,
            )

        def x_split_gpsimd(r):
            x_pairs[r] = sorted_place.bitcast(F32)
            sort_gpsimd(x_wide[r])

        def g_split(i):
            sort_gpsimd(hid[i][:].rearrange("p n k -> p (n k)"))

        g_pairs = sbuf("g_pairs", [P, L], F32)

        def g_split_scalar(i):
            nc.scalar.copy(
                g_pairs[:].rearrange("p (u m) -> p u m", u=2),
                hid[i][:].bitcast(F32).rearrange("p n (q u) -> p u (n q)", u=2),
            )

        def g_turn_split(i):
            bank = new_bank(("g", i))
            words = g_pairs[:] if i == 2 else sorted_place.bitcast(F32)
            for n in range(2):
                for u in range(2):
                    at = (2 * n + u) * P
                    nc.tensor.transpose(bank[:, at : at + P], words[:, (2 * u + n) * P : (2 * u + n + 1) * P], ident[:])

        def g_copy_out(i, copy=nc.scalar.copy):
            copy(
                g_val[i // 2][:, 2 * (i % 2) : 2 * (i % 2) + 2].bitcast(F32),
                read_bank(("g", i))[:].rearrange("p (n u r) -> p n r u", n=2, u=2),
            )

        def g_in(i):
            g_turn(i)
            g_copy_out(i)

        def joint_quantise(i, values):
            nc.vector.quantize_mx(
                out=joint_cod[i][:].rearrange("p a c -> p (a c)").bitcast(FP8X4),
                scales=joint_csc[i][:].rearrange("p a c -> p (a c)"),
                in_=values.rearrange("p a c -> p (a c)"),
            )

        def e_quantise(v):
            nc.vector.quantize_mx(
                out=e_cod[v].bitcast(FP8X4), scales=e_csc[v], in_=e_val[v].rearrange("p q j -> p (q j)")
            )

        def g_quantise(v):
            nc.vector.quantize_mx(
                out=g_cod[v].rearrange("p n r -> p (n r)").bitcast(FP8X4),
                scales=g_csc[v].rearrange("p n r -> p (n r)"),
                in_=g_val[v].rearrange("p n r j -> p (n r j)"),
            )

        def beta_product(v, qb):
            bank = new_bank(("gb", v, qb))
            for j in range(J):
                nc.tensor.matmul_mx(
                    out=bank[:, j * P : (j + 1) * P],
                    lhsT=g_cod[v][:, j, :].bitcast(FP8X4),
                    lhsT_scale=g_csc[v][:, j, :],
                    rhs=b_wrd[:, qb * P * FP4_BYTES : (qb + 1) * P * FP4_BYTES].bitcast(FP4X4),
                    rhs_scale=b_scl[:, qb * P : (qb + 1) * P],
                    start=True,
                    stop=True,
                )

        def residual(v, qb):
            cols = slice(qb * P, (qb + 1) * P)
            nc.vector.tensor_tensor(
                out=e_val[v][:, cols, :].rearrange("p (c i) j -> p c j i", i=RUN),
                in0=tgt[v][:, :, cols].rearrange("p j (c i) -> p c j i", i=RUN),
                in1=read_bank(("gb", v, qb))[:].rearrange("p (j c i) -> p c j i", j=J, i=RUN),
                op=ALU.subtract,
            )

        def h_turn(i, v):
            bank = new_bank(("h", i, v))
            at = i % 4 * P
            for j in range(J):
                nc.tensor.transpose(bank[:, j * P : (j + 1) * P], h[i // 4, v][:, j, at : at + P], ident[:])

        def energy(i, v):
            nc.scalar.activation(
                out=squares[0][:],
                in_=read_bank(("h", i, v))[:],
                func=ACT.Square,
                accum_out=hh_part[i // 4][:, i % 4, v : v + 1],
            )
            squares.reverse()

        def node_energy(i, v):
            h_turn(i, v)
            energy(i, v)

        def energy_sum(b, n0=0, n1=4):
            nc.vector.tensor_reduce(
                out=hh_sum[b][:, n0:n1], in_=hh_part[b][:, n0:n1], axis=mybir.AxisListType.X, op=ALU.add
            )

        def energy_inverse(b, n0=0, n1=4):
            nc.vector.reciprocal(out=hh_inv[b][:, n0:n1], in_=hh_sum[b][:, n0:n1])

        def hs_place(b, v, n0, n1):
            if (b, v) == (1, 1) and n1 <= NODE_HALF // 2:
                return hs_spare[:, n0:n1]
            return hs_val[b, v][:, n0:n1]

        def apply_gain(engine, gains, b, v, n0, n1):
            engine.tensor_tensor(
                out=hs_place(b, v, n0, n1).rearrange("p (c i) j -> p c j i", i=RUN),
                in0=h[b, v][:, :, n0:n1].rearrange("p j (c i) -> p c j i", i=RUN),
                in1=gains.unsqueeze(1).unsqueeze(3).to_broadcast([P, (n1 - n0) // RUN, J, RUN]),
                op=ALU.mult,
            )

        def gain_vector(b, v, n0, n1):
            gains = banks["constants"][1][:].bitcast(BF16)[:, Q + J * v : Q + J * (v + 1)]
            apply_gain(nc.vector, gains, b, v, n0, n1)

        def gain_gpsimd(b, v, n0, n1):
            nc.gpsimd.tensor_tensor(
                out=hs_place(b, v, n0, n1),
                in0=h[b, v][:, :, n0:n1].rearrange("p j f -> p f j"),
                in1=gain_f[:, v, :].unsqueeze(1).to_broadcast([P, n1 - n0, J]),
                op=ALU.mult,
            )

        def hs_quantise(b, v, n0=0, n1=NODE_HALF):
            nc.vector.quantize_mx(
                out=hs_cod[b, v][:, n0:n1].bitcast(FP8X4),
                scales=hs_csc[b, v][:, n0:n1],
                in_=hs_place(b, v, n0, n1).rearrange("p f j -> p (f j)"),
            )

        def correlate(i, v):
            bank = new_bank(("c", i)) if v == 0 else banks["c", i][1]
            cols = slice(i % 4 * P, (i % 4 + 1) * P)
            nc.tensor.matmul_mx(
                out=bank[:],
                lhsT=hs_cod[i // 4, v][:, cols].bitcast(FP8X4),
                lhsT_scale=hs_csc[i // 4, v][:, cols],
                rhs=e_cod[v].bitcast(FP8X4),
                rhs_scale=e_csc[v],
                start=(v == 0),
                stop=(v == 1),
            )

        def square(i, parts=1):
            bank = read_bank(("c", i))
            width = Q // parts
            for part in range(parts):
                cols = slice(part * width, (part + 1) * width)
                nc.scalar.activation(out=c_sq[i][:, cols], in_=bank[:, cols], func=ACT.Square)

        def correlation_squared(i):
            correlate(i, 0)
            correlate(i, 1)
            square(i)

        def score(i, parts=1):
            width = Q // parts
            for part in range(parts):
                cols = slice(part * width, (part + 1) * width)
                nc.vector.scalar_tensor_tensor(
                    out=res[i][:, cols],
                    in0=c_sq[i][:, cols],
                    scalar=hh_inv[i // 4][:, i % 4 : i % 4 + 1],
                    in1=banks["constants"][1][:].bitcast(BF16)[:, cols],
                    op0=ALU.mult,
                    op1=ALU.subtract,
                )
                nc.sync.dma_start(out=out[i * P : (i + 1) * P, cols], in_=res[i][:, cols])

        nc.vector.memset(dummy[:], 0.0)
        nc.vector.memset(ones[:], 1.0)
        make_identity(nc, ident[:])
        nc.scalar.activation(out=dummy[:, 1:2], in_=dummy[:, 0:1], func=ACT.Tanh)
        nc.scalar.copy(ident_b[:], ident[:])
        nc.vector.memset(w_scl[:].rearrange("p v n -> p (v n)").bitcast(I32), 0)
        nc.vector.memset(b_scl[:].bitcast(I32), 0)
        nc.vector.memset(gain_pad[:], 0.0)

        load = nc.sync.dma_start
        x_rows = x_bytes.rearrange("(v p j) k -> v p j k", p=P, j=J)
        hid_rows = hidden.rearrange("(v p j) k -> v p j k", p=P, j=J)
        tgt_rows = target.rearrange("(v p j) q -> v p j q", p=P, j=J)
        w_rows = w_words.rearrange("v p n -> p v n")

        def load_x(i):
            r = sum(X_LOADS[:i])
            load(out=x_raw[i][:], in_=x_rows[r // J][:, r % J : r % J + X_LOADS[i], :])

        def load_g(i):
            load(out=hid[i][:], in_=hid_rows[i // 2][:, 2 * (i % 2) : 2 * (i % 2) + 2, :])

        def load_w(b):
            width = FP4_BYTES * NODE_HALF
            load(out=w_wrd[b][:].bitcast(I32), in_=w_rows[:, :, b * width : (b + 1) * width].bitcast(I32))

        def load_scales(tile, rows):
            for quadrant in range(4):
                load(
                    out=tile[32 * quadrant : 32 * quadrant + 4].bitcast(I32),
                    in_=rows[4 * quadrant : 4 * quadrant + 4].bitcast(I32),
                )

        load_x(0)
        load_x(1)
        load(out=x_scl[:], in_=x_scale.rearrange("o (v p j) -> p (o v) j", p=P, j=J))
        load_x(2)
        load_x(3)
        load_x(4)
        load_g(0)
        load_g(1)
        load_w(0)
        load_scales(w_scl, w_scales.rearrange("v r n -> r v n"))
        load_g(2)
        load_w(1)
        load(out=gain_q[:], in_=gain.rearrange("(v p j) -> p v j", p=P, j=J))
        load_g(3)
        load(out=tau_b[:], in_=tau.partition_broadcast(P))
        load(out=b_wrd[:].bitcast(I32), in_=beta_words[0].bitcast(I32))
        load_scales(b_scl, beta_scales[0])
        load(out=tgt[0][:], in_=tgt_rows[0])
        load(out=tgt[1][:], in_=tgt_rows[1])

        with tc.manual_schedule():
            x_widen_split(0, 0, P)
            x_widen_split(0, P, 2 * P)
            x_widen_split(1)
            x_widen(nc.scalar.copy, 2)
            x_widen(nc.scalar.copy, 3)
            x_widen(nc.scalar.copy, 4)
            x_widen(nc.gpsimd.tensor_copy, 5)
            x_widen(nc.gpsimd.tensor_copy, 6)
            x_turn_split(0)
            x_turn_split(1)
            x_turn(2)
            g_turn(0)
            x_turn(3)
            g_turn(1)
            x_turn(4)
            x_split(5)
            x_scale_out(0)
            x_turn_pairs(5)
            x_scale_out(1)
            x_scale_out(2)
            x_quantise(0)
            x_widen(nc.gpsimd.tensor_copy, 7)
            g_copy_out(0)
            x_split(6)
            g_copy_out(1)
            g_split_scalar(2)
            nodes(0, 0)
            nodes(1, 0)
            x_split(7)
            nodes(0, 1)
            nodes(1, 1)
            x_scale_out(3)
            x_scale_out(4)
            x_quantise(1)
            g_split(3)
            x_turn_pairs(6)
            g_turn_split(2)
            g_copy_out(2)
            x_turn_pairs(7)
            nc.scalar.copy(gain_f[:], gain_q[:])
            nodes(2, 0)
            nodes(3, 0)
            nodes(2, 1)
            x_scale_out(5)
            x_scale_out(6)
            joint_quantise(0, trio[:, 0:2])
            nodes(3, 1)
            constants_to_psum()
            node_energy(0, 0)
            node_energy(1, 0)
            g_turn_split(3)
            g_copy_out(3)
            gain_gpsimd(0, 0, 304, 512)
            x_scale_out(7)
            gain_vector(0, 0, 0, 304)
            nodes(4, 0)
            nodes(5, 0)
            beta_product(0, 0)
            beta_product(0, 1)
            node_energy(2, 0)
            node_energy(3, 0)
            node_energy(4, 0)
            node_energy(5, 0)
            x_quantise(3)
            hs_quantise(0, 0)
            g_quantise(1)
            gain_gpsimd(1, 0, 208, 512)
            residual(0, 0)
            residual(0, 1)
            beta_product(0, 2)
            beta_product(0, 3)
            nodes(6, 0)
            nodes(7, 0)
            residual(0, 2)
            residual(0, 3)
            gain_vector(1, 0, 0, 208)
            node_energy(6, 0)
            node_energy(7, 0)
            node_energy(0, 1)
            node_energy(1, 1)
            beta_product(1, 0)
            beta_product(1, 1)
            e_quantise(0)
            hs_quantise(1, 0)
            gain_gpsimd(0, 1, 208, 512)
            residual(1, 0)
            residual(1, 1)
            nodes(4, 1)
            beta_product(1, 2)
            beta_product(1, 3)
            nodes(5, 1)
            residual(1, 2)
            residual(1, 3)
            nodes(6, 1)
            nodes(7, 1)
            gain_vector(0, 1, 0, 208)
            node_energy(2, 1)
            node_energy(3, 1)
            node_energy(4, 1)
            node_energy(5, 1)
            e_quantise(1)
            hs_quantise(0, 1)
            correlate(0, 0)
            correlate(1, 0)
            gain_gpsimd(1, 1, 256, 512)
            correlate(0, 1)
            correlate(1, 1)
            square(0)
            square(1)
            energy_sum(0)
            gain_vector(1, 1, 0, 128)
            energy_inverse(0)
            gain_vector(1, 1, 128, 256)
            correlation_squared(2)
            correlation_squared(3)
            node_energy(6, 1)
            node_energy(7, 1)
            correlate(4, 0)
            correlate(5, 0)
            score(0)
            score(1)
            hs_quantise(1, 1, 0, 256)
            hs_quantise(1, 1, 256, 512)
            energy_sum(1, 0, 2)
            score(2)
            energy_inverse(1, 0, 2)
            score(3)
            energy_sum(1, 2, 4)
            correlate(4, 1)
            square(4)
            correlate(5, 1)
            square(5)
            correlation_squared(6)
            correlate(7, 0)
            correlate(7, 1)
            square(7, parts=LAST_BLOCK_PARTS)
            score(4)
            energy_inverse(1, 2, 4)
            score(5)
            score(6)
            score(7, parts=LAST_BLOCK_PARTS)
